import numpy as np, ml_dtypes
CORES = [35,38,43,46]
N = 4
BF = ml_dtypes.bfloat16
def gentries(a):
    return np.ascontiguousarray(a.reshape(8, 16, -1).transpose(0, 2, 1)).reshape(8, -1)
def gtable(e):
    e = np.asarray(e); return np.ascontiguousarray(e.reshape(8, -1, 16).transpose(0, 2, 1)).reshape(128, -1).astype(np.int32)
W, P, V, EPS = 4096, 256, 5, 2
S = W // P
AG, LO, WIN, MAJ = 12, 4, 12, 9
def pick(rng, cl, want):
    out = np.zeros(want.shape, np.int64); z = rng.random(want.shape)
    for q in range(N):
        for g in range(8):
            o = np.argsort(cl[q, g], kind="stable"); lo = np.searchsorted(cl[q, g][o], np.arange(6)); n = np.maximum(lo[1:] - lo[:-1], 1); v = want[q, g]
            out[q, g] = o[np.minimum(lo[v] + (z[q, g] * n[v]).astype(np.int64), W - 1)]
    return out
def turned(a):
    return np.ascontiguousarray(np.swapaxes(a, 2, 3))
def pack(X, L, R, y, w):
    return {"xc": np.ascontiguousarray(X.reshape(N, 128, W)).astype(np.float32).astype(BF), "lsr": np.ascontiguousarray(L.reshape(N, 128, W)).astype(np.int32),
            "jur": np.stack([gtable(a.reshape(8, -1)) for a in R]), "own": np.ascontiguousarray(y.reshape(N, 128, P)).astype(np.float32).astype(BF), "wgt": w.reshape(N, 128, 1).astype(np.int32)}
def world(rng):
    pr = rng.integers(0, 16, (8, 4, 16)); gi = np.arange(8).reshape(1, 8, 1)
    z = np.where(rng.random((N, 8, W)) < 0.7, rng.random((1, 8, W)), rng.random((N, 8, W))); m = (0.45 + 0.04 * rng.permutation(8)).reshape(1, 8, 1)
    cl = (z >= m).astype(np.int64) + (z >= m + 0.15) + (z >= m + 0.2)
    p = pr[gi, cl]
    X = np.clip(p + rng.integers(-EPS, EPS + 1, p.shape), 0, 15)
    X = np.where(rng.random(p.shape) < rng.choice(np.array([0.04, 0.12, 0.3]), (N, 8, W, 1)), rng.integers(0, 16, p.shape), X)
    tr = (5 * np.arange(16) + rng.integers(0, 16, (N, 8, W, 1))) & 15
    X = np.where(cl[..., None] == 3, np.where(tr < 5 + rng.integers(0, 2, (N, 8, W, 1)), (p + 8) & 15, p), X)
    yc = rng.choice(4, (N, 8, P), p=[0.5, 0.25, 0.1, 0.15]); yp = pr[gi, yc]
    y = np.where(rng.random(yp.shape) < rng.choice(np.array([0.0, 0.1]), (N, 8, P, 1)), rng.integers(0, 16, yp.shape), yp)
    bias = rng.choice(np.array([0.0, 0.2, 0.5, 1.0]), (N, 8, P, 1)); want = np.repeat(yc[..., None], 16, axis=3)
    R = np.where(rng.random((N, 8, P, 16)) < bias, pick(rng, cl, want), rng.integers(0, W, (N, 8, P, 16)))
    return turned(X), rng.integers(0, W, (N, 8, 16, W)), R, turned(y), rng.integers(0, W, (N, 8, 16)), pr
def flood(rng, X, R, y):
    b = np.arange(16); h = np.where(b < 8, 15, 0); a = 15 * (b & 1)
    X[1, :, :, 0] = 0; X[1, :, :, W - 1] = 15; X[2, :, :, 0] = 15; X[2, :, :, W - 1] = h.reshape(1, 16)
    y[1] = h.reshape(1, 16, 1); y[2] = a.reshape(1, 16, 1); y[2, 7, :, P - 1] = h
    R[1] = (W - 1) * (np.argsort(rng.random((8, P, 16)), axis=2) < 5); R[2] = (W - 1) * rng.integers(0, 2, (8, P, 16)); R[2, 7, P - 1] = W - 1
def setup_inputs(rng):
    return pack(*world(rng)[:5])
def setup_inputs_spread(rng):
    X = (16 * rng.random((N, 8, 1, W)) ** 3 * rng.random((N, 8, 16, W))).astype(np.int64)
    y = (16 * rng.random((N, 8, 1, P)) ** 3 * rng.random((N, 8, 16, P))).astype(np.int64)
    e = 1 + 0.25 * rng.permutation(8); lw = W.bit_length() - 1
    L = (W * rng.random((N, 8, 16, W)) ** e.reshape(1, 8, 1, 1)).astype(np.int64)
    R = (W * rng.random((N, 8, P, 16)) ** e[::-1].reshape(1, 8, 1, 1)).astype(np.int64)
    w = np.minimum(np.exp2(lw * rng.random((N, 8, 16))).astype(np.int64), W - 1)
    return pack(X, L, R, y, w)
def setup_inputs_ends(rng):
    kind = rng.integers(0, 3, (N, 8, 1, W)); X = np.where(kind == 0, 0, np.where(kind == 1, 15, 15 * rng.integers(0, 2, (N, 8, 16, W))))
    L = (W - 1) * rng.integers(0, 2, (N, 8, 16, W)); flip = rng.integers(0, 2, (N, 8, 1)); X[..., 0] = 15 * flip; X[..., W - 1] = 15 - 15 * flip
    nf = rng.choice(np.array([0, 0, 1, 4, 5, 8]), (N, 8, 1, P)); base = rng.integers(0, 2, (N, 8, 1, P))
    y = 15 * np.where(np.argsort(rng.random((N, 8, 16, P)), axis=2) < nf, 1 - base, base)
    y[..., 0] = 15; y[..., 1] = 0; y[..., P - 1] = 15
    m = rng.choice(np.array([0, 4, 5, 11, 12, 16]), (N, 8, P, 1)); R = (W - 1) * (np.argsort(rng.random((N, 8, P, 16)), axis=3) < m)
    w = (W - 1) * rng.integers(0, 2, (N, 8, 16)); w[0, 0] = 0; w[N - 1, 7] = W - 1
    X[N - 1, 7, :, 0] = 0; X[N - 1, 7, :, W - 1] = 15; R[N - 1, 7, P - 1] = W - 1; R[N - 1, 7, 0] = W - 1
    h = P // 2
    for q, g in ((0, 2), (N - 1, 6)):
        w[q, g] = 0; w[q, g, 13:] = W - 1; X[q, g, :, W - 1] = 0; X[q, g, :, 0] = 15; L[q, g, :, W - 1] = 0
        y[q, g, :, h:] = 0; y[q, g, 15, h:] = 1; y[q, g, 13:15, h + h // 2:] = 15; R[q, g, h:] = W - 1; R[q, g, h::2, :4] = 0
    for q, g in ((0, 5), (N - 1, 7)):
        top = X[q, g, :, W - 1].copy(); X[q, g, :, W - 2] = top; X[q, g, 0, W - 2] = abs(int(top[0]) - 1); w[q, g, 0] = W - 1
        s = P - P // 4; i = np.arange(s, P - 1).reshape(-1, 1)
        y[q, g, :, s:P - 1] = (15 - top).reshape(16, 1); R[q, g, s:P - 1] = W - 1 - (np.arange(16) > i % 15).astype(np.int64)
    L[N - 1, 5, :, W - S:] = W - 1
    flood(rng, X, R, y)
    return pack(X, L, R, y, w)
def setup_inputs_corners(rng):
    b = np.arange(16); bb = np.where(b < 3, b, b - 1); pr = rng.integers(4, 12, (8, 16)); p = pr.reshape(1, 8, 1, 16)
    cl = rng.integers(0, 5, (N, 8, W)); c = cl[..., None]; tr = (4 * bb + rng.integers(0, 15, (N, 8, W, 1))) % 15
    off = ((b != 3) & (tr < np.where(c == 1, 5, np.where((c == 0) | (c == 2), 4, 0)))) | ((c == 2) & (b == 3))
    sg = np.where(b == 3, 1, 2 * rng.integers(0, 2, (N, 8, W, 16)) - 1); step = np.where(off, EPS + 1, np.where(c < 2, EPS, 0))
    X = np.where(c == 3, (p + 8) & 15, p + sg * step)
    na = rng.choice(np.array([0, 4, 5, 11, 12, 16]), (N, 8, P, 1)); kind = rng.integers(0, 5, (N, 8, P, 1)); o = np.argsort(rng.random((N, 8, P, 16)), axis=3)
    dis = np.where(kind < 3, kind + 1, np.where(o - na < np.where(kind == 3, 9, 8), 2, 1))
    R = pick(rng, cl, np.where(o < na, np.where((o & 1) == 1, 0, 4), dis)); h = P // 4
    R[:, 5, :h] = S * np.arange(h).reshape(1, h, 1) + (b & (S - 1)); R[:, 5, h:2 * h] = (W - 1) * rng.integers(0, 2, (N, h, 16))
    y = np.repeat(pr.reshape(1, 8, 16, 1), P, axis=3); y = np.repeat(y, N, axis=0); y[..., 7::8] = (y[..., 7::8] + 8) & 15
    way = rng.integers(0, 4, (N, 8, 16, W)); L = np.where(way == 0, np.arange(W), np.where(way == 1, 0, np.where(way == 2, W - 1, rng.integers(0, W, (N, 8, 16, W)))))
    L[:, 2] = np.arange(W); L[:, 3] = rng.integers(0, W, (N, 16, W)); L[:, 6] = rng.integers(0, W, (N, 16, W))
    w = rng.integers(0, W, (N, 8, 16)); w[:, 0] = 0; w[:, 1] = W - 1; w[:, 2] = 1; w[:, 3] = 0; w[:, 3, 15] = W - 1; w[:, 4] = 0; w[:, 4, 0] = 1
    return pack(turned(X), L, R, y, w)
def setup_inputs_crowd(rng):
    X, L, R, y, w, pr = world(rng); bc = rng.integers(1, W - 1, 8); b2 = rng.integers(1, W - 1, 8)
    for g in range(8):
        for q in range(N):
            X[q, g, :, b2[g]] = pr[g, (q >> 1) & 1]; X[q, g, :, bc[g]] = pr[g, q & 1]
        if (g & 3) < 2:
            one = np.argsort(rng.random((N, P, 16)), axis=2) == 0
            R[:, g] = np.where(one, R[:, g], bc[g]) if (g & 3) == 1 else bc[g]
        elif (g & 3) == 2: R[:, g] = rng.choice(np.array([0, bc[g], W - 1]), (N, P, 16))
        L[:, g] = rng.choice(np.array([bc[g], b2[g], 0, W - 1]), (N, 16, W)) if (g & 1) == 1 else b2[g]
    flood(rng, X, R, y)
    return pack(X, L, R, y, w)
def setup_inputs_calm(rng):
    pr = rng.integers(0, 16, (8, 16)); p = pr.reshape(1, 8, 16, 1)
    cl = (rng.random((8, W)) < (0.3 + 0.05 * rng.permutation(8)).reshape(8, 1)).astype(np.int64); cl[:, 1] = 0; cl[:, W - 1] = 1
    X = np.minimum(np.where(cl.reshape(1, 8, 1, W) == 1, (p + 8) & 15, p) + rng.integers(0, 2, (N, 8, 16, W)), 15)
    X[..., 0::2] = rng.integers(0, 16, (N, 8, 16, W // 2))
    y = np.minimum(p + rng.integers(0, 2, (N, 8, 16, P)), 15); w = 2 * rng.integers(0, W // 2, (N, 8, 16))
    o = np.argsort(rng.random((N, 8, P)), axis=2); c = np.where(o < P // 4, 5, rng.integers(6, 17, (N, 8, P)))
    few = np.array([0, 2, 1, 3])[(np.arange(N) + int(rng.integers(0, 4))) & 3]
    for q in range(N):
        for g in rng.permutation(8)[:int(few[q])]:
            c[q, g, np.argmax(o[q, g])] = rng.integers(0, 5)
    near = np.argsort(rng.random((N, 8, P, 16)), axis=3) < c[..., None]
    L = np.zeros((N, 8, 16, W), np.int64); R = np.zeros((N, 8, P, 16), np.int64); odd = np.arange(1, W, 2)
    for g in range(8):
        good, far = odd[cl[g, odd] == 0], odd[cl[g, odd] == 1]
        L[:, g] = np.where(cl[g] == 0, good[rng.integers(0, len(good), (N, 16, W))], far[rng.integers(0, len(far), (N, 16, W))])
        R[:, g] = np.where(near[:, g], good[rng.integers(0, len(good), (N, P, 16))], far[rng.integers(0, len(far), (N, P, 16))])
    return pack(X, L, R, y, w)
def check_inputs(d):
    bad = []
    for k, hi in (("xc", 15), ("lsr", W - 1), ("jur", W - 1), ("own", 15), ("wgt", W - 1)):
        v = np.asarray(d[k]).astype(np.float64)
        if not (np.min(v) >= 0 and np.max(v) <= hi): bad.append("range of " + k)
        elif np.any(v != np.floor(v)): bad.append("whole numbers of " + k)
    return bad
def reference(xc, lsr, jur, own, wgt):
    X = xc.astype(np.float32).astype(np.int32).reshape(N, 8, 16, W); L = lsr.astype(np.int64).reshape(N, 8, 16, W)
    R = np.stack([gentries(a) for a in jur]).astype(np.int64).reshape(N, 8, P, 16)
    y = own.astype(np.float32).astype(np.int32).reshape(N, 8, 16, P); w = wgt.astype(np.int64).reshape(N, 8, 16, 1)
    A = np.zeros(N, np.int64); k = np.arange(16); g3 = np.arange(8).reshape(8, 1, 1); g2 = np.arange(8).reshape(8, 1); i2 = np.arange(P).reshape(1, P); b3 = k.reshape(1, 16, 1)
    for t in range(V):
        for r in range(N):
            q = (r + t) % N; old = R[r].copy()
            x = np.take_along_axis(X[q], old.reshape(8, 1, 16 * P), 2).reshape(8, 16, P, 16)
            n = L[q][g3, (k + t) & 15, old]
            z = np.take_along_axis(X[q], n.reshape(8, 1, 16 * P), 2).reshape(8, 16, P, 16)
            v = y[r]; d = np.abs(x - v[..., None])
            a = np.sum(d <= EPS, axis=1) >= AG; c = np.sum(a, axis=2)
            lost = c <= LO + (A[q] & 1)
            rho = np.argmax(np.sum(d > EPS, axis=3) >= MAJ, axis=1)
            e = np.argmin(np.where(a, 1000, np.sum(d, axis=1)), axis=2)
            v = np.where(lost[:, None, :] & (b3 == rho[:, None, :]), x[g2, rho, i2, e][:, None, :], v)
            a = np.sum(np.abs(x - v[..., None]) <= EPS, axis=1) >= AG; c = np.sum(a, axis=2)[..., None]
            u = np.sum(w[q] * v, axis=1) & (W - 1)
            za = np.sum(np.abs(z - v[..., None]) <= EPS, axis=1) >= AG
            far = (((old * u[..., None]) >> 5) + old + 37 * k) & (W - 1)
            new = np.where((c >= WIN) & a, np.where(za, n, far), np.where((c > LO) & (c < WIN) & ~a, n, old))
            col = (S * i2 + (u & (S - 1)))[:, None, :]
            if t < V - 1: X[q][g3, b3, col] = v
            L[q][g3, b3, col] = new.transpose(0, 2, 1)
            R[r] = new; y[r] = v; A[q] = np.sum(lost)
    return {"yj": np.ascontiguousarray(R.transpose(0, 1, 3, 2)).reshape(N, 128, P).astype(np.float32), "yo": y.reshape(N, 128, P).astype(np.float32).astype(BF),
            "yz": np.sum(L * (k + 1).reshape(1, 1, 16, 1), axis=2).astype(np.float32)}

@@ -1,0 +1,634 @@
+import numpy as np
+from concourse.mybir import AluOpType, ActivationFunctionType
+
+ALU = AluOpType
+ACT = ActivationFunctionType
+NV, W, P, Q = 5, 4096, 256, 128
+OFF = 192.0 * 4096.0
+BIG16 = 1.5 * 2.0 ** 27
+BIG32 = 1.5 * 2.0 ** 28
+GCH = 4
+FZS = [1, 2]
+ZORD = [[0, 1, 2, 3], [3, 0, 1, 2], [2, 0, 3, 1], [1, 0, 2, 3], [0, 1, 2, 3]]
+UMS = [False, False]
+SENDF = True
+LCH = 8
+
+SCRATCH = {
+    "tab": ("sbuf", [128, W], "float32"), "lst": ("sbuf", [128, W], "int32"), "xb": ("sbuf", [128, W], "bfloat16"),
+    "jin": ("sbuf", [128, P], "int32"), "wi": ("sbuf", [128, 8], "int32"), "wj": ("sbuf", [128, 8], "int32"), "wf": ("sbuf", [128, 8], "float32"),
+    "ybuf": ("sbuf", [128, NV * P], "bfloat16"), "ynew": ("sbuf", [128, NV * P], "bfloat16"),
+    "roff": ("sbuf", [128, NV * P], "uint16"), "rnew": ("sbuf", [128, NV * P], "uint16"),
+    "noff": ("sbuf", [128, P], "uint16"), "soff": ("sbuf", [128, 16], "uint16"), "bcoff": ("sbuf", [128, 8], "uint16"),
+    "acc": ("sbuf", [128, 16], "float32"), "biasa": ("sbuf", [128, 8], "float32"), "toti": ("sbuf", [128, 8], "int32"),
+    "sm": ("sbuf", [128, 64], "float32"), "smi": ("sbuf", [128, 64], "int32"), "dl": ("sbuf", [128, 32], "bfloat16"),
+    "yzt": ("sbuf", [128, P], "float32"), "yzo": ("sbuf", [128, P], "float32"),
+    "ci": ("sbuf", [128, 16], "int32"), "cf": ("sbuf", [128, 16], "float32"),
+    "bo8": ("sbuf", [128, 8], "float32"), "bo512": ("sbuf", [128, 8], "bfloat16"), "wj32": ("sbuf", [128, 8], "float32"), "nwj": ("sbuf", [128, 8], "bfloat16"),
+    "wsel": ("sbuf", [128, 144], "bfloat16"), "io144": ("sbuf", [128, 144], "float32"),
+    "onesb": ("sbuf", [128, 512], "bfloat16"), "yc": ("sbuf", [128, P], "bfloat16"),
+}
+for _h in range(2):
+    SCRATCH["pg%d" % _h] = ("sbuf", [128, 16 * Q], "float32")
+    for _n in ("d", "ad", "far", "zg", "fz"):
+        SCRATCH["%s%d" % (_n, _h)] = ("sbuf", [128, 16 * Q], "bfloat16")
+    SCRATCH["dm%d" % _h] = ("sbuf", [128, 32 * Q], "bfloat16")
+    for _n in ("zb", "zl", "zi"):
+        SCRATCH["%s%d" % (_n, _h)] = ("sbuf", [128, 160], "bfloat16")
+for _n in ("sa", "fl", "sl", "cb", "m", "dr", "dr2", "rr", "dT", "tt", "s2", "sw", "gam", "bet"):
+    SCRATCH[_n] = ("sbuf", [128, P], "bfloat16")
+SCRATCH["fp"] = ("sbuf", [128, 2 * P], "bfloat16")
+SCRATCH["toff"] = ("sbuf", [128, 16], "uint16")
+SCRATCH["basel"] = ("sbuf", [128, 16], "float32")
+SCRATCH["cg160"] = ("sbuf", [128, 160], "float32")
+SCRATCH["pm160"] = ("sbuf", [128, 160], "float32")
+SCRATCH["rf"] = ("sbuf", [128, NV * P], "float32")
+SCRATCH["nw"] = ("sbuf", [128, NV * P], "float32")
+for _n in ("nf", "ks", "us", "us2", "y4", "g1", "t2"):
+    SCRATCH[_n] = ("sbuf", [128, P], "float32")
+for _n in ("ui", "um", "pi", "qi", "si", "fi"):
+    SCRATCH[_n] = ("sbuf", [128, P], "int32")
+for _n in ("ib", "nib", "i4096", "iz", "i3", "n3i", "i17", "i32", "bo", "l1", "l2", "tri", "vc", "v2c", "cy", "kc", "mneg", "mneg2", "wh", "wl", "w16"):
+    SCRATCH[_n] = ("sbuf", [128, 128], "bfloat16")
+for _n in ("pmc", "cg", "cm", "iff", "e16", "o16", "rmax", "rmin", "tmp1", "tmp2", "tmp3", "tmp4"):
+    SCRATCH[_n] = ("sbuf", [128, 128], "float32")
+for _b in range(8):
+    SCRATCH["ps%d" % _b] = ("psum", [128, 512], "float32")
+
+SEMAPHORES = (["sV", "sS", "sT", "sG", "sent", "ldw", "ldj", "ldy", "ldx0", "ldx1", "oj0", "oj1", "oy0", "oy1", "oz0", "oz1"]
+              + ["ldl%d" % i for i in range(LCH)]
+              + ["ar%d%d" % (t, h) for t in range(1, NV) for h in range(2)]
+              + ["af%d%d" % (t, h) for t in range(1, NV) for h in range(2)]
+              + ["ay%d%d" % (t, h) for t in range(1, NV) for h in range(2)])
+
+CYC = 0.00083 * 1.25
+GC, SC = 1.55, 3.8
+PEC = 0.00042 * 1.25
+HOP = 0.10
+
+
+def build(T, rem):
+    ops = []
+    ctx = {"h": "I", "n": {}}
+
+    def add(alts, r, w, banks=(), grp=None, sem=None, lat=0.0, name=""):
+        w = list(w)
+        base = (name or str(w[0][0] if isinstance(w[0], tuple) else w[0])) + ctx["h"]
+        ctx["n"][base] = ctx["n"].get(base, -1) + 1
+        ops.append({"tag": "%s%d" % (base, ctx["n"][base]), "alts": alts, "r": list(r), "w": list(w), "banks": list(banks), "grp": grp, "sem": sem, "lat": lat, "name": name})
+
+    def pk(b, a, n=1):
+        return [("ps", b, a + i) for i in range(n)]
+
+    def bk(keys):
+        return sorted(set(k[1] for k in keys if isinstance(k, tuple) and k[0] == "ps"))
+
+    def V(n, fn, r, w, name=""):
+        add([("V", 0.06 + max(64, n) * CYC, fn)], r, w, bk(list(r) + list(w)), name=name)
+
+    def S(n, fn, r, w, name=""):
+        add([("S", 0.08 + max(64, n) * CYC, fn)], r, w, bk(list(r) + list(w)), name=name)
+
+    def VS(n, fv, fs, r, w, name=""):
+        add([("V", 0.06 + n * CYC, fv), ("S", 0.08 + n * CYC, fs)], r, w, bk(list(r) + list(w)), name=name)
+
+    def G(n, fn, r, w):
+        add([("G", 0.17 + 2 * n * CYC, fn)], r, w)
+
+    def MM(mms, r, w, first=True, last=True, each=False, name=""):
+        def fn(g):
+            x = None
+            for i, (o, l, rr, c) in enumerate(mms):
+                x = g.tensor.matmul(o, l, rr, bool(each or (first and i == 0)), bool(each or (last and i == len(mms) - 1)))
+            return x
+        add([("T", 0.03 + sum(m[3] * PEC + 0.01 for m in mms), fn)], r, w, bk(w), grp=(first, last), name=name)
+
+    def DMA(q, fn, r, w, sem, val, lat):
+        add([(q, 0.1, fn)], r, w, sem=(sem, val), lat=lat)
+
+    def ts(o, i, a, b=None, op0=None, op1=None):
+        if op1 is None:
+            return lambda g: g.vector.tensor_scalar(o, i, a, None, op0)
+        return lambda g: g.vector.tensor_scalar(o, i, a, b, op0, op1)
+
+    def tt(o, a, b, op):
+        return lambda g: g.vector.tensor_tensor(o, a, b, op)
+
+    def cp(o, i):
+        return lambda g: g.vector.tensor_copy(o, i)
+
+    def act(o, i, f, bias=0.0, scale=1.0, acc=None):
+        if acc is None:
+            return lambda g: g.scalar.activation(o, i, f, bias=bias, scale=scale)
+        return lambda g: g.scalar.activation(o, i, f, bias=bias, scale=scale, accum_out=acc)
+
+    ps = [T["ps%d" % b] for b in range(8)]
+
+    cw = W // LCH
+    DMA("S", lambda g: g.scalar.dma_start(T.jin[:], T.jur[:]), [], ["jin"], "ldj", 16, 3.0)
+    DMA("Y", lambda g: g.sync.dma_start(T.ybuf[:, 0:P], T.own[:]), [], [("y", 0, 0), ("y", 0, 1)], "ldy", 16, 3.0)
+    DMA("Y", lambda g: g.sync.dma_start(T.xb[:, 0:W // 2], T.xc[:, 0:W // 2]), [], [("xb", c) for c in range(0, 4)], "ldx0", 16, 4.0)
+    DMA("S", lambda g: g.scalar.dma_start(T.xb[:, W // 2:W], T.xc[:, W // 2:W]), [], [("xb", c) for c in range(4, 8)], "ldx1", 16, 5.5)
+    for c in range(LCH):
+        if c % 2 == 0:
+            DMA("Y", lambda g, c=c: g.sync.dma_start(T.lst[:, c * cw:(c + 1) * cw], T.lsr[:, c * cw:(c + 1) * cw]), [], [("lst", c)], "ldl%d" % c, 16, 6.0 + 0.8 * c)
+        else:
+            DMA("S", lambda g, c=c: g.scalar.dma_start(T.lst[:, c * cw:(c + 1) * cw], T.lsr[:, c * cw:(c + 1) * cw]), [], [("lst", c)], "ldl%d" % c, 16, 6.0 + 0.8 * c)
+    DMA("G", lambda g: g.dma_start(T.wi[:, 0:1], T.wgt[:], allow_slow_non_contiguous=True), [], ["wi"], "ldw", 16, 5.0)
+
+    def iota(o, pat, base, cmul, key, n, flt=True):
+        if flt:
+            G(n, lambda g: g.iota(o, pat, base, cmul, allow_small_or_imprecise_dtypes=True), [], [key])
+        else:
+            G(n, lambda g: g.iota(o, pat, base, cmul), [], [key])
+
+    iota(T.pmc[:], [[1, 128]], 0, -1, "pmc", 128)
+    iota(T.ci[:, 0:1], [[0, 1]], 0, 1, "ci0", 1, False)
+    iota(T.cg[:], [[16, 8], [0, 16]], 0, 0, "cg", 128)
+    iota(T.cm[:], [[0, 8], [1, 16]], 0, 0, "cm", 128)
+    iota(T.io144[:], [[1, 144]], -15, 0, "io144", 144)
+    iota(T.ci[:, 8:16], [[1, 8]], 0, 0, "ci8", 8, False)
+    V(128, ts(T.iff[:], T.pmc[:], 0.0, None, ALU.is_equal), ["pmc"], ["iff"])
+    for nm, sc in (("i4096", 4096.0), ("ib", 1.0), ("nib", -1.0), ("iz", 3.0 / 4096), ("i3", 3.0), ("n3i", -3.0), ("i17", 2.0 ** 17), ("i32", 32.0)):
+        S(128, act(T[nm][:], T.iff[:], ACT.Copy, scale=sc), ["iff"], [nm])
+    V(1, ts(T.ci[:, 1:2], T.ci[:, 0:1], 0x70, None, ALU.bitwise_and), ["ci0"], ["ci1"])
+    V(1, ts(T.ci[:, 2:3], T.ci[:, 0:1], 15, None, ALU.bitwise_and), ["ci0"], ["ci2"])
+    V(2, cp(T.cf[:, 1:3], T.ci[:, 1:3]), ["ci1", "ci2"], ["cf"])
+    pg16, pm = T.cf[:, 1:2], T.cf[:, 2:3]
+    V(128, ts(T.bo[:], T.cg[:], pg16, None, ALU.is_equal), ["cg", "cf"], ["bo"])
+    V(8, ts(T.bo8[:], T.cg[:, 0:128:16], pg16, None, ALU.is_equal), ["cg", "cf"], ["bo8"])
+    V(8, ts(T.bo512[:], T.bo8[:], 512.0, None, ALU.mult), ["bo8"], ["bo512"])
+    V(1, ts(T.cf[:, 3:4], pm, 1.0, None, ALU.add), ["cf"], ["cf3"])
+    V(8, ts(T.wj32[:], T.bo8[:], T.cf[:, 3:4], None, ALU.mult), ["bo8", "cf3"], ["wj32"])
+    V(8, ts(T.nwj[:], T.wj32[:], -1.0, None, ALU.mult), ["wj32"], ["nwj"])
+    V(144, ts(T.wsel[:], T.io144[:], pg16, None, ALU.is_equal), ["io144", "cf"], ["wsel"])
+    V(128, ts(T.tmp1[:], T.pmc[:], 0.0, 64.0, ALU.is_equal, ALU.mult), ["pmc"], ["tmp1"])
+    V(256, tt(T.l1[:], T.tmp1[:], T.bo[:], ALU.add), ["tmp1", "bo"], ["l1"])
+    V(128, ts(T.tmp1[:], T.pmc[:], 0.0, -7.0, ALU.is_equal, ALU.mult), ["pmc"], ["tmp1"])
+    V(256, tt(T.tmp2[:], T.tmp1[:], T.bo[:], ALU.add), ["tmp1", "bo"], ["tmp2"])
+    V(128, ts(T.l2[:], T.tmp2[:], 1.125, None, ALU.mult), ["tmp2"], ["l2"])
+    V(64, lambda g: g.vector.memset(T.v2c[:], -7.875), [], ["v2c"])
+    V(256, lambda g: g.vector.memset(T.onesb[:], 1.0), [], ["onesb"])
+    V(128, lambda g: g.vector.memset(T.o16[:], 1.0 / 16), [], ["o16"])
+    V(128, lambda g: g.vector.memset(T.yc[:], 136.0 * OFF), [], ["yc"])
+    V(64, lambda g: g.vector.memset(T.biasa[:, 0:1], 7.0), [], [("bias", 0)])
+    V(64, lambda g: g.vector.memset(T.cy[:], -OFF), [], ["cy"])
+    G(128, lambda g: g.affine_select(T.cy[:], T.cy[:], [[0, 128]], ALU.not_equal, 2048.0, -1, 1), ["cy"], ["cy"])
+    G(128, lambda g: g.affine_select(T.cy[:], T.cy[:], [[0, 128]], ALU.not_equal, -0.5, -2, 1), ["cy"], ["cy"])
+    V(128, ts(T.tmp3[:], T.cm[:], 0.0, None, ALU.is_equal), ["cm"], ["tmp3"])
+    V(128, ts(T.tmp1[:], T.pmc[:], 0.0, None, ALU.is_gt), ["pmc"], ["tmp1"])
+    V(256, tt(T.tmp1[:], T.tmp1[:], T.tmp3[:], ALU.max), ["tmp1", "tmp3"], ["tmp1"])
+    V(256, tt(T.tmp1[:], T.tmp1[:], T.bo[:], ALU.mult), ["tmp1", "bo"], ["tmp1"])
+    V(128, ts(T.tmp2[:], T.tmp3[:], 16.0, 1.0, ALU.mult, ALU.add), ["tmp3"], ["tmp2"])
+    V(256, tt(T.tmp2[:], T.tmp2[:], T.iff[:], ALU.mult), ["tmp2", "iff"], ["tmp2"])
+    V(256, tt(T.tmp2[:], T.tmp2[:], T.tmp1[:], ALU.subtract), ["tmp2", "tmp1"], ["tmp2"])
+    V(128, ts(T.tri[:], T.tmp2[:], 1.0 / 64, None, ALU.mult), ["tmp2"], ["tri"])
+    V(128, ts(T.tmp1[:], T.cm[:], -1.0 / 64, -1.0, ALU.mult, ALU.add), ["cm"], ["tmp1"])
+    V(128, ts(T.tmp2[:], T.tmp3[:], 1.0 / 32, None, ALU.mult), ["tmp3"], ["tmp2"])
+    V(256, tt(T.vc[:], T.tmp1[:], T.tmp2[:], ALU.add), ["tmp1", "tmp2"], ["vc"])
+    V(128, ts(T.kc[:], T.cm[:], 32.0, None, ALU.mult), ["cm"], ["kc"])
+    V(1, ts(T.cf[:, 4:5], pm, 37.0, None, ALU.mult), ["cf"], ["cf4"])
+    iota(T.cg160[:], [[16, 10], [0, 16]], -16, 0, "cg160", 160)
+    iota(T.pm160[:], [[1, 160]], -16, -1, "pm160", 160)
+    iota(T.e16[:], [[16, 128]], 8192, 0, "e16", 128)
+    V(1, ts(T.ci[:, 3:4], T.ci[:, 0:1], 4, 1, ALU.logical_shift_right, ALU.bitwise_and), ["ci0"], ["ci3"])
+    V(1, cp(T.cf[:, 7:8], T.ci[:, 3:4]), ["ci3"], ["cf7"])
+    V(1, ts(T.cf[:, 6:7], T.cf[:, 7:8], -1.0, 1.0, ALU.mult, ALU.add), ["cf7"], ["cf6"])
+    V(2, ts(T.cf[:, 8:10], T.cf[:, 6:8], pm, None, ALU.mult), ["cf6", "cf7", "cf"], ["cf8"])
+    V(2, ts(T.cf[:, 10:12], T.cf[:, 6:8], 2048.0, None, ALU.mult), ["cf6", "cf7"], ["cf10"])
+    for e in range(2):
+        V(160, ts(T["zb%d" % e][:], T.cg160[:], pg16, T.cf[:, 8 + e:9 + e], ALU.is_equal, ALU.mult), ["cg160", "cf", "cf8"], ["zb%d" % e])
+        V(160, ts(T["zl%d" % e][:], T.cg160[:], pg16, T.cf[:, 10 + e:11 + e], ALU.is_equal, ALU.mult), ["cg160", "cf", "cf10"], ["zl%d" % e])
+        V(160, ts(T["zi%d" % e][:], T.pm160[:], 0.0, T.cf[:, 6 + e:7 + e], ALU.is_equal, ALU.mult), ["pm160", "cf6", "cf7"], ["zi%d" % e])
+        for c in range(4):
+            S(512, act(T["dm%d" % e][:, c * 512:(c + 1) * 512], T.onesb[:], ACT.Copy, scale=OFF), ["onesb"], [("dmc", e)])
+        V(1, ts(T.cf[:, 12 + e:13 + e], pm, 4.0 * (4 - FZS[e]) - 0.5, -11.5, ALU.is_gt, ALU.mult), ["cf"], [("thr", e)])
+        V(1, ts(T.cf[:, 12 + e:13 + e], T.cf[:, 12 + e:13 + e], 36.5, None, ALU.add), [("thr", e)], [("thr", e)])
+    V(128, ts(T.tmp4[:], T.cm[:], pm, None, ALU.is_equal), ["cm", "cf"], ["tmp4"])
+    V(256, tt(T.tmp4[:], T.tmp4[:], T.e16[:], ALU.mult), ["tmp4", "e16"], ["tmp4"])
+    V(128, ts(T.mneg2[:], T.tmp4[:], -8192.0, None, ALU.add), ["tmp4"], ["mneg2"])
+    V(128, ts(T.mneg[:], T.cm[:], pm, -8192.0, ALU.not_equal, ALU.mult), ["cm", "cf"], ["mneg"])
+    V(128, ts(T.rmax[:], T.tmp3[:], -65536.0, None, ALU.mult), ["tmp3"], ["rmax"])
+    V(128, ts(T.rmin[:], T.tmp3[:], 2.0 ** 21, None, ALU.mult), ["tmp3"], ["rmin"])
+    V(8, cp(T.bcoff[:], T.ci[:, 8:16]), ["ci8"], ["bcoff"])
+    for e in range(2):
+        V(8, ts(T.basel[:, 8 * e:8 * e + 8], T.cg[:, 0:128:16], pm, 16.0, ALU.add, ALU.mult), ["cg", "cf"], ["basel"])
+    for c, mk in ((1, 0xFC0), (2, 63), (3, 15)):
+        V(1, ts(T.wj[:, c:c + 1], T.wi[:, 0:1], mk, None, ALU.bitwise_and), ["wi"], [("wj", c)])
+    V(3, cp(T.wf[:, 1:4], T.wj[:, 1:4]), [("wj", 1), ("wj", 2), ("wj", 3)], ["wf"])
+    for c, nm in ((1, "wh"), (2, "wl"), (3, "w16")):
+        V(64, ts(T[nm][:], T.bo[:], T.wf[:, c:c + 1], None, ALU.mult), ["bo", "wf"], [nm])
+    V(256, cp(T.roff[:, 0:P], T.jin[:]), ["jin"], [("r", 0, 0), ("r", 0, 1)])
+
+    for c in range(8):
+        b = 2 + c % 2
+        cs = slice(c * 512, (c + 1) * 512)
+        MM([(ps[b][:, 0:512], T.i4096[:], T.xb[:, cs], 512)], ["i4096", ("xb", c)], pk(b, 0, 4))
+        V(512, tt(T.tab[:, cs], T.lst[:, cs], ps[b][:, 0:512], ALU.add), [("lst", c * 512 // cw)] + pk(b, 0, 4), [("tabc", c)])
+    TAB = [("tab", 0), ("tab", 1)]
+    zb = [0]
+
+    for t in range(NV):
+        TABR = TAB + ([("tabc", c) for c in range(8)] if t == 0 else [])
+        ctx["n"] = {}
+        for h in range(2):
+            ctx["h"] = "AB"[h]
+            hs = slice(h * Q, (h + 1) * Q)
+            o = t * P + h * Q
+            ts_ = slice(o, o + Q)
+            pg, d, ad, far, dm, zg, fz = (T["%s%d" % (n, h)] for n in ("pg", "d", "ad", "far", "dm", "zg", "fz"))
+            K = lambda n, h=h: (n, h)
+            B = ps[h]
+            y = T.ybuf[:, ts_]
+            yk = ("y", t, h)
+            pw = Q // GCH
+            PG = [("pg", h, c) for c in range(GCH)]
+            ZG = [("zg", h, c) for c in range(GCH)]
+            r4 = lambda b, i: ps[b][:, i * Q:(i + 1) * Q]
+            for c in range(GCH):
+                offs = T.roff[:, o + c * pw:o + (c + 1) * pw]
+                out = pg[:, c * pw * 16:(c + 1) * pw * 16]
+                VS(16 * pw * GC, (lambda g, out=out, offs=offs: g.vector.tensor_copy(out, T.tab[:, 0:W].indirect(offs))),
+                   (lambda g, out=out, offs=offs: g.scalar.activation(out, T.tab[:, 0:W].indirect(offs), ACT.Copy)),
+                   TABR + [("r", t, h)], [("pg", h, c)], name="G1")
+            rf, rfk = T.rf[:, ts_], ("rf", t, h)
+            if t == 0 or not SENDF:
+                V(128, cp(rf, T.roff[:, ts_]), [("r", t, h)], [rfk])
+            pb = 6 + h
+            RP, R37, NC, NMR = (r4(pb, i) for i in range(4))
+            S(128, act(RP, rf, ACT.Copy), [rfk], pk(pb, 0), name="RP")
+            S(128, act(R37, rf, ACT.Identity, bias=T.cf[:, 4:5]), [rfk, "cf4"], pk(pb, 1), name="R37")
+            MM([(B[:, 0:512], T.cy[0:3, :], T.onesb[0:3, :], 512)] + [(B[:, kk:512:4], T.i4096[:], y, 128) for kk in range(4)],
+               ["cy", "onesb", "i4096", yk], pk(h, 0, 4), name="ybc")
+            for q in range(4):
+                MM([(ps[pb][:, 2 * Q + k:3 * Q:16], pg[:, k:16 * Q:16], T.iff[:, (k + t) % 16:128:16], 256) for k in range(4 * q, 4 * q + 4)],
+                   PG + ["iff"], [("ps", pb, 2)], each=True, name="NT")
+            S(128, act(T.nf[:, hs], NC, ACT.Identity, bias=OFF), pk(pb, 2), [K("nf")])
+            S(128, act(T.rr[:, hs], NC, ACT.Identity, bias=OFF - 2047.5), pk(pb, 2), [K("rr")])
+            MM([(NC, T.nf[:, hs], T.iff[:], 512), (NC, T.rr[:, hs], T.nib[:], 128)], [K("nf"), K("rr"), "iff", "nib"], pk(pb, 2), name="NC")
+            V(128, cp(T.noff[:, hs], NC), pk(pb, 2), [K("noff")])
+            V(128, tt(NMR, NC, rf, ALU.subtract), pk(pb, 2) + [rfk], pk(pb, 3), name="NMR")
+            for c in range(GCH):
+                offs = T.noff[:, h * Q + c * pw:h * Q + (c + 1) * pw]
+                out = zg[:, c * pw * 16:(c + 1) * pw * 16]
+                VS(16 * pw * GC, (lambda g, out=out, offs=offs: g.vector.tensor_scalar(out, T.tab[:, 0:W].indirect(offs), OFF - 2047.5, None, ALU.add)),
+                   (lambda g, out=out, offs=offs: g.scalar.activation(out, T.tab[:, 0:W].indirect(offs), ACT.Identity, bias=OFF - 2047.5)),
+                   TABR + [K("noff")], [("zg", h, c)], name="G2")
+            for q in range(4):
+                qs = slice(q * 512, (q + 1) * 512)
+                V(512, tt(d[:, q:16 * Q:4], pg[:, q:16 * Q:4], B[:, 0:512], ALU.subtract), PG + pk(h, 0, 4), [("d", h, q)], name="SUB")
+                S(512, act(ad[:, qs], d[:, q:16 * Q:4], ACT.Abs, bias=-192.0, scale=1.0 / 4096), [("d", h, q)], [("ad", h, q)], name="ABS")
+                V(256, ts(far[:, qs], ad[:, qs], 2.5, None, ALU.is_gt), [("ad", h, q)], [("far", h, q)], name="FAR")
+            col = lambda buf, k: buf[:, (k % 4) * 512 + k // 4:(k % 4 + 1) * 512:4]
+            sel = lambda k: T.wsel[:, 15 - k:143 - k]
+            for q in range(4):
+                MM([(r4(4, h), sel(k), col(far, k), 128) for k in range(q, 16, 4)], ["wsel", ("far", h, q)], pk(4, h), first=q == 0, last=q == 3, name="CNT")
+                MM([(r4(5, h), T.ib[:], col(far, k), 128) for k in range(q, 16, 4)], ["ib", ("far", h, q)], pk(5, h), first=q == 0, last=q == 3, name="BB")
+            S(128, act(T.sa[:, hs], r4(4, h), ACT.Sign, bias=4.5, scale=-1.0), pk(4, h), [K("sa")])
+            VS(128, cp(T.cb[:, hs], r4(4, h)), act(T.cb[:, hs], r4(4, h), ACT.Copy), pk(4, h), [K("cb")])
+            S(128, act(T.fl[:, hs], r4(5, h), ACT.Sign, bias=-8.5), pk(5, h), [K("fl")])
+            MM([(r4(h, 0), T.bo[:], T.sa[:, hs], 128)], ["bo", K("sa")], pk(h, 0))
+            MM([(r4(h, 1), T.vc[0:1, :], T.onesb[0:1, 0:Q], 128), (r4(h, 1), T.tri[:], T.fl[:, hs], 128)], ["vc", "onesb", "tri", K("fl")], pk(h, 1))
+            S(128, act(T.sl[:, hs], r4(h, 0), ACT.Sign, bias=T.biasa[:, t:t + 1], acc=T.acc[:, 2 * t + h:2 * t + h + 1]), pk(h, 0) + [("bias", t)], [K("sl"), ("acc", t, h)])
+            V(128, tt(T.m[:, hs], r4(h, 1), T.sl[:, hs], ALU.is_gt), pk(h, 1) + [K("sl")], [K("m")], name="m")
+            MM([(r4(4, 2 + h), T.onesb[0:1, 0:Q], T.kc[0:1, :], 128), (r4(4, 2 + h), T.sa[:, hs], T.i17[:], 128)]
+               + [(ps[4][:, (2 + h) * Q + k:(3 + h) * Q:16], col(ad, k), T.bo512[:], 64) for k in range(16)],
+               ["onesb", "kc", "i17", "bo512", K("sa"), K("m")] + [("ad", h, q) for q in range(4)], pk(4, 2 + h), last=False, name="KEY")
+            for c in range(2):
+                V(512, (lambda g, c=c, d=d, dm=dm: g.vector.transpose(dm[:, 2048 + c * 1024:3072 + c * 1024], d[:, c * 1024:(c + 1) * 1024])),
+                  [("d", h, q) for q in range(4)], [("dm", h, c)], name="TR")
+            mm = [(r4(h, 2), T.ib[:], T.mneg2[:], 128)]
+            for g0 in range(2):
+                for j0 in range(2):
+                    sft = 16 * (1 - (j0 - g0))
+                    for nm in ("zb", "zl"):
+                        mm.append((B[:, 2 * Q + g0:3 * Q:2], T["%s%d" % (nm, g0)][:, sft:sft + 128], T.m[:, h * Q + j0:(h + 1) * Q:2], 64))
+            MM(mm, ["ib", "mneg2", "zb0", "zb1", "zl0", "zl1", K("m")], pk(h, 2), name="RHO")
+            V(128, lambda g, h=h, hs=hs, B=B: g.vector.tensor_tensor_scan(T.us[:, hs], T.rmax[:], B[:, 2 * Q:3 * Q], 0.0, ALU.add, ALU.max),
+              ["rmax"] + pk(h, 2), [K("us")], name="rscan")
+            V(8, cp(T.toff[:, 8 * h:8 * h + 8], T.us[:, h * Q + 15:(h + 1) * Q:16]), [K("us")], [K("toff")])
+            VS(128 * GC, (lambda g, h=h, hs=hs, dm=dm: g.vector.tensor_scalar(T.dr2[:, hs], dm[:, 0:4096].indirect(T.toff[:, 8 * h:8 * h + 8]), 1.0 / 4096, -192.0, ALU.mult, ALU.add)),
+               (lambda g, h=h, hs=hs, dm=dm: g.scalar.activation(T.dr2[:, hs], dm[:, 0:4096].indirect(T.toff[:, 8 * h:8 * h + 8]), ACT.Identity, bias=-192.0, scale=1.0 / 4096)),
+               [K("toff"), ("dm", h, 0), ("dm", h, 1), K("dmc")], [K("dr2")], name="dr2")
+            for j0 in range(2):
+                MM([(B[:, 3 * Q + j0:4 * Q:2], T["zi%d" % j0][:, 16 * (1 - (g0 - j0)):16 * (1 - (g0 - j0)) + 128], T.dr2[:, h * Q + g0:(h + 1) * Q:2], 64) for g0 in range(2)],
+                   ["zi0", "zi1", K("dr2")], pk(h, 3), name="DR")
+            VS(128, cp(T.dr[:, hs], r4(h, 3)), act(T.dr[:, hs], r4(h, 3), ACT.Copy), pk(h, 3), [K("dr")], name="dr")
+            MM([(r4(4, 2 + h), T.dr[:, hs], T.ib[:], 128)], [K("dr"), "ib"], pk(4, 2 + h), first=False, name="KEY2")
+            V(128, lambda g, h=h, hs=hs: g.vector.tensor_tensor_scan(T.ks[:, hs], T.rmin[:], ps[4][:, (2 + h) * Q:(3 + h) * Q], 0.0, ALU.add, ALU.min),
+              ["rmin"] + pk(4, 2 + h), [K("ks")])
+            kl = T.ks[:, h * Q + 15:(h + 1) * Q:16]
+            V(8, ts(T.sm[:, 8 * h:8 * h + 8], kl, BIG32, BIG32, ALU.add, ALU.subtract), [K("ks")], [K("hi")])
+            V(16, tt(T.dl[:, 16 * h:16 * h + 8], kl, T.sm[:, 8 * h:8 * h + 8], ALU.subtract), [K("ks"), K("hi")], [K("dl")])
+            VS(128 * GC, (lambda g, h=h, hs=hs: g.vector.tensor_copy(T.dT[:, hs], T.dl[:, 16 * h:16 * h + 8].indirect(T.bcoff[:, 0:8]))),
+               (lambda g, h=h, hs=hs: g.scalar.activation(T.dT[:, hs], T.dl[:, 16 * h:16 * h + 8].indirect(T.bcoff[:, 0:8]), ACT.Copy)),
+               [K("dl"), "bcoff"], [K("dT")])
+            MM([(r4(h, 0), T.dT[:, hs], T.ib[:], 128)], [K("dT"), "ib"], pk(h, 0))
+            MM([(r4(h, 2), T.i3[:], T.dr[:, hs], 128)], [K("dr"), "i3"], pk(h, 2))
+            MM([(r4(h, 1), T.i3[:], T.dr[:, hs], 128), (r4(h, 1), T.dT[:, hs], T.n3i[:], 128)], [K("dr"), K("dT"), "i3", "n3i"], pk(h, 1))
+            V(128, tt(T.tt[:, hs], r4(h, 0), T.m[:, hs], ALU.mult), pk(h, 0) + [K("m")], [K("tt")])
+            V(256, ts(T.fp[:, 2 * h * Q:2 * (h + 1) * Q], B[:, Q:3 * Q], BIG16, BIG16, ALU.add, ALU.not_equal), pk(h, 1, 2), [K("fp")])
+            MM([(r4(h, 3), T.ib[:], y, 128), (r4(h, 3), T.ib[:], T.tt[:, hs], 128)], ["ib", yk, K("tt")], pk(h, 3))
+            yn = T.ynew[:, ts_]
+            ynk = ("yn", t, h)
+            VS(128, cp(yn, r4(h, 3)), act(yn, r4(h, 3), ACT.Copy), pk(h, 3), [ynk], name="ynew")
+            S(128, act(T.y4[:, hs], yn, ACT.Copy, scale=4096.0), [ynk], [K("y4")])
+            if t < NV - 1:
+                DMA("G", rem(T.ybuf[:, o + P:o + P + Q], yn, "ay%d%d" % (t + 1, h)), [ynk], [("y", t + 1, h)], "ay%d%d" % (t + 1, h), rem(None, None, None), 3.0)
+            else:
+                DMA("Y", lambda g, yn=yn, hs=hs: g.sync.dma_start(T.yo[:, hs], yn), [ynk], [K("yo")], "oy%d" % h, 16, 2.0)
+            MM([(r4(h, 0), T.ib[:], T.cb[:, hs], 128), (r4(h, 0), T.ib[:], T.fp[:, 2 * h * Q:(2 * h + 1) * Q], 128), (r4(h, 0), T.nib[:], T.fp[:, (2 * h + 1) * Q:(2 * h + 2) * Q], 128)],
+               ["ib", "nib", K("cb"), K("fp")], pk(h, 0))
+            S(128, act(T.s2[:, hs], r4(h, 0), ACT.Sign, bias=4.5, scale=-1.0), pk(h, 0), [K("s2")])
+            MM([(r4(h, 1), T.l1[:], T.s2[:, hs], 128)], ["l1", K("s2")], pk(h, 1))
+            MM([(r4(h, 2), T.v2c[0:1, :], T.onesb[0:1, 0:Q], 128), (r4(h, 2), T.l2[:], T.s2[:, hs], 128)], ["v2c", "onesb", "l2", K("s2")], pk(h, 2))
+            MM([(r4(h, 3), T.wh[:], yn, 128), (r4(h, 3), T.wl[:], yn, 128)], ["wh", "wl", ynk], pk(h, 3), last=not UMS[h], name="U")
+            MM([(r4(4, 2 + h), T.w16[:], yn, 128), (r4(4, 2 + h), T.ib[:], T.mneg[:], 128)], ["w16", "ib", "mneg", ynk], pk(4, 2 + h), name="U2")
+            S(128, act(T.sw[:, hs], r4(h, 1), ACT.Sign, bias=-71.0), pk(h, 1), [K("sw")])
+            V(128, ts(T.gam[:, hs], r4(h, 2), BIG16, BIG16, ALU.add, ALU.is_equal), pk(h, 2), [K("gam")])
+            V(128, cp(T.ui[:, hs], r4(h, 3)), pk(h, 3), [K("ui")])
+            V(128, ts(T.um[:, hs], T.ui[:, hs], W - 1, None, ALU.bitwise_and), [K("ui")], [K("um")])
+            V(128, tt(T.pi[:, hs], T.um[:, hs], RP, ALU.mult), [K("um")] + pk(pb, 0), [K("pi")])
+            V(128, ts(T.qi[:, hs], T.pi[:, hs], 5, None, ALU.logical_shift_right), [K("pi")], [K("qi")])
+            V(128, tt(T.si[:, hs], T.qi[:, hs], R37, ALU.add), [K("qi")] + pk(pb, 1), [K("si")])
+            V(128, ts(T.fi[:, hs], T.si[:, hs], W - 1, None, ALU.bitwise_and), [K("si")], [K("fi")])
+            V(128, tt(R37, T.fi[:, hs], NC, ALU.subtract), [K("fi")] + pk(pb, 2), pk(pb, 1), name="E")
+            V(128, tt(T.g1[:, hs], T.gam[:, hs], NMR, ALU.mult), [K("gam")] + pk(pb, 3), [K("g1")])
+            V(128, tt(RP, T.g1[:, hs], RP, ALU.add), [K("g1")] + pk(pb, 0), pk(pb, 0), name="BASE")
+            V(128, lambda g, h=h, hs=hs: g.vector.tensor_tensor_scan(T.us2[:, hs], T.rmax[:], ps[4][:, (2 + h) * Q:(3 + h) * Q], 0.0, ALU.add, ALU.max),
+              ["rmax"] + pk(4, 2 + h), [K("us2")])
+            if h == 1:
+                V(16, cp(T.smi[:, 0:16], T.us2[:, 15:P:16]), [("us2", 0), ("us2", 1)], ["sl1"])
+                V(16, ts(T.smi[:, 16:32], T.smi[:, 0:16], 15, None, ALU.bitwise_and), ["sl1"], ["sl2"])
+                V(32, tt(T.sm[:, 16:32], T.smi[:, 16:32], T.basel[:], ALU.add), ["sl2", "basel"], ["sl3"])
+                V(16, cp(T.soff[:], T.sm[:, 16:32]), ["sl3"], ["soff"])
+            late = []
+            zo = ZORD[FZS[h]]
+            for q in zo:
+                b = 2 + zb[0] % 2
+                zb[0] += 1
+                qs = slice(q * 512, (q + 1) * 512)
+                mms = []
+                for kk in range(4):
+                    mms.append((r4(b, kk), T.iz[:], zg[:, 4 * q + kk:16 * Q:16], 128))
+                    mms.append((r4(b, kk), T.n3i[:], yn, 128))
+                def zfn(g, mms=mms):
+                    x = None
+                    for i, (o_, l_, r_, c_) in enumerate(mms):
+                        x = g.tensor.matmul(o_, l_, r_, i % 2 == 0, i % 2 == 1)
+                    return x
+                add([("T", 0.03 + 8 * (128 * PEC + 0.01), zfn)], ZG + ["iz", "n3i", ynk], pk(b, 0, 4), [b], grp=(True, True), name="ZD")
+                if q < 4 - FZS[h]:
+                    V(512, ts(fz[:, qs], ps[b][:, 0:512], BIG16 - 576.0, BIG16, ALU.add, ALU.not_equal), pk(b, 0, 4), [("fz", h, q)], name="FZ")
+                else:
+                    S(512, act(ad[:, qs], ps[b][:, 0:512], ACT.Abs, bias=-576.0), pk(b, 0, 4), [("ad", h, q)], name="FZa")
+                    S(512, act(fz[:, qs], ad[:, qs], ACT.Sign, bias=-7.5), [("ad", h, q)], [("fz", h, q)], name="FZb")
+                mm = [(r4(5, 2 + h), sel(4 * q + kk), fz[:, q * 512 + kk * Q:q * 512 + (kk + 1) * Q], 128) for kk in range(4)]
+                late.append((mm, q))
+            late.sort(key=lambda x: x[1])
+            for i, (mm, q) in enumerate(late):
+                if i == 3:
+                    mm = [(r4(5, 2 + h), T.i32[:], T.sw[:, hs], 128)] + mm
+                MM(mm, ["wsel", "i32", ("fz", h, q)] + ([K("sw")] if i == 3 else []), pk(5, 2 + h), first=i == 0, last=i == 3, name="CNT2")
+            V(128, ts(T.bet[:, hs], r4(5, 2 + h), T.cf[:, 12 + h:13 + h], None, ALU.is_gt), pk(5, 2 + h) + [K("thr")], [K("bet")])
+            V(128, tt(T.t2[:, hs], T.bet[:, hs], R37, ALU.mult), [K("bet")] + pk(pb, 1), [K("t2")])
+            nw, nwk = T.nw[:, ts_], ("nw", t, h)
+            V(128, tt(nw, T.t2[:, hs], RP, ALU.add), [K("t2")] + pk(pb, 0), [nwk], name="new")
+            if t < NV - 1:
+                V(128, cp(T.rnew[:, ts_], nw), [nwk], [("rn", t, h)])
+                DMA("G", rem(T.roff[:, o + P:o + P + Q], T.rnew[:, ts_], "ar%d%d" % (t + 1, h)), [("rn", t, h)], [("r", t + 1, h)], "ar%d%d" % (t + 1, h), rem(None, None, None), 3.0)
+                if SENDF:
+                    DMA("G", rem(T.rf[:, o + P:o + P + Q], nw, "af%d%d" % (t + 1, h)), [nwk, ("rn", t, h)], [("rf", t + 1, h)], "af%d%d" % (t + 1, h), rem(None, None, None), 3.5)
+            else:
+                DMA("Y", lambda g, hs=hs, nw=nw: g.sync.dma_start(T.yj[:, hs], nw), [nwk], [K("yj")], "oj%d" % h, 16, 2.0)
+        for h in range(2):
+            hs = slice(h * Q, (h + 1) * Q)
+            nw = T.nw[:, t * P + h * Q:t * P + (h + 1) * Q]
+            V(128 * SC, (lambda g, h=h, hs=hs, nw=nw: g.vector.tensor_tensor(T.tab[:, h * 2048:(h + 1) * 2048].indirect(T.soff[:, 8 * h:8 * h + 8]), nw, T.y4[:, hs], ALU.add)),
+              ["soff", ("nw", t, h), ("y4", h)], [("tab", h)], name="SCAT%d" % h)
+        if t < NV - 1:
+            MM([(ps[5][:, Q:Q + 1], T.o16[:], T.acc[:, 2 * t:2 * t + 1], 256), (ps[5][:, Q:Q + 1], T.o16[:], T.acc[:, 2 * t + 1:2 * t + 2], 256)],
+               ["o16", ("acc", t, 0), ("acc", t, 1)], pk(5, 1))
+            V(1, cp(T.toti[:, 0:1], ps[5][:, Q:Q + 1]), pk(5, 1), ["tot1"])
+            V(1, ts(T.toti[:, 1:2], T.toti[:, 0:1], 2, None, ALU.bitwise_and), ["tot1"], ["tot2"])
+            V(1, ts(T.biasa[:, t + 1:t + 2], T.toti[:, 1:2], -1.0, 7.0, ALU.mult, ALU.add), ["tot2"], [("bias", t + 1)])
+
+    ctx["h"] = "Z"
+    for c in range(8):
+        cs = slice(c * 512, (c + 1) * 512)
+        VS(512, ts(T.xb[:, cs], T.tab[:, cs], OFF - 2047.5, None, ALU.add), act(T.xb[:, cs], T.tab[:, cs], ACT.Identity, bias=OFF - 2047.5),
+           [("tab", c // 4)], [("xb", c)], name="XR")
+    for c in range(8):
+        mm = [(ps[2][:, 0:P], T.onesb[0:1, 0:Q], T.yc[0:1, :], 256)] if c == 0 else []
+        for e in range(4 * c, 4 * c + 4):
+            mm.append((ps[2][:, e:P:32], T.xb[:, e * Q:(e + 1) * Q], T.nwj[:], 64))
+            mm.append((ps[2][:, e:P:32], T.tab[:, e * Q:(e + 1) * Q], T.wj32[:], 256))
+        MM(mm, ["onesb", "yc", "nwj", "wj32", ("xb", c), ("tab", c // 4)], pk(2, 0, 2), first=c == 0, last=c == 7, name="YZ")
+    V(256, cp(T.yzt[:], ps[2][:, 0:P]), pk(2, 0, 2), ["yzt"])
+    for h in range(2):
+        hs = slice(h * Q, (h + 1) * Q)
+        MM([(ps[h][:, 0:Q], T.yzt[:, hs], T.iff[:], 512)], ["yzt", "iff"], pk(h, 0))
+        if h == 0:
+            V(128, cp(T.yzo[:, hs], ps[h][:, 0:Q]), pk(h, 0), [("yzo", h)])
+            DMA("Y", lambda g, hs=hs: g.sync.dma_start(T.yz[0:4, :], T.yzo[:, hs]), [("yzo", h)], [("yz", h)], "oz0", 16, 2.0)
+        else:
+            S(128, act(T.yzo[:, hs], ps[h][:, 0:Q], ACT.Copy), pk(h, 0), [("yzo", h)])
+            DMA("S", lambda g, hs=hs: g.scalar.dma_start(T.yz[4:8, :], T.yzo[:, hs]), [("yzo", h)], [("yz", h)], "oz1", 16, 2.0)
+    return ops
+
+
+def schedule(ops, tune):
+    n = len(ops)
+    deps = [set() for _ in range(n)]
+    lastw, readers = {}, {}
+    for i, o in enumerate(ops):
+        for k in o["r"]:
+            if k in lastw:
+                deps[i].add(lastw[k])
+        for k in o["w"]:
+            if k in lastw:
+                deps[i].add(lastw[k])
+            deps[i].update(readers.get(k, ()))
+        for k in o["r"]:
+            readers.setdefault(k, []).append(i)
+        for k in o["w"]:
+            lastw[k] = i
+            readers[k] = []
+        deps[i].discard(i)
+    succ = [[] for _ in range(n)]
+    for i in range(n):
+        for j in deps[i]:
+            succ[j].append(i)
+    pr = [0.0] * n
+    for i in range(n - 1, -1, -1):
+        pr[i] = min(a[1] for a in ops[i]["alts"]) + ops[i]["lat"] + HOP + max([pr[j] for j in succ[i]] + [0.0])
+    left = [len(x) for x in deps]
+    ready = [i for i in range(n) if left[i] == 0]
+    free = {e: 0.0 for e in "VSTGY"}
+    fin, eng, start = [0.0] * n, [None] * n, [0.0] * n
+    bank = [dict() for _ in range(8)]
+    opened = [None] * 8
+    order = []
+    rdy = [None] * n
+    pen = [tune.get("e" + o["tag"], 1.0) for o in ops]
+    slack = tune.get("slack", 0.1)
+    for i in range(n):
+        pr[i] += tune.get(ops[i]["tag"], 0.0)
+        if ops[i]["sem"] is not None and not deps[i]:
+            pr[i] = 1e4 - i
+    while ready:
+        cand = []
+        for i in ready:
+            o = ops[i]
+            if o["grp"] is not None and o["grp"][0] and any(opened[b] is not None for b in o["banks"]):
+                continue
+            if rdy[i] is None:
+                pe = o["alts"][0][0] == "T"
+                rdy[i] = max([fin[j] + HOP for j in deps[i] if not (pe and eng[j] == "T")] + [0.0])
+            best = None
+            for a, (e, c, f) in enumerate(o["alts"]):
+                s = max(free[e], rdy[i])
+                for b in o["banks"]:
+                    for e2, j in bank[b].items():
+                        if e2 != e and fin[j] + HOP > s:
+                            s = fin[j] + HOP
+                if best is None or s + c < best[0] + best[1] + pen[i]:
+                    best = (s, c, a, e)
+            cand.append((best[0], i, best))
+        c0 = min(cand)
+        s0, e0 = c0[0], c0[2][3]
+        near = [c for c in cand if c[2][3] == e0 and c[0] <= s0 + slack]
+        s, i, best = max(near, key=lambda c: pr[c[1]])
+        o = ops[i]
+        e = best[3]
+        eng[i], start[i] = e, s
+        o["pick"] = best[2]
+        free[e] = s + best[1]
+        fin[i] = s + best[1] + o["lat"]
+        for b in o["banks"]:
+            for e2, j in bank[b].items():
+                if e2 != e:
+                    deps[i].add(j)
+            bank[b][e] = i
+            if o["grp"] is not None:
+                opened[b] = None if o["grp"][1] else i
+        order.append(i)
+        ready.remove(i)
+        for j in succ[i]:
+            left[j] -= 1
+            if left[j] == 0:
+                ready.append(j)
+    return order, eng, deps, start, fin
+
+
+TUNE = {"eG1A0": 0, "eG1A1": 0, "eG1A2": 0, "eG1A3": 0, "rnB0": 8, "rB0": 8, "slack": 0.05,
+        "eG1B0": 2, "eG1B1": 2, "eG1B2": 2, "eG1B3": 2, "eG2A0": 9, "eG2A1": 2, "eG2A2": 2, "eG2A3": 9}
+ROUNDS = 900
+SPREAD = [(1, 1, 1, 1, HOP), (1, 1, 0.8, 1, HOP), (1, 1, 1, 1, 2 * HOP), (1, 1, 1, 0.7, HOP), (1, 1, 1, 1.3, HOP)]
+PLAN = []
+BEST = []
+
+
+def length(ops, order, eng, deps, fv, fs, ft, fg, hop):
+    fin, free = [0.0] * len(ops), {}
+    f = {"V": fv, "S": fs, "T": ft, "G": 1, "Y": 1}
+    for i in order:
+        o, e = ops[i], eng[i]
+        c = o["alts"][o["pick"]][1] * f[e] * (fg if o["name"] in ("G1", "G2") else 1)
+        s = free.get(e, 0.0)
+        for j in deps[i]:
+            if fin[j] + hop > s and not (e == "T" and eng[j] == "T"):
+                s = fin[j] + hop
+        free[e] = s + c
+        fin[i] = s + c + o["lat"]
+    return max(fin)
+
+
+def search(ops, rounds, seed=0):
+    rng = np.random.RandomState(seed)
+    tags = sorted(set(o["tag"] for o in ops if o["tag"][-2] in "ABZ"))
+    flex = sorted(set("e" + o["tag"] for o in ops if len(o["alts"]) > 1))
+
+    def score(tune):
+        order, eng, deps, start, fin = schedule(ops, tune)
+        return sum(length(ops, order, eng, deps, *p) for p in SPREAD) / len(SPREAD)
+    tune = dict(TUNE)
+    best = score(tune)
+    for _ in range(rounds):
+        t2 = dict(tune)
+        for _m in range(int(rng.choice([1, 1, 2, 3]))):
+            if rng.rand() < 0.2:
+                t2[flex[rng.randint(len(flex))]] = float(rng.choice([0, 0.3, 0.6, 1, 2, 9]))
+            else:
+                k = tags[rng.randint(len(tags))]
+                t2[k] = t2.get(k, 0.0) + float(rng.choice([-8, -4, -2, -1, -0.5, 0.5, 1, 2, 4, 8]))
+        s = score(t2)
+        if s < best + 0.03:
+            best, tune = s, t2
+    return tune
+
+
+def rank_program(g, core, T, topo):
+    rank = T.rank_of(core)
+    if rank is None:
+        return
+    nxt = T.cores[(rank + 1) % len(T.cores)]
+    prv = T.cores[(rank - 1) % len(T.cores)]
+    rid, pid, _se = topo.addr(nxt)
+    ne = min(len(topo.engines(a, b)) for a, b in zip(T.cores, list(T.cores[1:]) + [T.cores[0]]))
+    mask = sum(1 << e for e in topo.engines(core, nxt)[:ne])
+    nsent = [0]
+
+    def rem(dst, src, sem):
+        if dst is None:
+            return ne
+        def fn(g):
+            g.remote_dma(dst, src, T.sem[sem], T.sem.sent, pid, rid, mask)
+            nsent[0] += ne
+            return None
+        return fn
+
+    ops = build(T, rem)
+    if not BEST:
+        BEST.append(search(ops, ROUNDS))
+    order, eng, deps, start, fin = schedule(ops, BEST[0])
+    PLAN[:] = [ops, order, eng, start, fin]
+    qs = {"V": g.vector, "S": g.scalar, "T": g.tensor, "G": g, "Y": g.sync}
+    needed = set()
+    for i in order:
+        for j in deps[i]:
+            if ops[j]["sem"] is None and not (eng[i] == "T" and eng[j] == "T"):
+                needed.add(j)
+    count = {e: 0 for e in "VSTG"}
+    tick = {}
+    for i in order:
+        if ops[i]["sem"] is not None:
+            tick[i] = ops[i]["sem"]
+        elif i in needed:
+            count[eng[i]] += 1
+            tick[i] = ("s" + eng[i], count[eng[i]])
+    seen = {e: {} for e in qs}
+    waited = {}
+    for i in order:
+        e = eng[i]
+        want = {}
+        for j in deps[i]:
+            if e == "T" and eng[j] == "T":
+                continue
+            s, v = tick[j]
+            want[s] = max(want.get(s, 0), v)
+        for s in sorted(want):
+            if seen[e].get(s, 0) < want[s]:
+                qs[e].wait_ge(T.sem[s], want[s])
+                seen[e][s] = want[s]
+                waited[s] = max(waited.get(s, 0), want[s])
+        x = ops[i]["alts"][ops[i]["pick"]][2](g)
+        if x is not None and i in tick:
+            x.then_inc(T.sem[tick[i][0]], 16 if ops[i]["sem"] is not None else 1)
+    total = {}
+    for i in tick:
+        total[tick[i][0]] = max(total.get(tick[i][0], 0), tick[i][1])
+    total["sent"] = nsent[0]
+    for s in sorted(total):
+        if waited.get(s, 0) < total[s]:
+            g.wait_ge(T.sem[s], total[s])

@@ -7,10 +7,16 @@ NV, W, P, Q = 5, 4096, 256, 128
 OFF = 192.0 * 4096.0
 BIG16 = 1.5 * 2.0 ** 27
 BIG32 = 1.5 * 2.0 ** 28
-GCH = 4
-FZS = [1, 2]
+GCH = 2
+FZS = [0, 2]
 ZORD = [[0, 1, 2, 3], [3, 0, 1, 2], [2, 0, 3, 1], [1, 0, 2, 3], [0, 1, 2, 3]]
 UMS = [False, False]
+FPS = [False, False]
+BES = [False, False]
+BIGU = 1.5 * 2.0 ** 35
+YV = [True, True]
+REL = [False, False]
+FB = 1.5 * 2.0 ** 37
 SENDF = True
 LCH = 8
 
@@ -20,8 +26,8 @@ SCRATCH = {
     "ybuf": ("sbuf", [128, NV * P], "bfloat16"), "ynew": ("sbuf", [128, NV * P], "bfloat16"),
     "roff": ("sbuf", [128, NV * P], "uint16"), "rnew": ("sbuf", [128, NV * P], "uint16"),
     "noff": ("sbuf", [128, P], "uint16"), "soff": ("sbuf", [128, 16], "uint16"), "bcoff": ("sbuf", [128, 8], "uint16"),
-    "acc": ("sbuf", [128, 16], "float32"), "biasa": ("sbuf", [128, 8], "float32"), "toti": ("sbuf", [128, 8], "int32"),
-    "sm": ("sbuf", [128, 64], "float32"), "smi": ("sbuf", [128, 64], "int32"), "dl": ("sbuf", [128, 32], "bfloat16"),
+    "acc": ("sbuf", [128, 16], "float32"), "biasa": ("sbuf", [128, 8], "float32"),
+    "sm": ("sbuf", [128, 64], "float32"), "smi": ("sbuf", [128, 64], "int32"),
     "yzt": ("sbuf", [128, P], "float32"), "yzo": ("sbuf", [128, P], "float32"),
     "ci": ("sbuf", [128, 16], "int32"), "cf": ("sbuf", [128, 16], "float32"),
     "bo8": ("sbuf", [128, 8], "float32"), "bo512": ("sbuf", [128, 8], "bfloat16"), "wj32": ("sbuf", [128, 8], "float32"), "nwj": ("sbuf", [128, 8], "bfloat16"),
@@ -33,25 +39,32 @@ for _h in range(2):
     for _n in ("d", "ad", "far", "zg", "fz"):
         SCRATCH["%s%d" % (_n, _h)] = ("sbuf", [128, 16 * Q], "bfloat16")
     SCRATCH["dm%d" % _h] = ("sbuf", [128, 32 * Q], "bfloat16")
-    for _n in ("zb", "zl", "zi"):
+    for _n in ("zb", "zl", "zi", "zt"):
         SCRATCH["%s%d" % (_n, _h)] = ("sbuf", [128, 160], "bfloat16")
-for _n in ("sa", "fl", "sl", "cb", "m", "dr", "dr2", "rr", "dT", "tt", "s2", "sw", "gam", "bet"):
+for _n in ("sa", "fl", "sl", "cb", "m", "em", "dr", "dr2", "rr", "dT", "tt", "s2", "sw", "gam", "bet"):
     SCRATCH[_n] = ("sbuf", [128, P], "bfloat16")
 SCRATCH["fp"] = ("sbuf", [128, 2 * P], "bfloat16")
+SCRATCH["boq"] = ("sbuf", [128, 8], "bfloat16")
+SCRATCH["bon"] = ("sbuf", [128, 8], "bfloat16")
 SCRATCH["toff"] = ("sbuf", [128, 16], "uint16")
 SCRATCH["basel"] = ("sbuf", [128, 16], "float32")
 SCRATCH["cg160"] = ("sbuf", [128, 160], "float32")
 SCRATCH["pm160"] = ("sbuf", [128, 160], "float32")
 SCRATCH["rf"] = ("sbuf", [128, NV * P], "float32")
 SCRATCH["nw"] = ("sbuf", [128, NV * P], "float32")
-for _n in ("nf", "ks", "us", "us2", "y4", "g1", "t2"):
+SCRATCH["fpa"] = ("sbuf", [128, 2 * P], "bfloat16")
+for _n in ("nf", "ur", "ky", "ks", "us", "us2", "y4", "g1", "t2"):
     SCRATCH[_n] = ("sbuf", [128, P], "float32")
 for _n in ("ui", "um", "pi", "qi", "si", "fi"):
     SCRATCH[_n] = ("sbuf", [128, P], "int32")
-for _n in ("ib", "nib", "i4096", "iz", "i3", "n3i", "i17", "i32", "bo", "l1", "l2", "tri", "vc", "v2c", "cy", "kc", "mneg", "mneg2", "wh", "wl", "w16"):
+for _n in ("ib", "nib", "i4096", "iz", "ih", "nih", "cu", "n3bo", "n3i", "i17", "i32", "bo", "l1", "l2", "tri", "vc", "v2c", "cy", "kc", "mneg", "mneg2", "wh", "wl", "w16"):
     SCRATCH[_n] = ("sbuf", [128, 128], "bfloat16")
-for _n in ("pmc", "cg", "cm", "iff", "e16", "o16", "rmax", "rmin", "tmp1", "tmp2", "tmp3", "tmp4"):
+for _n in ("pmc", "cg", "cm", "iff", "e16", "o16", "rmax", "rmin", "tmp1", "tmp2", "tmp3"):
     SCRATCH[_n] = ("sbuf", [128, 128], "float32")
+for _f, _l in ((REL, ("boq", "bon")), (UMS, ("ur", "cu")), (FPS, ("ih", "nih", "fpa"))):
+    if not (_f[0] or _f[1]):
+        for _n in _l:
+            SCRATCH.pop(_n)
 for _b in range(8):
     SCRATCH["ps%d" % _b] = ("psum", [128, 512], "float32")
 
@@ -64,6 +77,7 @@ SEMAPHORES = (["sV", "sS", "sT", "sG", "sent", "ldw", "ldj", "ldy", "ldx0", "ldx
 CYC = 0.00083 * 1.25
 GC, SC = 1.55, 3.8
 PEC = 0.00042 * 1.25
+PEO = 0.005
 HOP = 0.10
 
 
@@ -101,7 +115,7 @@ def build(T, rem):
             for i, (o, l, rr, c) in enumerate(mms):
                 x = g.tensor.matmul(o, l, rr, bool(each or (first and i == 0)), bool(each or (last and i == len(mms) - 1)))
             return x
-        add([("T", 0.03 + sum(m[3] * PEC + 0.01 for m in mms), fn)], r, w, bk(w), grp=(first, last), name=name)
+        add([("T", 0.03 + sum(m[3] * PEC + PEO for m in mms), fn)], r, w, bk(w), grp=(first, last), name=name)
 
     def DMA(q, fn, r, w, sem, val, lat):
         add([(q, 0.1, fn)], r, w, sem=(sem, val), lat=lat)
@@ -147,50 +161,57 @@ def build(T, rem):
     iota(T.cg[:], [[16, 8], [0, 16]], 0, 0, "cg", 128)
     iota(T.cm[:], [[0, 8], [1, 16]], 0, 0, "cm", 128)
     iota(T.io144[:], [[1, 144]], -15, 0, "io144", 144)
-    iota(T.ci[:, 8:16], [[1, 8]], 0, 0, "ci8", 8, False)
+    iota(T.ci[:, 8:16], [[16, 8]], 15, 0, "ci8", 8, False)
     V(128, ts(T.iff[:], T.pmc[:], 0.0, None, ALU.is_equal), ["pmc"], ["iff"])
-    for nm, sc in (("i4096", 4096.0), ("ib", 1.0), ("nib", -1.0), ("iz", 3.0 / 4096), ("i3", 3.0), ("n3i", -3.0), ("i17", 2.0 ** 17), ("i32", 32.0)):
+    for nm, sc in (("i4096", 4096.0), ("ib", 1.0), ("nib", -1.0), ("iz", 3.0 / 4096), ("n3i", -3.0), ("i17", 2.0 ** 17), ("i32", 32.0)) + ((("ih", 0.5), ("nih", -0.5)) if FPS[0] or FPS[1] else ()):
         S(128, act(T[nm][:], T.iff[:], ACT.Copy, scale=sc), ["iff"], [nm])
     V(1, ts(T.ci[:, 1:2], T.ci[:, 0:1], 0x70, None, ALU.bitwise_and), ["ci0"], ["ci1"])
     V(1, ts(T.ci[:, 2:3], T.ci[:, 0:1], 15, None, ALU.bitwise_and), ["ci0"], ["ci2"])
     V(2, cp(T.cf[:, 1:3], T.ci[:, 1:3]), ["ci1", "ci2"], ["cf"])
     pg16, pm = T.cf[:, 1:2], T.cf[:, 2:3]
     V(128, ts(T.bo[:], T.cg[:], pg16, None, ALU.is_equal), ["cg", "cf"], ["bo"])
+    S(128, act(T.n3bo[:], T.bo[:], ACT.Copy, scale=-3.0), ["bo"], ["n3bo"])
     V(8, ts(T.bo8[:], T.cg[:, 0:128:16], pg16, None, ALU.is_equal), ["cg", "cf"], ["bo8"])
-    V(8, ts(T.bo512[:], T.bo8[:], 512.0, None, ALU.mult), ["bo8"], ["bo512"])
-    V(1, ts(T.cf[:, 3:4], pm, 1.0, None, ALU.add), ["cf"], ["cf3"])
-    V(8, ts(T.wj32[:], T.bo8[:], T.cf[:, 3:4], None, ALU.mult), ["bo8", "cf3"], ["wj32"])
-    V(8, ts(T.nwj[:], T.wj32[:], -1.0, None, ALU.mult), ["wj32"], ["nwj"])
+    def lin(n, o, i, sc, r, w, bias=0.0):
+        S(n, act(o, i, ACT.Identity, bias=bias, scale=sc), r, w)
+
+    lin(8, T.bo512[:], T.bo8[:], 512.0, ["bo8"], ["bo512"])
+    if REL[0] or REL[1]:
+        lin(8, T.boq[:], T.bo8[:], 0.25, ["bo8"], ["boq"])
+        lin(8, T.bon[:], T.bo8[:], -0.125, ["bo8"], ["bon"])
+    lin(1, T.cf[:, 3:4], pm, 1.0, ["cf"], ["cf3"], bias=1.0)
+    lin(8, T.wj32[:], T.bo8[:], T.cf[:, 3:4], ["bo8", "cf3"], ["wj32"])
+    lin(8, T.nwj[:], T.wj32[:], -1.0, ["wj32"], ["nwj"])
     V(144, ts(T.wsel[:], T.io144[:], pg16, None, ALU.is_equal), ["io144", "cf"], ["wsel"])
-    V(128, ts(T.tmp1[:], T.pmc[:], 0.0, 64.0, ALU.is_equal, ALU.mult), ["pmc"], ["tmp1"])
-    V(256, tt(T.l1[:], T.tmp1[:], T.bo[:], ALU.add), ["tmp1", "bo"], ["l1"])
-    V(128, ts(T.tmp1[:], T.pmc[:], 0.0, -7.0, ALU.is_equal, ALU.mult), ["pmc"], ["tmp1"])
-    V(256, tt(T.tmp2[:], T.tmp1[:], T.bo[:], ALU.add), ["tmp1", "bo"], ["tmp2"])
-    V(128, ts(T.l2[:], T.tmp2[:], 1.125, None, ALU.mult), ["tmp2"], ["l2"])
-    V(64, lambda g: g.vector.memset(T.v2c[:], -7.875), [], ["v2c"])
+    G(128, lambda g: g.affine_select(T.l1[:], T.bo[:], [[-1, 128]], ALU.not_equal, 65.0, 0, 1), ["bo"], ["l1"])
+    lin(128, T.l2[:], T.bo[:], 1.125, ["bo"], ["l2"])
+    G(128, lambda g: g.affine_select(T.l2[:], T.l2[:], [[-1, 128]], ALU.not_equal, -6.75, 0, 1), ["l2"], ["l2"])
     V(256, lambda g: g.vector.memset(T.onesb[:], 1.0), [], ["onesb"])
-    V(128, lambda g: g.vector.memset(T.o16[:], 1.0 / 16), [], ["o16"])
-    V(128, lambda g: g.vector.memset(T.yc[:], 136.0 * OFF), [], ["yc"])
-    V(64, lambda g: g.vector.memset(T.biasa[:, 0:1], 7.0), [], [("bias", 0)])
-    V(64, lambda g: g.vector.memset(T.cy[:], -OFF), [], ["cy"])
+    lin(128, T.v2c[:], T.onesb[:, 0:128], -7.875, ["onesb"], ["v2c"])
+    lin(128, T.o16[:], T.onesb[:, 0:128], 1.0 / 16, ["onesb"], ["o16"])
+    lin(256, T.yc[:], T.onesb[:, 0:P], 136.0 * OFF, ["onesb"], ["yc"])
+    lin(1, T.biasa[:, 0:1], T.onesb[:, 0:1], 7.0, ["onesb"], [("bias", 0)])
+    lin(128, T.cy[:], T.onesb[:, 0:128], -OFF, ["onesb"], ["cy"])
     G(128, lambda g: g.affine_select(T.cy[:], T.cy[:], [[0, 128]], ALU.not_equal, 2048.0, -1, 1), ["cy"], ["cy"])
     G(128, lambda g: g.affine_select(T.cy[:], T.cy[:], [[0, 128]], ALU.not_equal, -0.5, -2, 1), ["cy"], ["cy"])
+    if UMS[0] or UMS[1]:
+        V(64, lambda g: g.vector.memset(T.cu[:], -2048.0), [], ["cu"])
+        G(128, lambda g: g.affine_select(T.cu[:], T.cu[:], [[0, 128]], ALU.not_equal, 0.5, -1, 1), ["cu"], ["cu"])
     V(128, ts(T.tmp3[:], T.cm[:], 0.0, None, ALU.is_equal), ["cm"], ["tmp3"])
     V(128, ts(T.tmp1[:], T.pmc[:], 0.0, None, ALU.is_gt), ["pmc"], ["tmp1"])
     V(256, tt(T.tmp1[:], T.tmp1[:], T.tmp3[:], ALU.max), ["tmp1", "tmp3"], ["tmp1"])
     V(256, tt(T.tmp1[:], T.tmp1[:], T.bo[:], ALU.mult), ["tmp1", "bo"], ["tmp1"])
-    V(128, ts(T.tmp2[:], T.tmp3[:], 16.0, 1.0, ALU.mult, ALU.add), ["tmp3"], ["tmp2"])
-    V(256, tt(T.tmp2[:], T.tmp2[:], T.iff[:], ALU.mult), ["tmp2", "iff"], ["tmp2"])
+    lin(128, T.tmp2[:], T.tmp3[:], 16.0, ["tmp3"], ["tmp2"], bias=1.0)
+    G(128, lambda g: g.affine_select(T.tmp2[:], T.tmp2[:], [[-1, 128]], ALU.is_equal, 0.0, 0, 1), ["tmp2"], ["tmp2"])
     V(256, tt(T.tmp2[:], T.tmp2[:], T.tmp1[:], ALU.subtract), ["tmp2", "tmp1"], ["tmp2"])
-    V(128, ts(T.tri[:], T.tmp2[:], 1.0 / 64, None, ALU.mult), ["tmp2"], ["tri"])
-    V(128, ts(T.tmp1[:], T.cm[:], -1.0 / 64, -1.0, ALU.mult, ALU.add), ["cm"], ["tmp1"])
-    V(128, ts(T.tmp2[:], T.tmp3[:], 1.0 / 32, None, ALU.mult), ["tmp3"], ["tmp2"])
-    V(256, tt(T.vc[:], T.tmp1[:], T.tmp2[:], ALU.add), ["tmp1", "tmp2"], ["vc"])
-    V(128, ts(T.kc[:], T.cm[:], 32.0, None, ALU.mult), ["cm"], ["kc"])
-    V(1, ts(T.cf[:, 4:5], pm, 37.0, None, ALU.mult), ["cf"], ["cf4"])
+    lin(128, T.tri[:], T.tmp2[:], 1.0 / 64, ["tmp2"], ["tri"])
+    lin(128, T.vc[:], T.cm[:], -1.0 / 64, ["cm"], ["vc"], bias=-1.0)
+    lin(8, T.vc[:, 0:128:16], T.onesb[:, 0:8], -31.0 / 32, ["onesb", "vc"], ["vc"])
+    lin(128, T.kc[:], T.cm[:], 32.0, ["cm"], ["kc"])
+    lin(1, T.cf[:, 4:5], pm, 37.0, ["cf"], ["cf4"])
     iota(T.cg160[:], [[16, 10], [0, 16]], -16, 0, "cg160", 160)
     iota(T.pm160[:], [[1, 160]], -16, -1, "pm160", 160)
-    iota(T.e16[:], [[16, 128]], 8192, 0, "e16", 128)
+    iota(T.e16[:], [[16, 128]], 0, 0, "e16", 128)
     V(1, ts(T.ci[:, 3:4], T.ci[:, 0:1], 4, 1, ALU.logical_shift_right, ALU.bitwise_and), ["ci0"], ["ci3"])
     V(1, cp(T.cf[:, 7:8], T.ci[:, 3:4]), ["ci3"], ["cf7"])
     V(1, ts(T.cf[:, 6:7], T.cf[:, 7:8], -1.0, 1.0, ALU.mult, ALU.add), ["cf7"], ["cf6"])
@@ -200,16 +221,17 @@ def build(T, rem):
         V(160, ts(T["zb%d" % e][:], T.cg160[:], pg16, T.cf[:, 8 + e:9 + e], ALU.is_equal, ALU.mult), ["cg160", "cf", "cf8"], ["zb%d" % e])
         V(160, ts(T["zl%d" % e][:], T.cg160[:], pg16, T.cf[:, 10 + e:11 + e], ALU.is_equal, ALU.mult), ["cg160", "cf", "cf10"], ["zl%d" % e])
         V(160, ts(T["zi%d" % e][:], T.pm160[:], 0.0, T.cf[:, 6 + e:7 + e], ALU.is_equal, ALU.mult), ["pm160", "cf6", "cf7"], ["zi%d" % e])
+        S(160, act(T["zt%d" % e][:], T["zi%d" % e][:], ACT.Copy, scale=3.0), ["zi%d" % e], ["zt%d" % e])
         for c in range(4):
             S(512, act(T["dm%d" % e][:, c * 512:(c + 1) * 512], T.onesb[:], ACT.Copy, scale=OFF), ["onesb"], [("dmc", e)])
         V(1, ts(T.cf[:, 12 + e:13 + e], pm, 4.0 * (4 - FZS[e]) - 0.5, -11.5, ALU.is_gt, ALU.mult), ["cf"], [("thr", e)])
         V(1, ts(T.cf[:, 12 + e:13 + e], T.cf[:, 12 + e:13 + e], 36.5, None, ALU.add), [("thr", e)], [("thr", e)])
-    V(128, ts(T.tmp4[:], T.cm[:], pm, None, ALU.is_equal), ["cm", "cf"], ["tmp4"])
-    V(256, tt(T.tmp4[:], T.tmp4[:], T.e16[:], ALU.mult), ["tmp4", "e16"], ["tmp4"])
-    V(128, ts(T.mneg2[:], T.tmp4[:], -8192.0, None, ALU.add), ["tmp4"], ["mneg2"])
+        if BES[e]:
+            V(1, ts(T.cf[:, 14 + e:15 + e], T.cf[:, 12 + e:13 + e], -1.0, None, ALU.mult), [("thr", e)], [("nthr", e)])
     V(128, ts(T.mneg[:], T.cm[:], pm, -8192.0, ALU.not_equal, ALU.mult), ["cm", "cf"], ["mneg"])
-    V(128, ts(T.rmax[:], T.tmp3[:], -65536.0, None, ALU.mult), ["tmp3"], ["rmax"])
-    V(128, ts(T.rmin[:], T.tmp3[:], 2.0 ** 21, None, ALU.mult), ["tmp3"], ["rmin"])
+    V(256, tt(T.mneg2[:], T.mneg[:], T.e16[:], ALU.add), ["mneg", "e16"], ["mneg2"])
+    lin(128, T.rmax[:], T.tmp3[:], -65536.0, ["tmp3"], ["rmax"])
+    lin(128, T.rmin[:], T.tmp3[:], 2.0 ** 21, ["tmp3"], ["rmin"])
     V(8, cp(T.bcoff[:], T.ci[:, 8:16]), ["ci8"], ["bcoff"])
     for e in range(2):
         V(8, ts(T.basel[:, 8 * e:8 * e + 8], T.cg[:, 0:128:16], pm, 16.0, ALU.add, ALU.mult), ["cg", "cf"], ["basel"])
@@ -217,7 +239,7 @@ def build(T, rem):
         V(1, ts(T.wj[:, c:c + 1], T.wi[:, 0:1], mk, None, ALU.bitwise_and), ["wi"], [("wj", c)])
     V(3, cp(T.wf[:, 1:4], T.wj[:, 1:4]), [("wj", 1), ("wj", 2), ("wj", 3)], ["wf"])
     for c, nm in ((1, "wh"), (2, "wl"), (3, "w16")):
-        V(64, ts(T[nm][:], T.bo[:], T.wf[:, c:c + 1], None, ALU.mult), ["bo", "wf"], [nm])
+        lin(128, T[nm][:], T.bo[:], T.wf[:, c:c + 1], ["bo", "wf"], [nm])
     V(256, cp(T.roff[:, 0:P], T.jin[:]), ["jin"], [("r", 0, 0), ("r", 0, 1)])
 
     for c in range(8):
@@ -277,13 +299,22 @@ def build(T, rem):
             for q in range(4):
                 qs = slice(q * 512, (q + 1) * 512)
                 V(512, tt(d[:, q:16 * Q:4], pg[:, q:16 * Q:4], B[:, 0:512], ALU.subtract), PG + pk(h, 0, 4), [("d", h, q)], name="SUB")
-                S(512, act(ad[:, qs], d[:, q:16 * Q:4], ACT.Abs, bias=-192.0, scale=1.0 / 4096), [("d", h, q)], [("ad", h, q)], name="ABS")
-                V(256, ts(far[:, qs], ad[:, qs], 2.5, None, ALU.is_gt), [("ad", h, q)], [("far", h, q)], name="FAR")
-            col = lambda buf, k: buf[:, (k % 4) * 512 + k // 4:(k % 4 + 1) * 512:4]
+            DD = [("d", h, q) for q in range(4)]
             sel = lambda k: T.wsel[:, 15 - k:143 - k]
-            for q in range(4):
-                MM([(r4(4, h), sel(k), col(far, k), 128) for k in range(q, 16, 4)], ["wsel", ("far", h, q)], pk(4, h), first=q == 0, last=q == 3, name="CNT")
-                MM([(r4(5, h), T.ib[:], col(far, k), 128) for k in range(q, 16, 4)], ["ib", ("far", h, q)], pk(5, h), first=q == 0, last=q == 3, name="BB")
+            for c in range(2):
+                cs = slice(c * 1024, (c + 1) * 1024)
+                V(512, ts(far[:, cs], d[:, cs], FB - OFF, FB, ALU.add, ALU.not_equal), DD, [("far", h, c)], name="FAR")
+                if REL[h]:
+                    V(512, ts(ad[:, cs], d[:, cs], OFF, 0.0, ALU.subtract, ALU.max), DD, [("ad", h, 2 * c), ("ad", h, 2 * c + 1)], name="REL")
+                else:
+                    S(1024, act(ad[:, cs], d[:, cs], ACT.Abs, bias=-192.0, scale=1.0 / 4096), DD, [("ad", h, 2 * c), ("ad", h, 2 * c + 1)], name="ABS")
+            for c in range(2):
+                for q in range(2):
+                    MM([(ps[4][:, h * Q + 64 * c:h * Q + 64 * c + 64], sel(k), far[:, c * 1024 + k:(c + 1) * 1024:16], 64) for k in range(8 * q, 8 * q + 8)],
+                       ["wsel", ("far", h, c)], pk(4, h), first=q == 0, last=q == 1, name="CNT")
+                for q in range(2):
+                    MM([(ps[5][:, h * Q + 64 * c:h * Q + 64 * c + 64], T.ib[:], far[:, c * 1024 + k:(c + 1) * 1024:16], 64) for k in range(8 * q, 8 * q + 8)],
+                       ["ib", ("far", h, c)], pk(5, h), first=q == 0, last=q == 1, name="BB")
             S(128, act(T.sa[:, hs], r4(4, h), ACT.Sign, bias=4.5, scale=-1.0), pk(4, h), [K("sa")])
             VS(128, cp(T.cb[:, hs], r4(4, h)), act(T.cb[:, hs], r4(4, h), ACT.Copy), pk(4, h), [K("cb")])
             S(128, act(T.fl[:, hs], r4(5, h), ACT.Sign, bias=-8.5), pk(5, h), [K("fl")])
@@ -291,9 +322,21 @@ def build(T, rem):
             MM([(r4(h, 1), T.vc[0:1, :], T.onesb[0:1, 0:Q], 128), (r4(h, 1), T.tri[:], T.fl[:, hs], 128)], ["vc", "onesb", "tri", K("fl")], pk(h, 1))
             S(128, act(T.sl[:, hs], r4(h, 0), ACT.Sign, bias=T.biasa[:, t:t + 1], acc=T.acc[:, 2 * t + h:2 * t + h + 1]), pk(h, 0) + [("bias", t)], [K("sl"), ("acc", t, h)])
             V(128, tt(T.m[:, hs], r4(h, 1), T.sl[:, hs], ALU.is_gt), pk(h, 1) + [K("sl")], [K("m")], name="m")
+            kcol = lambda k: ps[4][:, (2 + h) * Q + k:(3 + h) * Q:16]
             MM([(r4(4, 2 + h), T.onesb[0:1, 0:Q], T.kc[0:1, :], 128), (r4(4, 2 + h), T.sa[:, hs], T.i17[:], 128)]
-               + [(ps[4][:, (2 + h) * Q + k:(3 + h) * Q:16], col(ad, k), T.bo512[:], 64) for k in range(16)],
-               ["onesb", "kc", "i17", "bo512", K("sa"), K("m")] + [("ad", h, q) for q in range(4)], pk(4, 2 + h), last=False, name="KEY")
+               + [(kcol(k), ad[:, k:16 * Q:16], (T.boq if REL[h] else T.bo512)[:], 64) for k in range(8)],
+               ["onesb", "kc", "i17", "bo512", "boq", K("sa")] + [("ad", h, q) for q in range(4)], pk(4, 2 + h), last=False, name="KEY")
+            MM([(kcol(k), ad[:, k:16 * Q:16], (T.boq if REL[h] else T.bo512)[:], 64) for k in range(8, 16)],
+               ["bo512", "boq"] + [("ad", h, q) for q in range(4)], pk(4, 2 + h), first=False, last=not REL[h], name="KEY")
+            if REL[h]:
+                for q in range(2):
+                    MM([(kcol(k), d[:, k:16 * Q:16], T.bon[:], 64) for k in range(8 * q, 8 * q + 8)], ["bon"] + DD, pk(4, 2 + h), first=False, last=q == 1, name="KEY")
+            VS(128, cp(T.ky[:, hs], r4(4, 2 + h)), act(T.ky[:, hs], r4(4, 2 + h), ACT.Copy), pk(4, 2 + h), [K("ky")], name="ky")
+            V(128, lambda g, hs=hs: g.vector.tensor_tensor_scan(T.ks[:, hs], T.rmin[:], T.ky[:, hs], 0.0, ALU.add, ALU.min), ["rmin", K("ky")], [K("ks")])
+            V(128 * GC, lambda g, hs=hs: g.vector.tensor_tensor(T.dT[:, hs], T.ks[:, hs].indirect(T.bcoff[:, 0:8]), T.ky[:, hs], ALU.is_equal),
+              [K("ks"), K("ky"), "bcoff"], [K("dT")], name="eq")
+            MM([(r4(4, 2 + h), T.dT[:, hs], T.ib[:], 128)], [K("dT"), "ib"], pk(4, 2 + h), name="EM")
+            VS(128, cp(T.em[:, hs], r4(4, 2 + h)), act(T.em[:, hs], r4(4, 2 + h), ACT.Copy), pk(4, 2 + h), [K("em")], name="em")
             for c in range(2):
                 V(512, (lambda g, c=c, d=d, dm=dm: g.vector.transpose(dm[:, 2048 + c * 1024:3072 + c * 1024], d[:, c * 1024:(c + 1) * 1024])),
                   [("d", h, q) for q in range(4)], [("dm", h, c)], name="TR")
@@ -313,42 +356,53 @@ def build(T, rem):
             for j0 in range(2):
                 MM([(B[:, 3 * Q + j0:4 * Q:2], T["zi%d" % j0][:, 16 * (1 - (g0 - j0)):16 * (1 - (g0 - j0)) + 128], T.dr2[:, h * Q + g0:(h + 1) * Q:2], 64) for g0 in range(2)],
                    ["zi0", "zi1", K("dr2")], pk(h, 3), name="DR")
-            VS(128, cp(T.dr[:, hs], r4(h, 3)), act(T.dr[:, hs], r4(h, 3), ACT.Copy), pk(h, 3), [K("dr")], name="dr")
-            MM([(r4(4, 2 + h), T.dr[:, hs], T.ib[:], 128)], [K("dr"), "ib"], pk(4, 2 + h), first=False, name="KEY2")
-            V(128, lambda g, h=h, hs=hs: g.vector.tensor_tensor_scan(T.ks[:, hs], T.rmin[:], ps[4][:, (2 + h) * Q:(3 + h) * Q], 0.0, ALU.add, ALU.min),
-              ["rmin"] + pk(4, 2 + h), [K("ks")])
-            kl = T.ks[:, h * Q + 15:(h + 1) * Q:16]
-            V(8, ts(T.sm[:, 8 * h:8 * h + 8], kl, BIG32, BIG32, ALU.add, ALU.subtract), [K("ks")], [K("hi")])
-            V(16, tt(T.dl[:, 16 * h:16 * h + 8], kl, T.sm[:, 8 * h:8 * h + 8], ALU.subtract), [K("ks"), K("hi")], [K("dl")])
-            VS(128 * GC, (lambda g, h=h, hs=hs: g.vector.tensor_copy(T.dT[:, hs], T.dl[:, 16 * h:16 * h + 8].indirect(T.bcoff[:, 0:8]))),
-               (lambda g, h=h, hs=hs: g.scalar.activation(T.dT[:, hs], T.dl[:, 16 * h:16 * h + 8].indirect(T.bcoff[:, 0:8]), ACT.Copy)),
-               [K("dl"), "bcoff"], [K("dT")])
-            MM([(r4(h, 0), T.dT[:, hs], T.ib[:], 128)], [K("dT"), "ib"], pk(h, 0))
-            MM([(r4(h, 2), T.i3[:], T.dr[:, hs], 128)], [K("dr"), "i3"], pk(h, 2))
-            MM([(r4(h, 1), T.i3[:], T.dr[:, hs], 128), (r4(h, 1), T.dT[:, hs], T.n3i[:], 128)], [K("dr"), K("dT"), "i3", "n3i"], pk(h, 1))
+            V(128, tt(T.dr[:, hs], r4(h, 3), T.em[:, hs], ALU.mult), pk(h, 3) + [K("em")], [K("dr")], name="de")
+            MM([(r4(h, 0), T.bo[:], T.dr[:, hs], 128)], [K("dr"), "bo"], pk(h, 0), name="DEL")
+            back = lambda reg, j0: [(B[:, reg * Q + j0:(reg + 1) * Q:2], T["zt%d" % j0][:, 16 * (1 - (g0 - j0)):16 * (1 - (g0 - j0)) + 128],
+                                     T.dr2[:, h * Q + g0:(h + 1) * Q:2], 64) for g0 in range(2)]
+            for j0 in range(2):
+                MM(back(2, j0), ["zt0", "zt1", K("dr2")], pk(h, 2), name="DR3")
+            for j0 in range(2):
+                MM(back(1, j0) + [(B[:, Q + j0:2 * Q:2], T.n3bo[:], T.dr[:, h * Q + j0:(h + 1) * Q:2], 64)], ["zt0", "zt1", "n3bo", K("dr2"), K("dr")], pk(h, 1), name="DD3")
             V(128, tt(T.tt[:, hs], r4(h, 0), T.m[:, hs], ALU.mult), pk(h, 0) + [K("m")], [K("tt")])
-            V(256, ts(T.fp[:, 2 * h * Q:2 * (h + 1) * Q], B[:, Q:3 * Q], BIG16, BIG16, ALU.add, ALU.not_equal), pk(h, 1, 2), [K("fp")])
-            MM([(r4(h, 3), T.ib[:], y, 128), (r4(h, 3), T.ib[:], T.tt[:, hs], 128)], ["ib", yk, K("tt")], pk(h, 3))
+            fps = slice(2 * h * Q, 2 * (h + 1) * Q)
+            if FPS[h]:
+                S(256, act(T.fpa[:, fps], B[:, Q:3 * Q], ACT.Abs), pk(h, 1, 2), [K("fpa")])
+                S(256, act(T.fp[:, fps], T.fpa[:, fps], ACT.Sign, bias=-7.5), [K("fpa")], [K("fp")])
+            else:
+                V(256, ts(T.fp[:, fps], B[:, Q:3 * Q], BIG16, BIG16, ALU.add, ALU.not_equal), pk(h, 1, 2), [K("fp")])
+            pos, neg = (T.ih, T.nih) if FPS[h] else (T.ib, T.nib)
             yn = T.ynew[:, ts_]
             ynk = ("yn", t, h)
-            VS(128, cp(yn, r4(h, 3)), act(yn, r4(h, 3), ACT.Copy), pk(h, 3), [ynk], name="ynew")
+            if YV[h]:
+                V(256, tt(yn, y, T.tt[:, hs], ALU.add), [yk, K("tt")], [ynk], name="ynew")
+            else:
+                MM([(r4(h, 3), T.ib[:], y, 128), (r4(h, 3), T.ib[:], T.tt[:, hs], 128)], ["ib", yk, K("tt")], pk(h, 3), name="YN")
+                VS(128, cp(yn, r4(h, 3)), act(yn, r4(h, 3), ACT.Copy), pk(h, 3), [ynk], name="ynew")
             S(128, act(T.y4[:, hs], yn, ACT.Copy, scale=4096.0), [ynk], [K("y4")])
             if t < NV - 1:
                 DMA("G", rem(T.ybuf[:, o + P:o + P + Q], yn, "ay%d%d" % (t + 1, h)), [ynk], [("y", t + 1, h)], "ay%d%d" % (t + 1, h), rem(None, None, None), 3.0)
             else:
                 DMA("Y", lambda g, yn=yn, hs=hs: g.sync.dma_start(T.yo[:, hs], yn), [ynk], [K("yo")], "oy%d" % h, 16, 2.0)
-            MM([(r4(h, 0), T.ib[:], T.cb[:, hs], 128), (r4(h, 0), T.ib[:], T.fp[:, 2 * h * Q:(2 * h + 1) * Q], 128), (r4(h, 0), T.nib[:], T.fp[:, (2 * h + 1) * Q:(2 * h + 2) * Q], 128)],
-               ["ib", "nib", K("cb"), K("fp")], pk(h, 0))
+            MM([(r4(h, 0), T.ib[:], T.cb[:, hs], 128), (r4(h, 0), pos[:], T.fp[:, 2 * h * Q:(2 * h + 1) * Q], 128), (r4(h, 0), neg[:], T.fp[:, (2 * h + 1) * Q:(2 * h + 2) * Q], 128)],
+               ["ib", "nib", "ih", "nih", K("cb"), K("fp")], pk(h, 0))
             S(128, act(T.s2[:, hs], r4(h, 0), ACT.Sign, bias=4.5, scale=-1.0), pk(h, 0), [K("s2")])
             MM([(r4(h, 1), T.l1[:], T.s2[:, hs], 128)], ["l1", K("s2")], pk(h, 1))
             MM([(r4(h, 2), T.v2c[0:1, :], T.onesb[0:1, 0:Q], 128), (r4(h, 2), T.l2[:], T.s2[:, hs], 128)], ["v2c", "onesb", "l2", K("s2")], pk(h, 2))
-            MM([(r4(h, 3), T.wh[:], yn, 128), (r4(h, 3), T.wl[:], yn, 128)], ["wh", "wl", ynk], pk(h, 3), last=not UMS[h], name="U")
+            MM(([(r4(h, 3), T.cu[0:2, :], T.onesb[0:2, 0:Q], 128)] if UMS[h] else []) + [(r4(h, 3), T.wh[:], yn, 128), (r4(h, 3), T.wl[:], yn, 128)],
+               ["wh", "wl", "cu", "onesb", ynk], pk(h, 3), name="U")
             MM([(r4(4, 2 + h), T.w16[:], yn, 128), (r4(4, 2 + h), T.ib[:], T.mneg[:], 128)], ["w16", "ib", "mneg", ynk], pk(4, 2 + h), name="U2")
             S(128, act(T.sw[:, hs], r4(h, 1), ACT.Sign, bias=-71.0), pk(h, 1), [K("sw")])
             V(128, ts(T.gam[:, hs], r4(h, 2), BIG16, BIG16, ALU.add, ALU.is_equal), pk(h, 2), [K("gam")])
-            V(128, cp(T.ui[:, hs], r4(h, 3)), pk(h, 3), [K("ui")])
-            V(128, ts(T.um[:, hs], T.ui[:, hs], W - 1, None, ALU.bitwise_and), [K("ui")], [K("um")])
-            V(128, tt(T.pi[:, hs], T.um[:, hs], RP, ALU.mult), [K("um")] + pk(pb, 0), [K("pi")])
+            if UMS[h]:
+                S(128, act(T.ur[:, hs], r4(h, 3), ACT.Identity, bias=BIGU), pk(h, 3), [K("ui")])
+                S(128, act(T.rr[:, hs], T.ur[:, hs], ACT.Identity, bias=-BIGU), [K("ui")], [K("rr")], name="um")
+                MM([(r4(h, 3), T.wh[:], yn, 128), (r4(h, 3), T.wl[:], yn, 128), (r4(h, 3), T.nib[:], T.rr[:, hs], 128)], ["wh", "wl", "nib", ynk, K("rr")], pk(h, 3), name="UU")
+                V(128, tt(T.pi[:, hs], rf, r4(h, 3), ALU.mult), [rfk] + pk(h, 3), [K("pi")])
+            else:
+                V(128, cp(T.ui[:, hs], r4(h, 3)), pk(h, 3), [K("ui")])
+                V(128, ts(T.um[:, hs], T.ui[:, hs], W - 1, None, ALU.bitwise_and), [K("ui")], [K("um")])
+                V(128, tt(T.pi[:, hs], T.um[:, hs], RP, ALU.mult), [K("um")] + pk(pb, 0), [K("pi")])
             V(128, ts(T.qi[:, hs], T.pi[:, hs], 5, None, ALU.logical_shift_right), [K("pi")], [K("qi")])
             V(128, tt(T.si[:, hs], T.qi[:, hs], R37, ALU.add), [K("qi")] + pk(pb, 1), [K("si")])
             V(128, ts(T.fi[:, hs], T.si[:, hs], W - 1, None, ALU.bitwise_and), [K("si")], [K("fi")])
@@ -377,7 +431,7 @@ def build(T, rem):
                     for i, (o_, l_, r_, c_) in enumerate(mms):
                         x = g.tensor.matmul(o_, l_, r_, i % 2 == 0, i % 2 == 1)
                     return x
-                add([("T", 0.03 + 8 * (128 * PEC + 0.01), zfn)], ZG + ["iz", "n3i", ynk], pk(b, 0, 4), [b], grp=(True, True), name="ZD")
+                add([("T", 0.03 + 8 * (128 * PEC + PEO), zfn)], ZG + ["iz", "n3i", ynk], pk(b, 0, 4), [b], grp=(True, True), name="ZD")
                 if q < 4 - FZS[h]:
                     V(512, ts(fz[:, qs], ps[b][:, 0:512], BIG16 - 576.0, BIG16, ALU.add, ALU.not_equal), pk(b, 0, 4), [("fz", h, q)], name="FZ")
                 else:
@@ -390,7 +444,11 @@ def build(T, rem):
                 if i == 3:
                     mm = [(r4(5, 2 + h), T.i32[:], T.sw[:, hs], 128)] + mm
                 MM(mm, ["wsel", "i32", ("fz", h, q)] + ([K("sw")] if i == 3 else []), pk(5, 2 + h), first=i == 0, last=i == 3, name="CNT2")
-            V(128, ts(T.bet[:, hs], r4(5, 2 + h), T.cf[:, 12 + h:13 + h], None, ALU.is_gt), pk(5, 2 + h) + [K("thr")], [K("bet")])
+            if BES[h]:
+                S(128, act(T.sw[:, hs], r4(5, 2 + h), ACT.Sign, bias=T.cf[:, 14 + h:15 + h]), pk(5, 2 + h) + [K("nthr")], [K("sw")], name="bs")
+                S(128, act(T.bet[:, hs], T.sw[:, hs], ACT.Relu), [K("sw")], [K("bet")])
+            else:
+                V(128, ts(T.bet[:, hs], r4(5, 2 + h), T.cf[:, 12 + h:13 + h], None, ALU.is_gt), pk(5, 2 + h) + [K("thr")], [K("bet")])
             V(128, tt(T.t2[:, hs], T.bet[:, hs], R37, ALU.mult), [K("bet")] + pk(pb, 1), [K("t2")])
             nw, nwk = T.nw[:, ts_], ("nw", t, h)
             V(128, tt(nw, T.t2[:, hs], RP, ALU.add), [K("t2")] + pk(pb, 0), [nwk], name="new")
@@ -409,9 +467,9 @@ def build(T, rem):
         if t < NV - 1:
             MM([(ps[5][:, Q:Q + 1], T.o16[:], T.acc[:, 2 * t:2 * t + 1], 256), (ps[5][:, Q:Q + 1], T.o16[:], T.acc[:, 2 * t + 1:2 * t + 2], 256)],
                ["o16", ("acc", t, 0), ("acc", t, 1)], pk(5, 1))
-            V(1, cp(T.toti[:, 0:1], ps[5][:, Q:Q + 1]), pk(5, 1), ["tot1"])
-            V(1, ts(T.toti[:, 1:2], T.toti[:, 0:1], 2, None, ALU.bitwise_and), ["tot1"], ["tot2"])
-            V(1, ts(T.biasa[:, t + 1:t + 2], T.toti[:, 1:2], -1.0, 7.0, ALU.mult, ALU.add), ["tot2"], [("bias", t + 1)])
+            V(1, cp(T.smi[:, 40:41], ps[5][:, Q:Q + 1]), pk(5, 1), ["tot1"])
+            V(1, ts(T.smi[:, 41:42], T.smi[:, 40:41], 2, None, ALU.bitwise_and), ["tot1"], ["tot2"])
+            V(1, ts(T.biasa[:, t + 1:t + 2], T.smi[:, 41:42], -1.0, 7.0, ALU.mult, ALU.add), ["tot2"], [("bias", t + 1)])
 
     ctx["h"] = "Z"
     for c in range(8):
@@ -521,9 +579,8 @@ def schedule(ops, tune):
     return order, eng, deps, start, fin
 
 
-TUNE = {"eG1A0": 0, "eG1A1": 0, "eG1A2": 0, "eG1A3": 0, "rnB0": 8, "rB0": 8, "slack": 0.05,
-        "eG1B0": 2, "eG1B1": 2, "eG1B2": 2, "eG1B3": 2, "eG2A0": 9, "eG2A1": 2, "eG2A2": 2, "eG2A3": 9}
-ROUNDS = 900
+TUNE = {'eG1A0':1,'eG1A1':1,'eG1A2':0,'eG1A3':0,'rnB0':4.5,'rB0':15.5,'slack':0.05,'eG1B0':2,'eG1B1':2,'eG1B2':0.6,'eG1B3':0.6,'eG2A0':0.3,'eG2A1':0.3,'eG2A2':2,'eG2A3':2,'eG2B0':0,'eG2B1':2,'eG2B2':2,'eG2B3':2,'TRB0':4,'SUBA1':-35.5,'eemA0':2,'U2B0':4.5,'ynewA0':-24.5,'DD3A1':10.5,'edr2A0':0,'G1A1':-22,'ttA0':13,'cbB0':3,'ekyB0':9,'YZZ5':-0.5,'NTB0':-15.5,'us2A0':13,'UA0':33,'umA0':-15,'eXRZ7':0,'EB0':6.5,'flA0':6,'yjA0':3,'rrB0':14,'ZDB3':-10.5,'deB0':2,'edr2B0':0,'eemB0':2,'eXRZ0':9,'CNTA1':0.5,'eXRZ5':0.3,'FZB1':11,'BBA2':10.5,'mB0':19,'SUBA3':15.5,'R37A0':-26.5,'yzoZ1':-26,'CNT2B3':-25.5,'eXRZ1':2,'yzZ1':-20.5,'DD3A0':-1.5,'ecbA0':9,'nfA0':-3,'rfB1':-4.5,'YZZ1':6,'rnA0':-2.5,'XRZ3':-14.5,'NMRA0':3,'SUBB0':8,'yztZ0':12,'g1B0':6,'piA0':-2.5,'YZZ4':-7,'rrA0':-1,'toffA0':11,'NTA1':-2,'gamA0':8,'SUBA0':-9,'yoB0':5.5,'FZA0':-15,'eqA0':11.5,'biasB0':-22,'FARB0':13.5,'rfA1':-19.5,'CNT2A2':16,'yA0':-16.5,'YZZ7':-19,'RHOA0':10,'FZA3':-0.5,'slB0':-14,'CNTA2':-0.5,'TRA1':8.5,'y4B0':3.5,'DELB0':1.5,'ksA0':26,'G1A0':14,'SCAT0B0':-10.5,'saB0':39.5,'eXRZ4':0,'FZbB1':-1.5,'YZZ2':-22.5,'TRA0':6.5,'psB5':-6.5,'qiB0':9.5,'SUBB1':13,'saA0':9.5,'FZA1':7.5,'swA0':16.5,'EMA0':13.5,'DRA1':4.5,'eXRZ6':1,'CNTA3':12.5,'siA0':24,'t2B0':-15.5,'newB0':2.5,'deA0':13,'ABSB0':-3,'ybcB0':-1.5,'kyB0':1.5,'XRZ6':-4,'betA0':22.5,'U2A0':-2,'eXRZ3':9,'kyA0':1.5,'TRB1':-0.5,'siB0':-32,'fpB0':36.5,'eqB0':10.5,'CNT2B2':2.5,'ksB0':8.5,'SCAT1B0':-3,'tot1B0':-11,'G2A1':-1.5,'G2A0':13,'FZaB0':1.5,'ekyA0':2,'ABSB1':17,'FZB0':32.5,'R37B0':-9,'G1B0':2,'sl1B0':1,'NTA2':15,'flB0':-24.5,'eXRZ2':0,'rscanA0':6.5,'EA0':-14,'SUBA2':2.5,'ybcA0':-30.5,'FZbB0':11.5,'ynewB0':1.5,'y4A0':1.5,'noffA0':2,'G2B1':4.5,'mA0':11,'soffB0':13.5,'ecbB0':9,'yzZ0':-1,'tot2B0':-12.5,'yjB0':8.5,'FZaB1':-20,'EMB0':3.5,'sl3B0':1.5,'fiB0':3,'CNT2B1':-1,'FARA0':8.5,'yB0':13,'psZ1':-23.5,'rscanB0':-6.5,'nfB0':-14,'fiA0':-3.5,'dr2B0':-6.5,'piB0':2.5,'rfA0':3,'yoA0':14,'psB4':-6,'NTA0':-22,'noffB0':13.5,'SUBB3':11,'BASEA0':-2,'umB0':13,'ZDA2':2,'YZZ0':-2,'newA0':2,'uiA0':-43,'psZ0':-13.5,'RPA0':-12,'gamB0':-0.5,'g1A0':-13,'DR3B1':24,'swB0':4.5,'CNTB0':3.5,'XRZ7':-11.5,'CNT2A1':9.5,'t2A0':17.5,'SUBB2':21,'DD3B0':0.5,'NTB2':0.5,'BBA3':-4,'BBA0':19.5,'yzoZ0':9.5,'sl2B0':14,'XRZ2':2,'psB0':16.5,'cbA0':2,'XRZ0':-0.5,'BASEB0':-13.5,'emB0':-17.5,'qiA0':7,'psA0':5,'YZZ3':-7,'G2B0':6.5,'s2A0':-6.5,'NTA3':1.5,'uiB0':-3,'us2B0':6.5,'rfB0':-6,'RPB0':-1.5,'BBB2':3.5,'XRZ5':-17.5,'FARA1':7,'CNTB1':9,'NMRB0':1,'toffB0':-10,'KEYB1':-0.5,'XRZ4':-1,'G1B1':10,'fpA0':17.5,'BBA1':6.5,'ZDB2':-0.5,'psB3':9,'s2B0':1.5,'ABSA1':-1,'DR3A1':2,'psA2':-1.5,'rA0':6,'DRB1':15.5,'dr2A0':-1,'FARB1':8,'NCB0':-0.5,'DELA0':5.5,'emA0':3,'DD3B1':2,'ttB0':-2.5,'KEYB0':2,'NTB3':-0.5,'KEYA0':5,'DR3B0':0.5,'CNT2B0':-4.5,'ZDB1':1.5,'psA1':7.5,'KEYA1':8,'RHOB0':30.5,'CNT2A3':-0.5,'betB0':10,'psB2':-1,'psA4':-0.5,'BBB0':8,'UB0':0.5}
+ROUNDS = 0
 SPREAD = [(1, 1, 1, 1, HOP), (1, 1, 0.8, 1, HOP), (1, 1, 1, 1, 2 * HOP), (1, 1, 1, 0.7, HOP), (1, 1, 1, 1.3, HOP)]
 PLAN = []
 BEST = []

@@ -6,65 +6,47 @@ ACT = ActivationFunctionType
 NV, W, P, Q = 5, 4096, 256, 128
 OFF = 192.0 * 4096.0
 BIG16 = 1.5 * 2.0 ** 27
-BIG32 = 1.5 * 2.0 ** 28
-GCH = 2
-FZS = [0, 2]
-ZORD = [[0, 1, 2, 3], [3, 0, 1, 2], [2, 0, 3, 1], [1, 0, 2, 3], [0, 1, 2, 3]]
-UMS = [False, False]
-FPS = [False, False]
-BES = [False, False]
 BIGU = 1.5 * 2.0 ** 35
-YV = [True, True]
-REL = [False, False]
 FB = 1.5 * 2.0 ** 37
-SENDF = True
 LCH = 8
+OPT = {"g1": [4, 4], "g2": [4, 4], "fzs": [[], [0, 1]], "nch": [2, 2], "sp": [True, True], "c2t": [True, True], "rsc": [True, True], "uy": True, "usc": True}
 
 SCRATCH = {
     "tab": ("sbuf", [128, W], "float32"), "lst": ("sbuf", [128, W], "int32"), "xb": ("sbuf", [128, W], "bfloat16"),
-    "jin": ("sbuf", [128, P], "int32"), "wi": ("sbuf", [128, 8], "int32"), "wj": ("sbuf", [128, 8], "int32"), "wf": ("sbuf", [128, 8], "float32"),
+    "jin": ("sbuf", [128, P], "int32"), "wi": ("sbuf", [128, 8], "int32"), "wj": ("sbuf", [128, 8], "int32"), "wf": ("sbuf", [128, 16], "float32"),
     "ybuf": ("sbuf", [128, NV * P], "bfloat16"), "ynew": ("sbuf", [128, NV * P], "bfloat16"),
     "roff": ("sbuf", [128, NV * P], "uint16"), "rnew": ("sbuf", [128, NV * P], "uint16"),
-    "noff": ("sbuf", [128, P], "uint16"), "soff": ("sbuf", [128, 16], "uint16"), "bcoff": ("sbuf", [128, 8], "uint16"),
-    "acc": ("sbuf", [128, 16], "float32"), "biasa": ("sbuf", [128, 8], "float32"),
-    "sm": ("sbuf", [128, 64], "float32"), "smi": ("sbuf", [128, 64], "int32"),
+    "rf": ("sbuf", [128, NV * P], "float32"), "nw": ("sbuf", [128, NV * P], "float32"),
+    "noff": ("sbuf", [128, P], "uint16"), "soff": ("sbuf", [128, 16], "uint16"), "bcoff": ("sbuf", [128, 8], "uint16"), "toff": ("sbuf", [128, 16], "uint16"),
+    "acc": ("sbuf", [128, 16], "float32"), "biasa": ("sbuf", [128, 8], "float32"), "basel": ("sbuf", [128, 16], "float32"),
+    "km": ("sbuf", [128, 16], "float32"), "sm": ("sbuf", [128, 64], "float32"), "smi": ("sbuf", [128, 64], "int32"),
     "yzt": ("sbuf", [128, P], "float32"), "yzo": ("sbuf", [128, P], "float32"),
-    "ci": ("sbuf", [128, 16], "int32"), "cf": ("sbuf", [128, 16], "float32"),
-    "bo8": ("sbuf", [128, 8], "float32"), "bo512": ("sbuf", [128, 8], "bfloat16"), "wj32": ("sbuf", [128, 8], "float32"), "nwj": ("sbuf", [128, 8], "bfloat16"),
-    "wsel": ("sbuf", [128, 144], "bfloat16"), "io144": ("sbuf", [128, 144], "float32"),
-    "onesb": ("sbuf", [128, 512], "bfloat16"), "yc": ("sbuf", [128, P], "bfloat16"),
+    "ci": ("sbuf", [128, 16], "int32"), "cf": ("sbuf", [128, 24], "float32"),
+    "bo8": ("sbuf", [128, 8], "bfloat16"), "wj32": ("sbuf", [128, 8], "float32"), "nwj": ("sbuf", [128, 8], "bfloat16"), "crow": ("sbuf", [128, 8], "bfloat16"),
+    "wsel": ("sbuf", [128, 144], "bfloat16"), "onesb": ("sbuf", [128, 512], "bfloat16"), "yc": ("sbuf", [128, P], "bfloat16"),
+    "fp": ("sbuf", [128, 2 * P], "bfloat16"), "cbs": ("sbuf", [128, 16 * Q], "bfloat16"),
 }
 for _h in range(2):
     SCRATCH["pg%d" % _h] = ("sbuf", [128, 16 * Q], "float32")
     for _n in ("d", "ad", "far", "zg", "fz"):
         SCRATCH["%s%d" % (_n, _h)] = ("sbuf", [128, 16 * Q], "bfloat16")
     SCRATCH["dm%d" % _h] = ("sbuf", [128, 32 * Q], "bfloat16")
-    for _n in ("zb", "zl", "zi", "zt"):
+    for _n in ("zi", "zd", "zt", "zq"):
         SCRATCH["%s%d" % (_n, _h)] = ("sbuf", [128, 160], "bfloat16")
-for _n in ("sa", "fl", "sl", "cb", "m", "em", "dr", "dr2", "rr", "dT", "tt", "s2", "sw", "gam", "bet"):
+for _n in ("cb", "m", "em", "dr", "dr2", "rr", "dT", "tt", "s2", "gam", "bet", "ur", "dsg", "fl"):
     SCRATCH[_n] = ("sbuf", [128, P], "bfloat16")
-SCRATCH["fp"] = ("sbuf", [128, 2 * P], "bfloat16")
-SCRATCH["boq"] = ("sbuf", [128, 8], "bfloat16")
-SCRATCH["bon"] = ("sbuf", [128, 8], "bfloat16")
-SCRATCH["toff"] = ("sbuf", [128, 16], "uint16")
-SCRATCH["basel"] = ("sbuf", [128, 16], "float32")
-SCRATCH["cg160"] = ("sbuf", [128, 160], "float32")
-SCRATCH["pm160"] = ("sbuf", [128, 160], "float32")
-SCRATCH["rf"] = ("sbuf", [128, NV * P], "float32")
-SCRATCH["nw"] = ("sbuf", [128, NV * P], "float32")
-SCRATCH["fpa"] = ("sbuf", [128, 2 * P], "bfloat16")
-for _n in ("nf", "ur", "ky", "ks", "us", "us2", "y4", "g1", "t2"):
+for _n in ("io160", "pm160", "cg160"):
+    SCRATCH[_n] = ("sbuf", [128, 160], "float32")
+SCRATCH["zr"] = ("sbuf", [128, 160], "bfloat16")
+SCRATCH["zw"] = ("sbuf", [128, 144], "bfloat16")
+for _n in ("nf", "ks", "us", "us2", "y4", "ee", "t2", "lo"):
     SCRATCH[_n] = ("sbuf", [128, P], "float32")
-for _n in ("ui", "um", "pi", "qi", "si", "fi"):
+for _n in ("pi", "qi", "si", "fi"):
     SCRATCH[_n] = ("sbuf", [128, P], "int32")
-for _n in ("ib", "nib", "i4096", "iz", "ih", "nih", "cu", "n3bo", "n3i", "i17", "i32", "bo", "l1", "l2", "tri", "vc", "v2c", "cy", "kc", "mneg", "mneg2", "wh", "wl", "w16"):
+for _n in ("ib", "nib", "i4096", "iz", "ih", "n3bo", "n3i", "ikey", "i16", "bo", "l2", "tri", "mq", "e16", "wh", "wl", "kd", "zero", "ntri"):
     SCRATCH[_n] = ("sbuf", [128, 128], "bfloat16")
-for _n in ("pmc", "cg", "cm", "iff", "e16", "o16", "rmax", "rmin", "tmp1", "tmp2", "tmp3"):
+for _n in ("pmc", "cg", "cm", "iff", "sel0", "rsel", "rmin", "tmp1", "tmp2", "tmp3"):
     SCRATCH[_n] = ("sbuf", [128, 128], "float32")
-for _f, _l in ((REL, ("boq", "bon")), (UMS, ("ur", "cu")), (FPS, ("ih", "nih", "fpa"))):
-    if not (_f[0] or _f[1]):
-        for _n in _l:
-            SCRATCH.pop(_n)
 for _b in range(8):
     SCRATCH["ps%d" % _b] = ("psum", [128, 512], "float32")
 
@@ -83,13 +65,13 @@ HOP = 0.10
 
 def build(T, rem):
     ops = []
-    ctx = {"h": "I", "n": {}}
+    ctx = {"h": "I", "n": {}, "t": -1}
 
     def add(alts, r, w, banks=(), grp=None, sem=None, lat=0.0, name=""):
         w = list(w)
         base = (name or str(w[0][0] if isinstance(w[0], tuple) else w[0])) + ctx["h"]
         ctx["n"][base] = ctx["n"].get(base, -1) + 1
-        ops.append({"tag": "%s%d" % (base, ctx["n"][base]), "alts": alts, "r": list(r), "w": list(w), "banks": list(banks), "grp": grp, "sem": sem, "lat": lat, "name": name})
+        ops.append({"t": ctx["t"], "tag": "%s%d" % (base, ctx["n"][base]), "alts": alts, "r": list(r), "w": list(w), "banks": list(banks), "grp": grp, "sem": sem, "lat": lat, "name": name})
 
     def pk(b, a, n=1):
         return [("ps", b, a + i) for i in range(n)]
@@ -103,17 +85,17 @@ def build(T, rem):
     def S(n, fn, r, w, name=""):
         add([("S", 0.08 + max(64, n) * CYC, fn)], r, w, bk(list(r) + list(w)), name=name)
 
-    def VS(n, fv, fs, r, w, name=""):
-        add([("V", 0.06 + n * CYC, fv), ("S", 0.08 + n * CYC, fs)], r, w, bk(list(r) + list(w)), name=name)
+    def VS(n, fv, fs, r, w, name="", half=False):
+        add([("V", 0.06 + n * CYC * (0.5 if half else 1.0), fv), ("S", 0.08 + n * CYC, fs)], r, w, bk(list(r) + list(w)), name=name)
 
     def G(n, fn, r, w):
         add([("G", 0.17 + 2 * n * CYC, fn)], r, w)
 
-    def MM(mms, r, w, first=True, last=True, each=False, name=""):
+    def MM(mms, r, w, first=True, last=True, each=False, name="", pause=False):
         def fn(g):
             x = None
             for i, (o, l, rr, c) in enumerate(mms):
-                x = g.tensor.matmul(o, l, rr, bool(each or (first and i == 0)), bool(each or (last and i == len(mms) - 1)))
+                x = g.tensor.matmul(o, l, rr, bool(each or (first and i == 0)), bool(each or ((last or pause) and i == len(mms) - 1)))
             return x
         add([("T", 0.03 + sum(m[3] * PEC + PEO for m in mms), fn)], r, w, bk(w), grp=(first, last), name=name)
 
@@ -136,6 +118,13 @@ def build(T, rem):
             return lambda g: g.scalar.activation(o, i, f, bias=bias, scale=scale)
         return lambda g: g.scalar.activation(o, i, f, bias=bias, scale=scale, accum_out=acc)
 
+    def LIN(n, o, i, r, w, scale=1.0, bias=0.0, name=""):
+        VS(n, ts(o, i, scale, bias, ALU.mult, ALU.add), act(o, i, ACT.Identity, bias=bias, scale=scale), r, w, name=name)
+
+    def STEP(n, o, i, thr, r, w, up=True, name="", half=False):
+        s = 256.0 if up else -256.0
+        VS(n, ts(o, i, thr, None, ALU.is_gt if up else ALU.is_lt), act(o, i, ACT.Sigmoid, bias=-s * thr, scale=s), r, w, name=name, half=half)
+
     ps = [T["ps%d" % b] for b in range(8)]
 
     cw = W // LCH
@@ -156,91 +145,105 @@ def build(T, rem):
         else:
             G(n, lambda g: g.iota(o, pat, base, cmul), [], [key])
 
+    def lin(n, o, i, sc, r, w, bias=0.0):
+        S(n, act(o, i, ACT.Identity, bias=bias, scale=sc), r, w)
+
     iota(T.pmc[:], [[1, 128]], 0, -1, "pmc", 128)
     iota(T.ci[:, 0:1], [[0, 1]], 0, 1, "ci0", 1, False)
     iota(T.cg[:], [[16, 8], [0, 16]], 0, 0, "cg", 128)
     iota(T.cm[:], [[0, 8], [1, 16]], 0, 0, "cm", 128)
-    iota(T.io144[:], [[1, 144]], -15, 0, "io144", 144)
-    iota(T.ci[:, 8:16], [[16, 8]], 15, 0, "ci8", 8, False)
-    V(128, ts(T.iff[:], T.pmc[:], 0.0, None, ALU.is_equal), ["pmc"], ["iff"])
-    for nm, sc in (("i4096", 4096.0), ("ib", 1.0), ("nib", -1.0), ("iz", 3.0 / 4096), ("n3i", -3.0), ("i17", 2.0 ** 17), ("i32", 32.0)) + ((("ih", 0.5), ("nih", -0.5)) if FPS[0] or FPS[1] else ()):
-        S(128, act(T[nm][:], T.iff[:], ACT.Copy, scale=sc), ["iff"], [nm])
-    V(1, ts(T.ci[:, 1:2], T.ci[:, 0:1], 0x70, None, ALU.bitwise_and), ["ci0"], ["ci1"])
-    V(1, ts(T.ci[:, 2:3], T.ci[:, 0:1], 15, None, ALU.bitwise_and), ["ci0"], ["ci2"])
-    V(2, cp(T.cf[:, 1:3], T.ci[:, 1:3]), ["ci1", "ci2"], ["cf"])
-    pg16, pm = T.cf[:, 1:2], T.cf[:, 2:3]
-    V(128, ts(T.bo[:], T.cg[:], pg16, None, ALU.is_equal), ["cg", "cf"], ["bo"])
-    S(128, act(T.n3bo[:], T.bo[:], ACT.Copy, scale=-3.0), ["bo"], ["n3bo"])
-    V(8, ts(T.bo8[:], T.cg[:, 0:128:16], pg16, None, ALU.is_equal), ["cg", "cf"], ["bo8"])
-    def lin(n, o, i, sc, r, w, bias=0.0):
-        S(n, act(o, i, ACT.Identity, bias=bias, scale=sc), r, w)
-
-    lin(8, T.bo512[:], T.bo8[:], 512.0, ["bo8"], ["bo512"])
-    if REL[0] or REL[1]:
-        lin(8, T.boq[:], T.bo8[:], 0.25, ["bo8"], ["boq"])
-        lin(8, T.bon[:], T.bo8[:], -0.125, ["bo8"], ["bon"])
-    lin(1, T.cf[:, 3:4], pm, 1.0, ["cf"], ["cf3"], bias=1.0)
-    lin(8, T.wj32[:], T.bo8[:], T.cf[:, 3:4], ["bo8", "cf3"], ["wj32"])
-    lin(8, T.nwj[:], T.wj32[:], -1.0, ["wj32"], ["nwj"])
-    V(144, ts(T.wsel[:], T.io144[:], pg16, None, ALU.is_equal), ["io144", "cf"], ["wsel"])
-    G(128, lambda g: g.affine_select(T.l1[:], T.bo[:], [[-1, 128]], ALU.not_equal, 65.0, 0, 1), ["bo"], ["l1"])
-    lin(128, T.l2[:], T.bo[:], 1.125, ["bo"], ["l2"])
-    G(128, lambda g: g.affine_select(T.l2[:], T.l2[:], [[-1, 128]], ALU.not_equal, -6.75, 0, 1), ["l2"], ["l2"])
-    V(256, lambda g: g.vector.memset(T.onesb[:], 1.0), [], ["onesb"])
-    lin(128, T.v2c[:], T.onesb[:, 0:128], -7.875, ["onesb"], ["v2c"])
-    lin(128, T.o16[:], T.onesb[:, 0:128], 1.0 / 16, ["onesb"], ["o16"])
-    lin(256, T.yc[:], T.onesb[:, 0:P], 136.0 * OFF, ["onesb"], ["yc"])
-    lin(1, T.biasa[:, 0:1], T.onesb[:, 0:1], 7.0, ["onesb"], [("bias", 0)])
-    lin(128, T.cy[:], T.onesb[:, 0:128], -OFF, ["onesb"], ["cy"])
-    G(128, lambda g: g.affine_select(T.cy[:], T.cy[:], [[0, 128]], ALU.not_equal, 2048.0, -1, 1), ["cy"], ["cy"])
-    G(128, lambda g: g.affine_select(T.cy[:], T.cy[:], [[0, 128]], ALU.not_equal, -0.5, -2, 1), ["cy"], ["cy"])
-    if UMS[0] or UMS[1]:
-        V(64, lambda g: g.vector.memset(T.cu[:], -2048.0), [], ["cu"])
-        G(128, lambda g: g.affine_select(T.cu[:], T.cu[:], [[0, 128]], ALU.not_equal, 0.5, -1, 1), ["cu"], ["cu"])
-    V(128, ts(T.tmp3[:], T.cm[:], 0.0, None, ALU.is_equal), ["cm"], ["tmp3"])
-    V(128, ts(T.tmp1[:], T.pmc[:], 0.0, None, ALU.is_gt), ["pmc"], ["tmp1"])
-    V(256, tt(T.tmp1[:], T.tmp1[:], T.tmp3[:], ALU.max), ["tmp1", "tmp3"], ["tmp1"])
-    V(256, tt(T.tmp1[:], T.tmp1[:], T.bo[:], ALU.mult), ["tmp1", "bo"], ["tmp1"])
-    lin(128, T.tmp2[:], T.tmp3[:], 16.0, ["tmp3"], ["tmp2"], bias=1.0)
-    G(128, lambda g: g.affine_select(T.tmp2[:], T.tmp2[:], [[-1, 128]], ALU.is_equal, 0.0, 0, 1), ["tmp2"], ["tmp2"])
-    V(256, tt(T.tmp2[:], T.tmp2[:], T.tmp1[:], ALU.subtract), ["tmp2", "tmp1"], ["tmp2"])
-    lin(128, T.tri[:], T.tmp2[:], 1.0 / 64, ["tmp2"], ["tri"])
-    lin(128, T.vc[:], T.cm[:], -1.0 / 64, ["cm"], ["vc"], bias=-1.0)
-    lin(8, T.vc[:, 0:128:16], T.onesb[:, 0:8], -31.0 / 32, ["onesb", "vc"], ["vc"])
-    lin(128, T.kc[:], T.cm[:], 32.0, ["cm"], ["kc"])
-    lin(1, T.cf[:, 4:5], pm, 37.0, ["cf"], ["cf4"])
-    iota(T.cg160[:], [[16, 10], [0, 16]], -16, 0, "cg160", 160)
+    iota(T.io160[:], [[1, 160]], -30, 0, "io160", 160)
     iota(T.pm160[:], [[1, 160]], -16, -1, "pm160", 160)
+    iota(T.cg160[:], [[16, 10], [0, 16]], -16, 0, "cg160", 160)
     iota(T.e16[:], [[16, 128]], 0, 0, "e16", 128)
-    V(1, ts(T.ci[:, 3:4], T.ci[:, 0:1], 4, 1, ALU.logical_shift_right, ALU.bitwise_and), ["ci0"], ["ci3"])
-    V(1, cp(T.cf[:, 7:8], T.ci[:, 3:4]), ["ci3"], ["cf7"])
-    V(1, ts(T.cf[:, 6:7], T.cf[:, 7:8], -1.0, 1.0, ALU.mult, ALU.add), ["cf7"], ["cf6"])
-    V(2, ts(T.cf[:, 8:10], T.cf[:, 6:8], pm, None, ALU.mult), ["cf6", "cf7", "cf"], ["cf8"])
-    V(2, ts(T.cf[:, 10:12], T.cf[:, 6:8], 2048.0, None, ALU.mult), ["cf6", "cf7"], ["cf10"])
+    iota(T.ci[:, 8:16], [[1, 8]], 0, 0, "ci8", 8, False)
+    V(128, ts(T.iff[:], T.pmc[:], 0.0, None, ALU.is_equal), ["pmc"], ["iff"])
+    for nm, sc in (("i4096", 4096.0), ("ib", 1.0), ("nib", -1.0), ("iz", 3.0 / 4096), ("n3i", -3.0), ("ikey", -256.0), ("i16", 16.0), ("ih", 1.0 / 64), ("zero", 0.0)):
+        S(128, act(T[nm][:], T.iff[:], ACT.Copy, scale=sc), ["iff"], [nm])
+    for c, mk in ((1, 0x70), (2, 15), (4, 0x60)):
+        V(1, ts(T.ci[:, c:c + 1], T.ci[:, 0:1], mk, None, ALU.bitwise_and), ["ci0"], [("ci", c)])
+    V(1, ts(T.ci[:, 3:4], T.ci[:, 0:1], 4, 1, ALU.logical_shift_right, ALU.bitwise_and), ["ci0"], [("ci", 3)])
+    V(4, cp(T.cf[:, 1:5], T.ci[:, 1:5]), [("ci", c) for c in range(1, 5)], ["cf"])
+    pg16, pm, odd, pair = (T.cf[:, c:c + 1] for c in range(1, 5))
+    col = lambda c: T.cf[:, c:c + 1]
+    lin(1, col(5), pm, 1.0, ["cf"], ["cf5"], bias=1.0)
+    lin(1, col(6), odd, -1.0, ["cf"], ["cf6"], bias=1.0)
+    lin(1, col(7), odd, 1.0, ["cf"], ["cf6"])
+    lin(1, col(8), pm, 37.0, ["cf"], ["cf8"])
+    V(1, ts(col(10), pm, 0.0, None, ALU.is_equal), ["cf"], ["cf10"])
+    V(1, ts(col(11), col(10), 2048.0, pm, ALU.mult, ALU.add), ["cf", "cf10"], ["cf11"])
+    V(1, ts(col(13), pm, 0.5, None, ALU.is_gt), ["cf"], ["cf13"])
+    V(2, ts(T.cf[:, 14:16], T.cf[:, 6:8], col(13), None, ALU.mult), ["cf6", "cf13"], ["cf14"])
+    lin(1, T.biasa[:, 0:1], col(10), 2048.0, ["cf10"], [("bias", 0)], bias=-2944.0)
+    V(1, ts(col(17), pg16, -15.0, None, ALU.add), ["cf"], ["cf17"])
+    V(2, ts(T.cf[:, 18:20], T.cf[:, 6:8], col(11), None, ALU.mult), ["cf6", "cf11"], ["cf18"])
+    V(1, ts(col(20), pm, 14.5, -8192.0, ALU.is_lt, ALU.mult), ["cf"], ["cf20"])
+    V(128, ts(T.bo[:], T.cg[:], pg16, None, ALU.is_equal), ["cg", "cf"], ["bo"])
+    lin(128, T.n3bo[:], T.bo[:], -3.0, ["bo"], ["n3bo"])
+    lin(8, T.bo8[:], T.bo[:, 0:128:16], 1.0, ["bo"], ["bo8"])
+    lin(8, T.wj32[:], T.bo8[:], col(5), ["bo8", "cf5"], ["wj32"])
+    lin(8, T.nwj[:], T.wj32[:], -1.0, ["wj32"], ["nwj"])
+    V(144, ts(T.wsel[:], T.io160[:, 0:144], col(17), None, ALU.is_equal), ["io160", "cf17"], ["wsel"])
+    if not all(OPT["rsc"]):
+        lin(1, col(9), pm, 16.0, ["cf"], ["cf9"])
+        V(1, ts(col(12), pair, odd, None, ALU.add), ["cf"], ["cf12"])
+        lin(8, T.crow[:], T.cg[:, 0:128:16], 16.0, ["cg"], ["crow"])
+        V(160, ts(T.zr[:], T.io160[:], col(12), col(11), ALU.is_equal, ALU.mult), ["io160", "cf11", "cf12"], ["zr"])
+    lin(128, T.l2[:], T.bo[:], 2.0, ["bo"], ["l2"])
+    G(128, lambda g: g.affine_select(T.l2[:], T.l2[:], [[-1, 128]], ALU.not_equal, -12.0, 0, 1), ["l2"], ["l2"])
+    V(256, lambda g: g.vector.memset(T.onesb[:], 1.0), [], ["onesb"])
+    lin(128, T.sel0[:], T.onesb[:, 0:128], col(10), ["onesb", "cf10"], ["sel0"])
+    lin(256, T.yc[:], T.onesb[:, 0:P], 136.0 * OFF, ["onesb"], ["yc"])
+    S(128, act(T.tmp1[:], T.pmc[:], ACT.Sigmoid, bias=-128.0, scale=256.0), ["pmc"], ["tmp1"])
+    V(128, ts(T.tmp1[:], T.tmp1[:], 0.5, None, ALU.is_gt), ["tmp1"], ["tmp1"])
+    V(256, tt(T.tmp1[:], T.iff[:], T.tmp1[:], ALU.subtract), ["tmp1", "iff"], ["tmp1"])
+    V(256, tt(T.tmp1[:], T.tmp1[:], T.bo[:], ALU.mult), ["tmp1", "bo"], ["tmp1"])
+    V(128, ts(T.tmp2[:], T.cm[:], 0.5, 16.0, ALU.is_gt, ALU.mult), ["cm"], ["tmp2"])
+    V(256, tt(T.tri[:], T.tmp1[:], T.tmp2[:], ALU.mult), ["tmp1", "tmp2"], ["tri"])
+    lin(128, T.ntri[:], T.tri[:], -1.0, ["tri"], ["ntri"])
+    V(128, ts(T.tmp3[:], T.cm[:], 0.0, None, ALU.is_equal), ["cm"], ["tmp3"])
+    V(256, tt(T.tmp2[:], T.iff[:], T.bo[:], ALU.subtract), ["iff", "bo"], ["tmp2"])
+    V(256, tt(T.tmp2[:], T.tmp2[:], T.tmp3[:], ALU.mult), ["tmp2", "tmp3"], ["tmp2"])
+    V(256, tt(T.mq[:], T.tmp2[:], T.iff[:], ALU.add), ["tmp2", "iff"], ["mq"])
     for e in range(2):
-        V(160, ts(T["zb%d" % e][:], T.cg160[:], pg16, T.cf[:, 8 + e:9 + e], ALU.is_equal, ALU.mult), ["cg160", "cf", "cf8"], ["zb%d" % e])
-        V(160, ts(T["zl%d" % e][:], T.cg160[:], pg16, T.cf[:, 10 + e:11 + e], ALU.is_equal, ALU.mult), ["cg160", "cf", "cf10"], ["zl%d" % e])
-        V(160, ts(T["zi%d" % e][:], T.pm160[:], 0.0, T.cf[:, 6 + e:7 + e], ALU.is_equal, ALU.mult), ["pm160", "cf6", "cf7"], ["zi%d" % e])
-        S(160, act(T["zt%d" % e][:], T["zi%d" % e][:], ACT.Copy, scale=3.0), ["zi%d" % e], ["zt%d" % e])
-        for c in range(4):
-            S(512, act(T["dm%d" % e][:, c * 512:(c + 1) * 512], T.onesb[:], ACT.Copy, scale=OFF), ["onesb"], [("dmc", e)])
-        V(1, ts(T.cf[:, 12 + e:13 + e], pm, 4.0 * (4 - FZS[e]) - 0.5, -11.5, ALU.is_gt, ALU.mult), ["cf"], [("thr", e)])
-        V(1, ts(T.cf[:, 12 + e:13 + e], T.cf[:, 12 + e:13 + e], 36.5, None, ALU.add), [("thr", e)], [("thr", e)])
-        if BES[e]:
-            V(1, ts(T.cf[:, 14 + e:15 + e], T.cf[:, 12 + e:13 + e], -1.0, None, ALU.mult), [("thr", e)], [("nthr", e)])
-    V(128, ts(T.mneg[:], T.cm[:], pm, -8192.0, ALU.not_equal, ALU.mult), ["cm", "cf"], ["mneg"])
-    V(256, tt(T.mneg2[:], T.mneg[:], T.e16[:], ALU.add), ["mneg", "e16"], ["mneg2"])
-    lin(128, T.rmax[:], T.tmp3[:], -65536.0, ["tmp3"], ["rmax"])
-    lin(128, T.rmin[:], T.tmp3[:], 2.0 ** 21, ["tmp3"], ["rmin"])
-    V(8, cp(T.bcoff[:], T.ci[:, 8:16]), ["ci8"], ["bcoff"])
-    for e in range(2):
+        V(160, ts(T["zi%d" % e][:], T.pm160[:], 0.0, col(6 + e), ALU.is_equal, ALU.mult), ["pm160", "cf6"], ["zi%d" % e])
+        V(160, ts(T["zd%d" % e][:], T.pm160[:], -1.0, col(14 + e), ALU.is_equal, ALU.mult), ["pm160", "cf14"], ["zd%d" % e])
+        V(320, tt(T["zd%d" % e][:], T["zi%d" % e][:], T["zd%d" % e][:], ALU.subtract), ["zi%d" % e, "zd%d" % e], ["zd%d" % e])
+        V(160, ts(T["zq%d" % e][:], T.cg160[:], pg16, col(18 + e), ALU.is_equal, ALU.mult), ["cg160", "cf", "cf18"], ["zq%d" % e])
+        lin(160, T["zt%d" % e][:], T["zi%d" % e][:], 3.0, ["zi%d" % e], ["zt%d" % e])
         V(8, ts(T.basel[:, 8 * e:8 * e + 8], T.cg[:, 0:128:16], pm, 16.0, ALU.add, ALU.mult), ["cg", "cf"], ["basel"])
-    for c, mk in ((1, 0xFC0), (2, 63), (3, 15)):
-        V(1, ts(T.wj[:, c:c + 1], T.wi[:, 0:1], mk, None, ALU.bitwise_and), ["wi"], [("wj", c)])
+    V(128, ts(T.rsel[:], T.cm[:], pm, -65536.0, ALU.is_equal, ALU.mult), ["cm", "cf"], ["rsel"])
+    V(128, ts(T.tmp1[:], T.cm[:], col(5), 8192.0, ALU.is_equal, ALU.mult), ["cm", "cf5"], ["tmp1"])
+    V(256, tt(T.rsel[:], T.rsel[:], T.tmp1[:], ALU.add), ["rsel", "tmp1"], ["rsel"])
+    lin(128, T.rmin[:], T.tmp3[:], 4096.0, ["tmp3"], ["rmin"])
+    V(8, cp(T.bcoff[:], T.ci[:, 8:16]), ["ci8"], ["bcoff"])
+    wc = lambda c: T.wf[:, c:c + 1]
+    V(1, ts(T.wj[:, 0:1], T.wi[:, 0:1], 2048.0, None, ALU.add), ["wi"], [("wj", 0)])
+    for c, src, mk in ((1, T.wj, 0xFC0), (2, T.wi, 63), (3, T.wi, 15)):
+        V(1, ts(T.wj[:, c:c + 1], src[:, 0:1], mk, None, ALU.bitwise_and), ["wi", ("wj", 0)], [("wj", c)])
     V(3, cp(T.wf[:, 1:4], T.wj[:, 1:4]), [("wj", 1), ("wj", 2), ("wj", 3)], ["wf"])
-    for c, nm in ((1, "wh"), (2, "wl"), (3, "w16")):
-        lin(128, T[nm][:], T.bo[:], T.wf[:, c:c + 1], ["bo", "wf"], [nm])
+    V(1, ts(wc(1), wc(1), -2048.0, None, ALU.add), ["wf"], ["wf"])
+    if not OPT["usc"]:
+        lin(144, T.zw[:], T.wsel[:], wc(3), ["wsel", "wf"], ["zw"])
+    for c, nm in ((1, "wh"), (2, "wl")):
+        lin(128, T[nm][:], T.bo[:], wc(c), ["bo", "wf"], [nm])
+    MM([(ps[7][:, Q:Q + 1], T.wh[:], T.onesb[:, 0:1], 64), (ps[7][:, Q:Q + 1], T.wl[:], T.onesb[:, 0:1], 64)], ["wh", "wl", "onesb"], pk(7, 1))
+    V(1, ts(wc(4), ps[7][:, Q:Q + 1], 7.5, BIGU, ALU.mult, ALU.add), pk(7, 1), ["wf4"])
+    V(1, ts(wc(5), wc(4), BIGU, -1.0, ALU.subtract, ALU.mult), ["wf4"], ["wf5"])
+    lin(1, wc(6), wc(5), 1.0, ["wf5"], ["wf6"], bias=OFF)
+    lin(1, wc(7), wc(5), 1.0, ["wf5"], ["wf7"], bias=OFF - 2047.5)
+    lin(128, T.kd[:], T.ib[:], wc(6), ["ib", "wf6"], ["kd"])
     V(256, cp(T.roff[:, 0:P], T.jin[:]), ["jin"], [("r", 0, 0), ("r", 0, 1)])
+    V(256, cp(T.rf[:, 0:P], T.jin[:]), ["jin"], [("rf", 0, 0), ("rf", 0, 1)])
+
+    for e in range(2):
+        iota(T["dm%d" % e][:, 0:2048], [[0, 2048]], int(OFF), 0, ("dmc", e), 2048)
+    sel = lambda k: T.wsel[:, 15 - k:143 - k]
+    r4 = lambda b, i: ps[b][:, i * Q:(i + 1) * Q]
+    for q in range(4):
+        for kk in range(4):
+            MM([(r4(4 + q % 2, kk), T.ib[:], sel(4 * q + kk), 128), (r4(4 + q % 2, kk), T.ib[:], T.ih[:], 128)], ["ib", "ih", "wsel"], pk(4 + q % 2, kk))
+        lin(512, T.cbs[:, q * 512:(q + 1) * 512], ps[4 + q % 2][:], 1.0, pk(4 + q % 2, 0, 4), ["cbs"])
 
     for c in range(8):
         b = 2 + c % 2
@@ -252,230 +255,221 @@ def build(T, rem):
 
     for t in range(NV):
         TABR = TAB + ([("tabc", c) for c in range(8)] if t == 0 else [])
-        ctx["n"] = {}
-        for h in range(2):
+        ctx["n"], ctx["t"] = {}, t
+        def half(h):
             ctx["h"] = "AB"[h]
             hs = slice(h * Q, (h + 1) * Q)
             o = t * P + h * Q
             ts_ = slice(o, o + Q)
             pg, d, ad, far, dm, zg, fz = (T["%s%d" % (n, h)] for n in ("pg", "d", "ad", "far", "dm", "zg", "fz"))
             K = lambda n, h=h: (n, h)
-            B = ps[h]
-            y = T.ybuf[:, ts_]
-            yk = ("y", t, h)
-            pw = Q // GCH
-            PG = [("pg", h, c) for c in range(GCH)]
-            ZG = [("zg", h, c) for c in range(GCH)]
-            r4 = lambda b, i: ps[b][:, i * Q:(i + 1) * Q]
-            for c in range(GCH):
+            X, Y, Z = h, 4 + h, 6 + h
+            B = ps[X]
+            y, yk = T.ybuf[:, ts_], ("y", t, h)
+            rf, rfk = T.rf[:, ts_], ("rf", t, h)
+            R37, NC, NMR, UU = (r4(Z, i) for i in range(4))
+            n1, n2 = OPT["g1"][h], OPT["g2"][h]
+            PG = [("pg", h, c) for c in range(n1)]
+            ZG = [("zg", h, c) for c in range(n2)]
+            pw = Q // n1
+            for c in range(n1):
                 offs = T.roff[:, o + c * pw:o + (c + 1) * pw]
                 out = pg[:, c * pw * 16:(c + 1) * pw * 16]
-                VS(16 * pw * GC, (lambda g, out=out, offs=offs: g.vector.tensor_copy(out, T.tab[:, 0:W].indirect(offs))),
-                   (lambda g, out=out, offs=offs: g.scalar.activation(out, T.tab[:, 0:W].indirect(offs), ACT.Copy)),
+                VS(16 * pw * GC, (lambda g, out=out, offs=offs: g.vector.tensor_scalar(out, T.tab[:, 0:W].indirect(offs), OFF - 2047.5, None, ALU.add)),
+                   (lambda g, out=out, offs=offs: g.scalar.activation(out, T.tab[:, 0:W].indirect(offs), ACT.Identity, bias=OFF - 2047.5)),
                    TABR + [("r", t, h)], [("pg", h, c)], name="G1")
-            rf, rfk = T.rf[:, ts_], ("rf", t, h)
-            if t == 0 or not SENDF:
-                V(128, cp(rf, T.roff[:, ts_]), [("r", t, h)], [rfk])
-            pb = 6 + h
-            RP, R37, NC, NMR = (r4(pb, i) for i in range(4))
-            S(128, act(RP, rf, ACT.Copy), [rfk], pk(pb, 0), name="RP")
-            S(128, act(R37, rf, ACT.Identity, bias=T.cf[:, 4:5]), [rfk, "cf4"], pk(pb, 1), name="R37")
-            MM([(B[:, 0:512], T.cy[0:3, :], T.onesb[0:3, :], 512)] + [(B[:, kk:512:4], T.i4096[:], y, 128) for kk in range(4)],
-               ["cy", "onesb", "i4096", yk], pk(h, 0, 4), name="ybc")
+            ub, ur_ = (Y, 1) if OPT["uy"] else (Z, 3)
+            UU = r4(ub, ur_)
+            LIN(128, R37, rf, [rfk, "cf8"], pk(Z, 0), bias=col(8), name="R37")
+            sp = OPT["sp"][h]
+            if sp:
+                for c, b in enumerate((X, 2 + h)):
+                    MM([(ps[b][:, kk:512:8], T.i4096[:], T.ybuf[:, o + 64 * c:o + 64 * c + 64], 64) for kk in range(8)], ["i4096", yk], pk(b, 0, 4), each=True, name="ybc")
+            else:
+                MM([(B[:, kk:512:4], T.i4096[:], y, 128) for kk in range(4)], ["i4096", yk], pk(X, 0, 4), each=True, name="ybc")
             for q in range(4):
-                MM([(ps[pb][:, 2 * Q + k:3 * Q:16], pg[:, k:16 * Q:16], T.iff[:, (k + t) % 16:128:16], 256) for k in range(4 * q, 4 * q + 4)],
-                   PG + ["iff"], [("ps", pb, 2)], each=True, name="NT")
-            S(128, act(T.nf[:, hs], NC, ACT.Identity, bias=OFF), pk(pb, 2), [K("nf")])
-            S(128, act(T.rr[:, hs], NC, ACT.Identity, bias=OFF - 2047.5), pk(pb, 2), [K("rr")])
-            MM([(NC, T.nf[:, hs], T.iff[:], 512), (NC, T.rr[:, hs], T.nib[:], 128)], [K("nf"), K("rr"), "iff", "nib"], pk(pb, 2), name="NC")
-            V(128, cp(T.noff[:, hs], NC), pk(pb, 2), [K("noff")])
-            V(128, tt(NMR, NC, rf, ALU.subtract), pk(pb, 2) + [rfk], pk(pb, 3), name="NMR")
-            for c in range(GCH):
+                MM([(ps[Z][:, Q + k:2 * Q:16], pg[:, k:16 * Q:16], T.iff[:, (k + t) % 16:128:16], 256) for k in range(4 * q, 4 * q + 4)],
+                   PG + ["iff"], pk(Z, 1) + pk(Z, 9), each=True, name="NT")
+            LIN(128, T.nf[:, hs], NC, pk(Z, 1), [K("nf")], bias=2047.5)
+            LIN(128, T.rr[:, hs], NC, pk(Z, 1), [K("rr")])
+            MM([(NC, T.nf[:, hs], T.iff[:], 512), (NC, T.rr[:, hs], T.nib[:], 128)], [K("nf"), K("rr"), "iff", "nib"], pk(Z, 1) + pk(Z, 9), name="NC")
+            V(128, cp(T.noff[:, hs], NC), pk(Z, 1), [K("noff")])
+            V(128, tt(NMR, NC, rf, ALU.subtract), pk(Z, 1) + [rfk], pk(Z, 2), name="NMR")
+            pw = Q // n2
+            for c in range(n2):
                 offs = T.noff[:, h * Q + c * pw:h * Q + (c + 1) * pw]
                 out = zg[:, c * pw * 16:(c + 1) * pw * 16]
                 VS(16 * pw * GC, (lambda g, out=out, offs=offs: g.vector.tensor_scalar(out, T.tab[:, 0:W].indirect(offs), OFF - 2047.5, None, ALU.add)),
                    (lambda g, out=out, offs=offs: g.scalar.activation(out, T.tab[:, 0:W].indirect(offs), ACT.Identity, bias=OFF - 2047.5)),
                    TABR + [K("noff")], [("zg", h, c)], name="G2")
             for q in range(4):
-                qs = slice(q * 512, (q + 1) * 512)
-                V(512, tt(d[:, q:16 * Q:4], pg[:, q:16 * Q:4], B[:, 0:512], ALU.subtract), PG + pk(h, 0, 4), [("d", h, q)], name="SUB")
-            DD = [("d", h, q) for q in range(4)]
-            sel = lambda k: T.wsel[:, 15 - k:143 - k]
-            for c in range(2):
-                cs = slice(c * 1024, (c + 1) * 1024)
-                V(512, ts(far[:, cs], d[:, cs], FB - OFF, FB, ALU.add, ALU.not_equal), DD, [("far", h, c)], name="FAR")
-                if REL[h]:
-                    V(512, ts(ad[:, cs], d[:, cs], OFF, 0.0, ALU.subtract, ALU.max), DD, [("ad", h, 2 * c), ("ad", h, 2 * c + 1)], name="REL")
+                if sp:
+                    c, b = q // 2, (X, 2 + h)[q // 2]
+                    qs = slice(c * 1024 + q % 2, (c + 1) * 1024, 2)
+                    V(512, tt(d[:, qs], pg[:, qs], ps[b][:], ALU.subtract), PG[c * n1 // 2:(c + 1) * n1 // 2] + pk(b, 0, 4), [("d", h, q)], name="SUB")
                 else:
-                    S(1024, act(ad[:, cs], d[:, cs], ACT.Abs, bias=-192.0, scale=1.0 / 4096), DD, [("ad", h, 2 * c), ("ad", h, 2 * c + 1)], name="ABS")
-            for c in range(2):
+                    V(512, tt(d[:, q:16 * Q:4], pg[:, q:16 * Q:4], B[:, 0:512], ALU.subtract), PG + pk(X, 0, 4), [("d", h, q)], name="SUB")
+            yield
+            ctx["h"] = "AB"[h]
+            DA = [("d", h, q) for q in range(4)]
+            AD = [("ad", h, q) for q in range(4)]
+            nch = OPT["nch"][h]
+            cl = 2048 // nch
+            for c in range(nch):
+                cs = slice(c * cl, (c + 1) * cl)
+                DD = DA[2 * c:2 * c + 2] if sp and nch == 2 else DA
+                V(cl // 2, ts(far[:, cs], d[:, cs], FB - OFF, FB, ALU.add, ALU.not_equal), DD, [("far", h, c)], name="FAR")
+                S(cl, act(ad[:, cs], d[:, cs], ACT.Abs, bias=-192.0, scale=1.0 / 4096), DD, AD[4 * c // nch:4 * (c + 1) // nch], name="ABS")
+                V(cl // 2, (lambda g, c=c, cs=cs, d=d, dm=dm, cl=cl: g.vector.transpose(dm[:, 2048 + c * cl:2048 + (c + 1) * cl], d[:, cs])), DD, [("dm", h, c)], name="TR")
+            wd = Q // nch
+            for c in range(nch):
                 for q in range(2):
-                    MM([(ps[4][:, h * Q + 64 * c:h * Q + 64 * c + 64], sel(k), far[:, c * 1024 + k:(c + 1) * 1024:16], 64) for k in range(8 * q, 8 * q + 8)],
-                       ["wsel", ("far", h, c)], pk(4, h), first=q == 0, last=q == 1, name="CNT")
-                for q in range(2):
-                    MM([(ps[5][:, h * Q + 64 * c:h * Q + 64 * c + 64], T.ib[:], far[:, c * 1024 + k:(c + 1) * 1024:16], 64) for k in range(8 * q, 8 * q + 8)],
-                       ["ib", ("far", h, c)], pk(5, h), first=q == 0, last=q == 1, name="BB")
-            S(128, act(T.sa[:, hs], r4(4, h), ACT.Sign, bias=4.5, scale=-1.0), pk(4, h), [K("sa")])
-            VS(128, cp(T.cb[:, hs], r4(4, h)), act(T.cb[:, hs], r4(4, h), ACT.Copy), pk(4, h), [K("cb")])
-            S(128, act(T.fl[:, hs], r4(5, h), ACT.Sign, bias=-8.5), pk(5, h), [K("fl")])
-            MM([(r4(h, 0), T.bo[:], T.sa[:, hs], 128)], ["bo", K("sa")], pk(h, 0))
-            MM([(r4(h, 1), T.vc[0:1, :], T.onesb[0:1, 0:Q], 128), (r4(h, 1), T.tri[:], T.fl[:, hs], 128)], ["vc", "onesb", "tri", K("fl")], pk(h, 1))
-            S(128, act(T.sl[:, hs], r4(h, 0), ACT.Sign, bias=T.biasa[:, t:t + 1], acc=T.acc[:, 2 * t + h:2 * t + h + 1]), pk(h, 0) + [("bias", t)], [K("sl"), ("acc", t, h)])
-            V(128, tt(T.m[:, hs], r4(h, 1), T.sl[:, hs], ALU.is_gt), pk(h, 1) + [K("sl")], [K("m")], name="m")
-            kcol = lambda k: ps[4][:, (2 + h) * Q + k:(3 + h) * Q:16]
-            MM([(r4(4, 2 + h), T.onesb[0:1, 0:Q], T.kc[0:1, :], 128), (r4(4, 2 + h), T.sa[:, hs], T.i17[:], 128)]
-               + [(kcol(k), ad[:, k:16 * Q:16], (T.boq if REL[h] else T.bo512)[:], 64) for k in range(8)],
-               ["onesb", "kc", "i17", "bo512", "boq", K("sa")] + [("ad", h, q) for q in range(4)], pk(4, 2 + h), last=False, name="KEY")
-            MM([(kcol(k), ad[:, k:16 * Q:16], (T.boq if REL[h] else T.bo512)[:], 64) for k in range(8, 16)],
-               ["bo512", "boq"] + [("ad", h, q) for q in range(4)], pk(4, 2 + h), first=False, last=not REL[h], name="KEY")
-            if REL[h]:
-                for q in range(2):
-                    MM([(kcol(k), d[:, k:16 * Q:16], T.bon[:], 64) for k in range(8 * q, 8 * q + 8)], ["bon"] + DD, pk(4, 2 + h), first=False, last=q == 1, name="KEY")
-            VS(128, cp(T.ky[:, hs], r4(4, 2 + h)), act(T.ky[:, hs], r4(4, 2 + h), ACT.Copy), pk(4, 2 + h), [K("ky")], name="ky")
-            V(128, lambda g, hs=hs: g.vector.tensor_tensor_scan(T.ks[:, hs], T.rmin[:], T.ky[:, hs], 0.0, ALU.add, ALU.min), ["rmin", K("ky")], [K("ks")])
-            V(128 * GC, lambda g, hs=hs: g.vector.tensor_tensor(T.dT[:, hs], T.ks[:, hs].indirect(T.bcoff[:, 0:8]), T.ky[:, hs], ALU.is_equal),
-              [K("ks"), K("ky"), "bcoff"], [K("dT")], name="eq")
-            MM([(r4(4, 2 + h), T.dT[:, hs], T.ib[:], 128)], [K("dT"), "ib"], pk(4, 2 + h), name="EM")
-            VS(128, cp(T.em[:, hs], r4(4, 2 + h)), act(T.em[:, hs], r4(4, 2 + h), ACT.Copy), pk(4, 2 + h), [K("em")], name="em")
-            for c in range(2):
-                V(512, (lambda g, c=c, d=d, dm=dm: g.vector.transpose(dm[:, 2048 + c * 1024:3072 + c * 1024], d[:, c * 1024:(c + 1) * 1024])),
-                  [("d", h, q) for q in range(4)], [("dm", h, c)], name="TR")
-            mm = [(r4(h, 2), T.ib[:], T.mneg2[:], 128)]
-            for g0 in range(2):
-                for j0 in range(2):
-                    sft = 16 * (1 - (j0 - g0))
-                    for nm in ("zb", "zl"):
-                        mm.append((B[:, 2 * Q + g0:3 * Q:2], T["%s%d" % (nm, g0)][:, sft:sft + 128], T.m[:, h * Q + j0:(h + 1) * Q:2], 64))
-            MM(mm, ["ib", "mneg2", "zb0", "zb1", "zl0", "zl1", K("m")], pk(h, 2), name="RHO")
-            V(128, lambda g, h=h, hs=hs, B=B: g.vector.tensor_tensor_scan(T.us[:, hs], T.rmax[:], B[:, 2 * Q:3 * Q], 0.0, ALU.add, ALU.max),
-              ["rmax"] + pk(h, 2), [K("us")], name="rscan")
-            V(8, cp(T.toff[:, 8 * h:8 * h + 8], T.us[:, h * Q + 15:(h + 1) * Q:16]), [K("us")], [K("toff")])
+                    mm = [(r4(Y, 0), T.zero[0:1, :], T.onesb[0:1, 0:Q], 128)] if nch > 1 and c == 0 and q == 0 else []
+                    MM(mm + [(ps[Y][:, wd * c:wd * (c + 1)], T.cbs[:, k * Q:(k + 1) * Q], far[:, c * cl + k:(c + 1) * cl:16], wd) for k in range(8 * q, 8 * q + 8)],
+                       ["cbs", "zero", "onesb", ("far", h, c)], pk(Y, 0), first=c == 0 and q == 0, last=c == nch - 1 and q == 1, name="CNT")
+            dis, fl = T.dsg[:, hs], T.fl[:, hs]
+            S(128, act(dis, r4(Y, 0), ACT.Sign, bias=-4.5), pk(Y, 0), [K("dis")])
+            LIN(128, T.cb[:, hs], r4(Y, 0), pk(Y, 0), [K("cb")], bias=191.875)
+            LIN(128, fl, r4(Y, 0), pk(Y, 0), [K("fl")], bias=192.5 - 8.5 / 64)
+            MM([(r4(X, 0), T.bo[:], dis, 128), (r4(X, 0), T.tri[:], fl, 128), (r4(X, 0), T.ntri[:], T.cb[:, hs], 128)],
+               ["bo", "tri", "ntri", K("dis"), K("fl"), K("cb")], pk(X, 0), name="M")
+            S(128, act(T.m[:, hs], r4(X, 0), ACT.Sigmoid, bias=T.biasa[:, t:t + 1], scale=128.0, acc=T.acc[:, 2 * t + h:2 * t + h + 1]),
+              pk(X, 0) + [("bias", t)], [K("m"), ("acc", t, h)])
+            kcol = lambda k: ps[Y][:, 2 * Q + k:3 * Q:16]
+            MM([(r4(Y, 2), dis, T.ikey[:], 128)] + [(kcol(k), ad[:, k:16 * Q:16], T.bo8[:], 64) for k in range(8)],
+               ["ikey", "bo8", K("dis")] + AD, pk(Y, 2), last=False, name="KEY")
+            MM([(kcol(k), ad[:, k:16 * Q:16], T.bo8[:], 64) for k in range(8, 16)], ["bo8"] + AD, pk(Y, 2), first=False, name="KEY")
+            V(128, lambda g, hs=hs, Y=Y: g.vector.tensor_tensor_scan(T.ks[:, hs], T.rmin[:], r4(Y, 2), 0.0, ALU.add, ALU.min), ["rmin"] + pk(Y, 2), [K("ks")])
+            VS(64, cp(T.km[:, 8 * h:8 * h + 8], T.ks[:, h * Q + 15:(h + 1) * Q:16]), act(T.km[:, 8 * h:8 * h + 8], T.ks[:, h * Q + 15:(h + 1) * Q:16], ACT.Copy), [K("ks")], [K("km")])
+            V(128 * GC, lambda g, hs=hs: g.vector.tensor_tensor(T.dT[:, hs], T.km[:, 8 * h:8 * h + 8].indirect(T.bcoff[:, 0:8]), T.ks[:, hs], ALU.is_equal),
+              [K("ks"), K("km"), "bcoff"], [K("dT")], name="eq")
+            MM([(r4(Y, 2), T.dT[:, hs], T.ib[:], 128)], [K("dT"), "ib"], pk(Y, 2), name="EM")
+            LIN(128, T.em[:, hs], r4(Y, 2), pk(Y, 2), [K("em")])
+            if OPT["rsc"][h]:
+                mm = [(r4(X, 2), T.onesb[0:1, 0:Q], T.e16[0:1, :], 128)]
+                for g0 in range(2):
+                    for j0 in range(2):
+                        sft = 16 * (1 - (j0 - g0))
+                        mm.append((B[:, 2 * Q + g0:3 * Q:2], T["zq%d" % g0][:, sft:sft + 128], T.m[:, h * Q + j0:(h + 1) * Q:2], 64))
+                MM(mm, ["onesb", "e16", "zq0", "zq1", K("m")], pk(X, 2), name="RHO")
+                V(128, lambda g, hs=hs, X=X: g.vector.tensor_tensor_scan(T.us[:, hs], T.rsel[:], r4(X, 2), 0.0, ALU.add, ALU.max), ["rsel"] + pk(X, 2), [K("us")])
+                V(8, ts(T.toff[:, 8 * h:8 * h + 8], T.us[:, h * Q + 15:(h + 1) * Q:16], col(20), None, ALU.add), [K("us"), "cf20"], [K("toff")])
+            else:
+                rho = B[:, 2 * Q:2 * Q + 8]
+                mm = [(rho, T.onesb[0:1, 0:Q], T.crow[0:1, :], 64)]
+                for i4 in range(16):
+                    sft = 30 - 16 * (i4 % 2) - 2 * (i4 // 2)
+                    mm.append((rho, T.zr[:, sft:sft + 128], T.m[:, h * Q + i4:(h + 1) * Q:16], 64))
+                MM(mm, ["onesb", "crow", "zr", K("m")], pk(X, 2), name="RHO")
+                V(8, ts(T.toff[:, 8 * h:8 * h + 8], rho, col(9), None, ALU.add), pk(X, 2) + ["cf9"], [K("toff")])
             VS(128 * GC, (lambda g, h=h, hs=hs, dm=dm: g.vector.tensor_scalar(T.dr2[:, hs], dm[:, 0:4096].indirect(T.toff[:, 8 * h:8 * h + 8]), 1.0 / 4096, -192.0, ALU.mult, ALU.add)),
                (lambda g, h=h, hs=hs, dm=dm: g.scalar.activation(T.dr2[:, hs], dm[:, 0:4096].indirect(T.toff[:, 8 * h:8 * h + 8]), ACT.Identity, bias=-192.0, scale=1.0 / 4096)),
-               [K("toff"), ("dm", h, 0), ("dm", h, 1), K("dmc")], [K("dr2")], name="dr2")
+               [K("toff"), K("dmc")] + [("dm", h, c) for c in range(nch)], [K("dr2")], name="dr2")
+            back = lambda nm, reg, j0: [(B[:, reg * Q + j0:(reg + 1) * Q:2], T["%s%d" % (nm, j0)][:, 16 * (1 - (g0 - j0)):16 * (1 - (g0 - j0)) + 128],
+                                         T.dr2[:, h * Q + g0:(h + 1) * Q:2], 64) for g0 in range(2)]
             for j0 in range(2):
-                MM([(B[:, 3 * Q + j0:4 * Q:2], T["zi%d" % j0][:, 16 * (1 - (g0 - j0)):16 * (1 - (g0 - j0)) + 128], T.dr2[:, h * Q + g0:(h + 1) * Q:2], 64) for g0 in range(2)],
-                   ["zi0", "zi1", K("dr2")], pk(h, 3), name="DR")
-            V(128, tt(T.dr[:, hs], r4(h, 3), T.em[:, hs], ALU.mult), pk(h, 3) + [K("em")], [K("dr")], name="de")
-            MM([(r4(h, 0), T.bo[:], T.dr[:, hs], 128)], [K("dr"), "bo"], pk(h, 0), name="DEL")
-            back = lambda reg, j0: [(B[:, reg * Q + j0:(reg + 1) * Q:2], T["zt%d" % j0][:, 16 * (1 - (g0 - j0)):16 * (1 - (g0 - j0)) + 128],
-                                     T.dr2[:, h * Q + g0:(h + 1) * Q:2], 64) for g0 in range(2)]
+                MM(back("zd", 3, j0), ["zd0", "zd1", K("dr2")], pk(X, 3), name="DR")
+            V(128, tt(T.dr[:, hs], r4(X, 3), T.em[:, hs], ALU.mult), pk(X, 3) + [K("em")], [K("dr")], name="de")
+            MM([(r4(X, 0), T.bo[:], T.dr[:, hs], 128)], [K("dr"), "bo"], pk(X, 0), name="DEL")
             for j0 in range(2):
-                MM(back(2, j0), ["zt0", "zt1", K("dr2")], pk(h, 2), name="DR3")
+                MM(back("zt", 2, j0), ["zt0", "zt1", K("dr2")], pk(X, 2), name="DR3")
             for j0 in range(2):
-                MM(back(1, j0) + [(B[:, Q + j0:2 * Q:2], T.n3bo[:], T.dr[:, h * Q + j0:(h + 1) * Q:2], 64)], ["zt0", "zt1", "n3bo", K("dr2"), K("dr")], pk(h, 1), name="DD3")
-            V(128, tt(T.tt[:, hs], r4(h, 0), T.m[:, hs], ALU.mult), pk(h, 0) + [K("m")], [K("tt")])
-            fps = slice(2 * h * Q, 2 * (h + 1) * Q)
-            if FPS[h]:
-                S(256, act(T.fpa[:, fps], B[:, Q:3 * Q], ACT.Abs), pk(h, 1, 2), [K("fpa")])
-                S(256, act(T.fp[:, fps], T.fpa[:, fps], ACT.Sign, bias=-7.5), [K("fpa")], [K("fp")])
-            else:
-                V(256, ts(T.fp[:, fps], B[:, Q:3 * Q], BIG16, BIG16, ALU.add, ALU.not_equal), pk(h, 1, 2), [K("fp")])
-            pos, neg = (T.ih, T.nih) if FPS[h] else (T.ib, T.nib)
-            yn = T.ynew[:, ts_]
-            ynk = ("yn", t, h)
-            if YV[h]:
-                V(256, tt(yn, y, T.tt[:, hs], ALU.add), [yk, K("tt")], [ynk], name="ynew")
-            else:
-                MM([(r4(h, 3), T.ib[:], y, 128), (r4(h, 3), T.ib[:], T.tt[:, hs], 128)], ["ib", yk, K("tt")], pk(h, 3), name="YN")
-                VS(128, cp(yn, r4(h, 3)), act(yn, r4(h, 3), ACT.Copy), pk(h, 3), [ynk], name="ynew")
-            S(128, act(T.y4[:, hs], yn, ACT.Copy, scale=4096.0), [ynk], [K("y4")])
+                MM(back("zt", 1, j0) + [(B[:, Q + j0:2 * Q:2], T.n3bo[:], T.dr[:, h * Q + j0:(h + 1) * Q:2], 64)], ["zt0", "zt1", "n3bo", K("dr2"), K("dr")], pk(X, 1), name="DD3")
+            V(128, tt(T.tt[:, hs], r4(X, 0), T.m[:, hs], ALU.mult), pk(X, 0) + [K("m")], [K("tt")])
+            V(256, ts(T.fp[:, 2 * h * Q:2 * (h + 1) * Q], B[:, Q:3 * Q], BIG16, BIG16, ALU.add, ALU.not_equal), pk(X, 1, 2), [K("fp")])
+            yn, ynk = T.ynew[:, ts_], ("yn", t, h)
+            MM([(r4(X, 3), T.ib[:], y, 128), (r4(X, 3), T.mq[:], T.tt[:, hs], 128)], ["ib", "mq", yk, K("tt")], pk(X, 3), name="YN")
+            LIN(128, yn, r4(X, 3), pk(X, 3), [ynk], name="ynew")
+            LIN(128, T.y4[:, hs], yn, [ynk], [K("y4")], scale=4096.0)
             if t < NV - 1:
                 DMA("G", rem(T.ybuf[:, o + P:o + P + Q], yn, "ay%d%d" % (t + 1, h)), [ynk], [("y", t + 1, h)], "ay%d%d" % (t + 1, h), rem(None, None, None), 3.0)
             else:
                 DMA("Y", lambda g, yn=yn, hs=hs: g.sync.dma_start(T.yo[:, hs], yn), [ynk], [K("yo")], "oy%d" % h, 16, 2.0)
-            MM([(r4(h, 0), T.ib[:], T.cb[:, hs], 128), (r4(h, 0), pos[:], T.fp[:, 2 * h * Q:(2 * h + 1) * Q], 128), (r4(h, 0), neg[:], T.fp[:, (2 * h + 1) * Q:(2 * h + 2) * Q], 128)],
-               ["ib", "nib", "ih", "nih", K("cb"), K("fp")], pk(h, 0))
-            S(128, act(T.s2[:, hs], r4(h, 0), ACT.Sign, bias=4.5, scale=-1.0), pk(h, 0), [K("s2")])
-            MM([(r4(h, 1), T.l1[:], T.s2[:, hs], 128)], ["l1", K("s2")], pk(h, 1))
-            MM([(r4(h, 2), T.v2c[0:1, :], T.onesb[0:1, 0:Q], 128), (r4(h, 2), T.l2[:], T.s2[:, hs], 128)], ["v2c", "onesb", "l2", K("s2")], pk(h, 2))
-            MM(([(r4(h, 3), T.cu[0:2, :], T.onesb[0:2, 0:Q], 128)] if UMS[h] else []) + [(r4(h, 3), T.wh[:], yn, 128), (r4(h, 3), T.wl[:], yn, 128)],
-               ["wh", "wl", "cu", "onesb", ynk], pk(h, 3), name="U")
-            MM([(r4(4, 2 + h), T.w16[:], yn, 128), (r4(4, 2 + h), T.ib[:], T.mneg[:], 128)], ["w16", "ib", "mneg", ynk], pk(4, 2 + h), name="U2")
-            S(128, act(T.sw[:, hs], r4(h, 1), ACT.Sign, bias=-71.0), pk(h, 1), [K("sw")])
-            V(128, ts(T.gam[:, hs], r4(h, 2), BIG16, BIG16, ALU.add, ALU.is_equal), pk(h, 2), [K("gam")])
-            if UMS[h]:
-                S(128, act(T.ur[:, hs], r4(h, 3), ACT.Identity, bias=BIGU), pk(h, 3), [K("ui")])
-                S(128, act(T.rr[:, hs], T.ur[:, hs], ACT.Identity, bias=-BIGU), [K("ui")], [K("rr")], name="um")
-                MM([(r4(h, 3), T.wh[:], yn, 128), (r4(h, 3), T.wl[:], yn, 128), (r4(h, 3), T.nib[:], T.rr[:, hs], 128)], ["wh", "wl", "nib", ynk, K("rr")], pk(h, 3), name="UU")
-                V(128, tt(T.pi[:, hs], rf, r4(h, 3), ALU.mult), [rfk] + pk(h, 3), [K("pi")])
-            else:
-                V(128, cp(T.ui[:, hs], r4(h, 3)), pk(h, 3), [K("ui")])
-                V(128, ts(T.um[:, hs], T.ui[:, hs], W - 1, None, ALU.bitwise_and), [K("ui")], [K("um")])
-                V(128, tt(T.pi[:, hs], T.um[:, hs], RP, ALU.mult), [K("um")] + pk(pb, 0), [K("pi")])
+            MM([(r4(X, 0), T.ib[:], T.cb[:, hs], 128), (r4(X, 0), T.ib[:], T.fp[:, 2 * h * Q:(2 * h + 1) * Q], 128), (r4(X, 0), T.nib[:], T.fp[:, (2 * h + 1) * Q:(2 * h + 2) * Q], 128)],
+               ["ib", "nib", K("cb"), K("fp")], pk(X, 0), name="CU")
+            STEP(128, T.s2[:, hs], r4(X, 0), 196.5, pk(X, 0), [K("s2")], up=False)
+            MM([(r4(X, 2), T.l2[:], T.s2[:, hs], 128)], ["l2", K("s2")], pk(X, 2), name="L2")
+            V(128, ts(T.gam[:, hs], r4(X, 2), BIG16, BIG16 + 16.0, ALU.add, ALU.is_equal), pk(X, 2), [K("gam")])
+            MM([(UU, T.wh[:], yn, 128), (UU, T.wl[:], yn, 128)], ["wh", "wl", ynk], pk(ub, ur_), name="U")
+            LIN(128, T.ur[:, hs], UU, pk(ub, ur_) + ["wf7"], [K("ur")], bias=wc(7))
+            MM([(UU, T.kd[:], T.onesb[:, 0:Q], 128), (UU, T.wh[:], yn, 128), (UU, T.wl[:], yn, 128), (UU, T.nib[:], T.ur[:, hs], 128)],
+               ["kd", "onesb", "wh", "wl", "nib", ynk, K("ur")], pk(ub, ur_), name="UU")
+            V(128, tt(T.pi[:, hs], rf, UU, ALU.mult), [rfk] + pk(ub, ur_), [K("pi")])
             V(128, ts(T.qi[:, hs], T.pi[:, hs], 5, None, ALU.logical_shift_right), [K("pi")], [K("qi")])
-            V(128, tt(T.si[:, hs], T.qi[:, hs], R37, ALU.add), [K("qi")] + pk(pb, 1), [K("si")])
+            V(128, tt(T.si[:, hs], T.qi[:, hs], R37, ALU.add), [K("qi")] + pk(Z, 0), [K("si")])
             V(128, ts(T.fi[:, hs], T.si[:, hs], W - 1, None, ALU.bitwise_and), [K("si")], [K("fi")])
-            V(128, tt(R37, T.fi[:, hs], NC, ALU.subtract), [K("fi")] + pk(pb, 2), pk(pb, 1), name="E")
-            V(128, tt(T.g1[:, hs], T.gam[:, hs], NMR, ALU.mult), [K("gam")] + pk(pb, 3), [K("g1")])
-            V(128, tt(RP, T.g1[:, hs], RP, ALU.add), [K("g1")] + pk(pb, 0), pk(pb, 0), name="BASE")
-            V(128, lambda g, h=h, hs=hs: g.vector.tensor_tensor_scan(T.us2[:, hs], T.rmax[:], ps[4][:, (2 + h) * Q:(3 + h) * Q], 0.0, ALU.add, ALU.max),
-              ["rmax"] + pk(4, 2 + h), [K("us2")])
+            c2t = OPT["c2t"][h]
+            if c2t:
+                V(128, tt(T.ee[:, hs], T.fi[:, hs], NC, ALU.subtract), [K("fi")] + pk(Z, 9), [K("ee")], name="E")
+            else:
+                V(128, tt(R37, T.fi[:, hs], NC, ALU.subtract), [K("fi")] + pk(Z, 1), pk(Z, 0), name="E")
+            V(128, tt(NMR, T.gam[:, hs], NMR, ALU.mult), [K("gam")] + pk(Z, 2), pk(Z, 2), name="g1")
+            V(128, tt(NMR, rf, NMR, ALU.add), [rfk] + pk(Z, 2), pk(Z, 2), name="BASE")
+            if OPT["usc"]:
+                V(128, lambda g, hs=hs, UU=UU: g.vector.tensor_tensor_scan(T.us2[:, hs], T.rsel[:], UU, 0.0, ALU.add, ALU.max), ["rsel"] + pk(ub, ur_), [K("us2")])
             if h == 1:
-                V(16, cp(T.smi[:, 0:16], T.us2[:, 15:P:16]), [("us2", 0), ("us2", 1)], ["sl1"])
+                if OPT["usc"]:
+                    V(16, cp(T.smi[:, 0:16], T.us2[:, 15:P:16]), [("us2", 0), ("us2", 1)], ["sl1"])
+                else:
+                    MM([(B[:, Q:Q + 16], T.zw[:, 15 - r:143 - r], T.ynew[:, t * P + r:(t + 1) * P:16], 64) for r in range(16)], ["zw", ("yn", t, 0), ynk], pk(X, 1), name="U2")
+                    V(16, cp(T.smi[:, 0:16], B[:, Q:Q + 16]), pk(X, 1), ["sl1"])
                 V(16, ts(T.smi[:, 16:32], T.smi[:, 0:16], 15, None, ALU.bitwise_and), ["sl1"], ["sl2"])
                 V(32, tt(T.sm[:, 16:32], T.smi[:, 16:32], T.basel[:], ALU.add), ["sl2", "basel"], ["sl3"])
                 V(16, cp(T.soff[:], T.sm[:, 16:32]), ["sl3"], ["soff"])
-            late = []
-            zo = ZORD[FZS[h]]
-            for q in zo:
+            for q in range(4):
                 b = 2 + zb[0] % 2
                 zb[0] += 1
                 qs = slice(q * 512, (q + 1) * 512)
-                mms = []
-                for kk in range(4):
-                    mms.append((r4(b, kk), T.iz[:], zg[:, 4 * q + kk:16 * Q:16], 128))
-                    mms.append((r4(b, kk), T.n3i[:], yn, 128))
-                def zfn(g, mms=mms):
-                    x = None
-                    for i, (o_, l_, r_, c_) in enumerate(mms):
-                        x = g.tensor.matmul(o_, l_, r_, i % 2 == 0, i % 2 == 1)
-                    return x
-                add([("T", 0.03 + 8 * (128 * PEC + PEO), zfn)], ZG + ["iz", "n3i", ynk], pk(b, 0, 4), [b], grp=(True, True), name="ZD")
-                if q < 4 - FZS[h]:
+                c, e = q // 2, q % 2
+                qs = slice(e * 1024 + c * 512, e * 1024 + (c + 1) * 512)
+                MM([(ps[b][:], T.iz[:], zg[:, c * 1024 + e:(c + 1) * 1024:2], 512)]
+                   + [(ps[b][:, kk:512:8], T.n3i[:], T.ynew[:, o + 64 * c:o + 64 * c + 64], 64) for kk in range(8)],
+                   ZG[c * n2 // 2:(c + 1) * n2 // 2] + ["iz", "n3i", ynk], pk(b, 0, 4), name="ZD")
+                if q not in OPT["fzs"][h]:
                     V(512, ts(fz[:, qs], ps[b][:, 0:512], BIG16 - 576.0, BIG16, ALU.add, ALU.not_equal), pk(b, 0, 4), [("fz", h, q)], name="FZ")
                 else:
-                    S(512, act(ad[:, qs], ps[b][:, 0:512], ACT.Abs, bias=-576.0), pk(b, 0, 4), [("ad", h, q)], name="FZa")
-                    S(512, act(fz[:, qs], ad[:, qs], ACT.Sign, bias=-7.5), [("ad", h, q)], [("fz", h, q)], name="FZb")
-                mm = [(r4(5, 2 + h), sel(4 * q + kk), fz[:, q * 512 + kk * Q:q * 512 + (kk + 1) * Q], 128) for kk in range(4)]
-                late.append((mm, q))
-            late.sort(key=lambda x: x[1])
-            for i, (mm, q) in enumerate(late):
-                if i == 3:
-                    mm = [(r4(5, 2 + h), T.i32[:], T.sw[:, hs], 128)] + mm
-                MM(mm, ["wsel", "i32", ("fz", h, q)] + ([K("sw")] if i == 3 else []), pk(5, 2 + h), first=i == 0, last=i == 3, name="CNT2")
-            if BES[h]:
-                S(128, act(T.sw[:, hs], r4(5, 2 + h), ACT.Sign, bias=T.cf[:, 14 + h:15 + h]), pk(5, 2 + h) + [K("nthr")], [K("sw")], name="bs")
-                S(128, act(T.bet[:, hs], T.sw[:, hs], ACT.Relu), [K("sw")], [K("bet")])
+                    aq = ad[:, q * 512:(q + 1) * 512]
+                    S(512, act(aq, ps[b][:, 0:512], ACT.Abs, bias=-576.0), pk(b, 0, 4), [("ad", h, q)], name="FZa")
+                    STEP(512, fz[:, qs], aq, 7.5, [("ad", h, q)], [("fz", h, q)], name="FZb", half=True)
+            fzk = lambda k: fz[:, (k % 2) * 1024 + k // 2:(k % 2 + 1) * 1024:8]
+            MM([(r4(Y, 3), T.s2[:, hs], T.i16[:], 128), (r4(Y, 3), T.gam[:, hs], T.i16[:], 128)],
+               ["i16", K("s2"), K("gam")], pk(Y, 3), last=False, name="CNT2")
+            for e in range(2):
+                MM([(ps[Y][:, 3 * Q + k:4 * Q:16], fzk(k), T.bo8[:], 64) for k in range(e, 16, 2)],
+                   ["bo8", ("fz", h, e), ("fz", h, e + 2)], pk(Y, 3), first=False, last=e == 1, name="CNT2")
+            STEP(128, T.bet[:, hs], r4(Y, 3), 36.5, pk(Y, 3), [K("bet")])
+            if c2t:
+                MM([(r4(Y, 0), T.bet[:, hs], T.ib[:], 128)], [K("bet"), "ib"], pk(Y, 0), name="BT")
+                V(128, tt(T.t2[:, hs], T.ee[:, hs], r4(Y, 0), ALU.mult), [K("ee")] + pk(Y, 0), [K("t2")])
             else:
-                V(128, ts(T.bet[:, hs], r4(5, 2 + h), T.cf[:, 12 + h:13 + h], None, ALU.is_gt), pk(5, 2 + h) + [K("thr")], [K("bet")])
-            V(128, tt(T.t2[:, hs], T.bet[:, hs], R37, ALU.mult), [K("bet")] + pk(pb, 1), [K("t2")])
+                V(128, tt(T.t2[:, hs], T.bet[:, hs], R37, ALU.mult), [K("bet")] + pk(Z, 0), [K("t2")])
             nw, nwk = T.nw[:, ts_], ("nw", t, h)
-            V(128, tt(nw, T.t2[:, hs], RP, ALU.add), [K("t2")] + pk(pb, 0), [nwk], name="new")
+            V(128, tt(nw, T.t2[:, hs], NMR, ALU.add), [K("t2")] + pk(Z, 2), [nwk], name="new")
             if t < NV - 1:
                 V(128, cp(T.rnew[:, ts_], nw), [nwk], [("rn", t, h)])
                 DMA("G", rem(T.roff[:, o + P:o + P + Q], T.rnew[:, ts_], "ar%d%d" % (t + 1, h)), [("rn", t, h)], [("r", t + 1, h)], "ar%d%d" % (t + 1, h), rem(None, None, None), 3.0)
-                if SENDF:
-                    DMA("G", rem(T.rf[:, o + P:o + P + Q], nw, "af%d%d" % (t + 1, h)), [nwk, ("rn", t, h)], [("rf", t + 1, h)], "af%d%d" % (t + 1, h), rem(None, None, None), 3.5)
+                DMA("G", rem(T.rf[:, o + P:o + P + Q], nw, "af%d%d" % (t + 1, h)), [nwk, ("rn", t, h)], [("rf", t + 1, h)], "af%d%d" % (t + 1, h), rem(None, None, None), 3.5)
             else:
                 DMA("Y", lambda g, hs=hs, nw=nw: g.sync.dma_start(T.yj[:, hs], nw), [nwk], [K("yj")], "oj%d" % h, 16, 2.0)
+        parts = [half(0), half(1)]
+        for part in parts + parts:
+            next(part, None)
         for h in range(2):
             hs = slice(h * Q, (h + 1) * Q)
             nw = T.nw[:, t * P + h * Q:t * P + (h + 1) * Q]
             V(128 * SC, (lambda g, h=h, hs=hs, nw=nw: g.vector.tensor_tensor(T.tab[:, h * 2048:(h + 1) * 2048].indirect(T.soff[:, 8 * h:8 * h + 8]), nw, T.y4[:, hs], ALU.add)),
               ["soff", ("nw", t, h), ("y4", h)], [("tab", h)], name="SCAT%d" % h)
         if t < NV - 1:
-            MM([(ps[5][:, Q:Q + 1], T.o16[:], T.acc[:, 2 * t:2 * t + 1], 256), (ps[5][:, Q:Q + 1], T.o16[:], T.acc[:, 2 * t + 1:2 * t + 2], 256)],
-               ["o16", ("acc", t, 0), ("acc", t, 1)], pk(5, 1))
-            V(1, cp(T.smi[:, 40:41], ps[5][:, Q:Q + 1]), pk(5, 1), ["tot1"])
-            V(1, ts(T.smi[:, 41:42], T.smi[:, 40:41], 2, None, ALU.bitwise_and), ["tot1"], ["tot2"])
-            V(1, ts(T.biasa[:, t + 1:t + 2], T.smi[:, 41:42], -1.0, 7.0, ALU.mult, ALU.add), ["tot2"], [("bias", t + 1)])
+            tot = ps[5][:, Q:Q + 1]
+            MM([(tot, T.sel0[:], T.acc[:, 2 * t:2 * t + 1], 256), (tot, T.sel0[:], T.acc[:, 2 * t + 1:2 * t + 2], 256)], ["sel0", ("acc", t, 0), ("acc", t, 1)], pk(5, 1), name="TOT")
+            V(1, cp(T.smi[:, 40:41], tot), pk(5, 1), ["tot1"])
+            V(1, ts(T.smi[:, 41:42], T.smi[:, 40:41], 1, None, ALU.bitwise_and), ["tot1"], ["tot2"])
+            V(1, ts(T.biasa[:, t + 1:t + 2], T.smi[:, 41:42], 256.0, T.biasa[:, 0:1], ALU.mult, ALU.add), ["tot2", ("bias", 0)], [("bias", t + 1)])
 
     ctx["h"] = "Z"
     for c in range(8):
         cs = slice(c * 512, (c + 1) * 512)
-        VS(512, ts(T.xb[:, cs], T.tab[:, cs], OFF - 2047.5, None, ALU.add), act(T.xb[:, cs], T.tab[:, cs], ACT.Identity, bias=OFF - 2047.5),
-           [("tab", c // 4)], [("xb", c)], name="XR")
+        LIN(512, T.xb[:, cs], T.tab[:, cs], [("tab", c // 4)], [("xb", c)], bias=OFF - 2047.5, name="XR")
     for c in range(8):
         mm = [(ps[2][:, 0:P], T.onesb[0:1, 0:Q], T.yc[0:1, :], 256)] if c == 0 else []
         for e in range(4 * c, 4 * c + 4):
@@ -495,7 +489,7 @@ def build(T, rem):
     return ops
 
 
-def schedule(ops, tune):
+def graph(ops):
     n = len(ops)
     deps = [set() for _ in range(n)]
     lastw, readers = {}, {}
@@ -520,6 +514,13 @@ def schedule(ops, tune):
     pr = [0.0] * n
     for i in range(n - 1, -1, -1):
         pr[i] = min(a[1] for a in ops[i]["alts"]) + ops[i]["lat"] + HOP + max([pr[j] for j in succ[i]] + [0.0])
+    return deps, succ, pr
+
+
+def schedule(ops, gr, tune):
+    n = len(ops)
+    deps = [set(x) for x in gr[0]]
+    succ, pr = gr[1], list(gr[2])
     left = [len(x) for x in deps]
     ready = [i for i in range(n) if left[i] == 0]
     free = {e: 0.0 for e in "VSTGY"}
@@ -528,8 +529,8 @@ def schedule(ops, tune):
     opened = [None] * 8
     order = []
     rdy = [None] * n
-    pen = [tune.get("e" + o["tag"], 1.0) for o in ops]
-    slack = tune.get("slack", 0.1)
+    pen = [tune.get("e" + o["tag"], 0.0) for o in ops]
+    slack = tune.get("slack", 0.05)
     for i in range(n):
         pr[i] += tune.get(ops[i]["tag"], 0.0)
         if ops[i]["sem"] is not None and not deps[i]:
@@ -550,7 +551,7 @@ def schedule(ops, tune):
                     for e2, j in bank[b].items():
                         if e2 != e and fin[j] + HOP > s:
                             s = fin[j] + HOP
-                if best is None or s + c < best[0] + best[1] + pen[i]:
+                if best is None or s + c < best[0] + best[1] + pen[i] + 1.0:
                     best = (s, c, a, e)
             cand.append((best[0], i, best))
         c0 = min(cand)
@@ -579,10 +580,9 @@ def schedule(ops, tune):
     return order, eng, deps, start, fin
 
 
-TUNE = {'eG1A0':1,'eG1A1':1,'eG1A2':0,'eG1A3':0,'rnB0':4.5,'rB0':15.5,'slack':0.05,'eG1B0':2,'eG1B1':2,'eG1B2':0.6,'eG1B3':0.6,'eG2A0':0.3,'eG2A1':0.3,'eG2A2':2,'eG2A3':2,'eG2B0':0,'eG2B1':2,'eG2B2':2,'eG2B3':2,'TRB0':4,'SUBA1':-35.5,'eemA0':2,'U2B0':4.5,'ynewA0':-24.5,'DD3A1':10.5,'edr2A0':0,'G1A1':-22,'ttA0':13,'cbB0':3,'ekyB0':9,'YZZ5':-0.5,'NTB0':-15.5,'us2A0':13,'UA0':33,'umA0':-15,'eXRZ7':0,'EB0':6.5,'flA0':6,'yjA0':3,'rrB0':14,'ZDB3':-10.5,'deB0':2,'edr2B0':0,'eemB0':2,'eXRZ0':9,'CNTA1':0.5,'eXRZ5':0.3,'FZB1':11,'BBA2':10.5,'mB0':19,'SUBA3':15.5,'R37A0':-26.5,'yzoZ1':-26,'CNT2B3':-25.5,'eXRZ1':2,'yzZ1':-20.5,'DD3A0':-1.5,'ecbA0':9,'nfA0':-3,'rfB1':-4.5,'YZZ1':6,'rnA0':-2.5,'XRZ3':-14.5,'NMRA0':3,'SUBB0':8,'yztZ0':12,'g1B0':6,'piA0':-2.5,'YZZ4':-7,'rrA0':-1,'toffA0':11,'NTA1':-2,'gamA0':8,'SUBA0':-9,'yoB0':5.5,'FZA0':-15,'eqA0':11.5,'biasB0':-22,'FARB0':13.5,'rfA1':-19.5,'CNT2A2':16,'yA0':-16.5,'YZZ7':-19,'RHOA0':10,'FZA3':-0.5,'slB0':-14,'CNTA2':-0.5,'TRA1':8.5,'y4B0':3.5,'DELB0':1.5,'ksA0':26,'G1A0':14,'SCAT0B0':-10.5,'saB0':39.5,'eXRZ4':0,'FZbB1':-1.5,'YZZ2':-22.5,'TRA0':6.5,'psB5':-6.5,'qiB0':9.5,'SUBB1':13,'saA0':9.5,'FZA1':7.5,'swA0':16.5,'EMA0':13.5,'DRA1':4.5,'eXRZ6':1,'CNTA3':12.5,'siA0':24,'t2B0':-15.5,'newB0':2.5,'deA0':13,'ABSB0':-3,'ybcB0':-1.5,'kyB0':1.5,'XRZ6':-4,'betA0':22.5,'U2A0':-2,'eXRZ3':9,'kyA0':1.5,'TRB1':-0.5,'siB0':-32,'fpB0':36.5,'eqB0':10.5,'CNT2B2':2.5,'ksB0':8.5,'SCAT1B0':-3,'tot1B0':-11,'G2A1':-1.5,'G2A0':13,'FZaB0':1.5,'ekyA0':2,'ABSB1':17,'FZB0':32.5,'R37B0':-9,'G1B0':2,'sl1B0':1,'NTA2':15,'flB0':-24.5,'eXRZ2':0,'rscanA0':6.5,'EA0':-14,'SUBA2':2.5,'ybcA0':-30.5,'FZbB0':11.5,'ynewB0':1.5,'y4A0':1.5,'noffA0':2,'G2B1':4.5,'mA0':11,'soffB0':13.5,'ecbB0':9,'yzZ0':-1,'tot2B0':-12.5,'yjB0':8.5,'FZaB1':-20,'EMB0':3.5,'sl3B0':1.5,'fiB0':3,'CNT2B1':-1,'FARA0':8.5,'yB0':13,'psZ1':-23.5,'rscanB0':-6.5,'nfB0':-14,'fiA0':-3.5,'dr2B0':-6.5,'piB0':2.5,'rfA0':3,'yoA0':14,'psB4':-6,'NTA0':-22,'noffB0':13.5,'SUBB3':11,'BASEA0':-2,'umB0':13,'ZDA2':2,'YZZ0':-2,'newA0':2,'uiA0':-43,'psZ0':-13.5,'RPA0':-12,'gamB0':-0.5,'g1A0':-13,'DR3B1':24,'swB0':4.5,'CNTB0':3.5,'XRZ7':-11.5,'CNT2A1':9.5,'t2A0':17.5,'SUBB2':21,'DD3B0':0.5,'NTB2':0.5,'BBA3':-4,'BBA0':19.5,'yzoZ0':9.5,'sl2B0':14,'XRZ2':2,'psB0':16.5,'cbA0':2,'XRZ0':-0.5,'BASEB0':-13.5,'emB0':-17.5,'qiA0':7,'psA0':5,'YZZ3':-7,'G2B0':6.5,'s2A0':-6.5,'NTA3':1.5,'uiB0':-3,'us2B0':6.5,'rfB0':-6,'RPB0':-1.5,'BBB2':3.5,'XRZ5':-17.5,'FARA1':7,'CNTB1':9,'NMRB0':1,'toffB0':-10,'KEYB1':-0.5,'XRZ4':-1,'G1B1':10,'fpA0':17.5,'BBA1':6.5,'ZDB2':-0.5,'psB3':9,'s2B0':1.5,'ABSA1':-1,'DR3A1':2,'psA2':-1.5,'rA0':6,'DRB1':15.5,'dr2A0':-1,'FARB1':8,'NCB0':-0.5,'DELA0':5.5,'emA0':3,'DD3B1':2,'ttB0':-2.5,'KEYB0':2,'NTB3':-0.5,'KEYA0':5,'DR3B0':0.5,'CNT2B0':-4.5,'ZDB1':1.5,'psA1':7.5,'KEYA1':8,'RHOB0':30.5,'CNT2A3':-0.5,'betB0':10,'psB2':-1,'psA4':-0.5,'BBB0':8,'UB0':0.5}
+TUNE = {}
 ROUNDS = 0
 SPREAD = [(1, 1, 1, 1, HOP), (1, 1, 0.8, 1, HOP), (1, 1, 1, 1, 2 * HOP), (1, 1, 1, 0.7, HOP), (1, 1, 1, 1.3, HOP)]
-PLAN = []
 BEST = []
 
 
@@ -601,21 +601,21 @@ def length(ops, order, eng, deps, fv, fs, ft, fg, hop):
     return max(fin)
 
 
-def search(ops, rounds, seed=0):
+def search(ops, gr, rounds, seed=0, tune=None):
     rng = np.random.RandomState(seed)
     tags = sorted(set(o["tag"] for o in ops if o["tag"][-2] in "ABZ"))
     flex = sorted(set("e" + o["tag"] for o in ops if len(o["alts"]) > 1))
 
     def score(tune):
-        order, eng, deps, start, fin = schedule(ops, tune)
+        order, eng, deps, start, fin = schedule(ops, gr, tune)
         return sum(length(ops, order, eng, deps, *p) for p in SPREAD) / len(SPREAD)
-    tune = dict(TUNE)
+    tune = dict(TUNE if tune is None else tune)
     best = score(tune)
     for _ in range(rounds):
         t2 = dict(tune)
         for _m in range(int(rng.choice([1, 1, 2, 3]))):
-            if rng.rand() < 0.2:
-                t2[flex[rng.randint(len(flex))]] = float(rng.choice([0, 0.3, 0.6, 1, 2, 9]))
+            if rng.rand() < 0.3:
+                t2[flex[rng.randint(len(flex))]] = float(rng.choice([-3, -1, -0.7, -0.4, 0, 1, 8]))
             else:
                 k = tags[rng.randint(len(tags))]
                 t2[k] = t2.get(k, 0.0) + float(rng.choice([-8, -4, -2, -1, -0.5, 0.5, 1, 2, 4, 8]))
@@ -625,12 +625,68 @@ def search(ops, rounds, seed=0):
     return tune
 
 
+ORDER = "KEYB1 TRB1 ttA0 RHOB0 nfB0* DD3A1 R37A0* G2A2 YNA0 usB0 ynewA0* toffB0 NCB0 fpA0 ZDA1 dr2B0 ksB0 G2A3 noffB0 kmB0* CUA0 ZDA0 UA0 eqB0 FZA1 DRB0 EMB0 s2A0* L2A0 FZA0 DRB1 urA0 emB0 deB0 UUA0 ZDA2 us2A0 NMRA0 G2B1 DELB0 ZDA3 gamA0 piA0 ttB0 yA0 G2B0 FZA2 FZA3 CNT2A0 DR3B0 DD3B0 qiA0 DD3B1 DR3B1 YNB0 ynewB0* yB0 CNT2A1 CNT2A2 G2B3 siA0 g1A0 ZDB0 G2B2 fpB0 CUB0 betA0* UB0 FZaB0 fiA0 BASEA0 BTA0 yoB0 EA0 s2B0* y4A0 urB0 ZDB1 L2B0 t2A0 ZDB2 FZaB1 NMRB0 newA0 gamB0 UUB0 rnA0 g1B0 ZDB3 FZB0 piB0 us2B0 qiB0 FZB1 FZbB0 FZbB1 CNT2B0 R37B0 sl1B0 rA0 CNT2B1 CNT2B2 betB0 ybcA0+ siB0 sl2B0 fiB0 BTB0 sl3B0 EB0 BASEB0 t2B0 soffB0 ybcB0+ y4B0 TOTB0 newB0 rnB0 SCAT0B0 XRZ0* SCAT1B0 tot1B0 ybcB1+ G1A3+ ybcA1+ G1A1+* G1A2+ G1A0+* rB0 NTA0+ tot2B0 SUBA0+ SUBA2+ NTA1+ G1B2+ SUBA1+ NTA2+ SUBA3+ NTA3+ FARA0+ G1B1+ G1B0+ FARA1+ CNTA0+ XRZ1 biasB0 YZZ0 SUBB0+ rrA0+ G1B3+ SUBB1+ CNTA1+ CNTA2+ ABSA1+ SUBB2+ CNTA3+ NTB0+ cbA0+ FARB0+ SUBB3+ flA0+ XRZ2 nfA0+* disA0+ NTB1+ ABSA0+ NTB2+ FARB1+ XRZ3* MA0+ CNTB0+ TRA1+ KEYA0+ mA0+ YZZ1 KEYA1+ CNTB1+ ABSB0+ ABSB1+ RHOA0+ CNTB2+ TRA0+ YZZ2 CNTB3+ ksA0+ TRB0+ kmA0+* usA0+ eqA0+ NCA0+ toffA0+ disB0+ flB0+ NTB3+ cbB0+ EMA0+ rfB0 dr2A0+ rrB0+ MB0+ emA0+ DRA0+ mB0+ noffA0+ DR3A0+ G2A1+ DRA1+ G2A0+* DR3A1+ deA0+ KEYB0+ DD3A0+ DELA0+ rfA0 XRZ4* yoA0 XRZ6* yjB0 YZZ3 YZZ4 XRZ5 YZZ5 YZZ6 XRZ7 YZZ7 yztZ0 psZ1 yzoZ1 psZ0 yzZ1 yjA0 yzoZ0 yzZ0"
+
+
+def arrange(ops, gr):
+    names = ORDER.split()
+    bare = [x.rstrip("+-*") for x in names]
+    period = max(n for n, x in enumerate(bare) if x[-2] != "Z" and x[:2] not in ("yo", "yj")) + 1
+    place = {b: n + period * (("-" in x) - ("+" in x)) for n, (b, x) in enumerate(zip(bare, names))}
+    onv = set(b for b, x in zip(bare, names) if "*" in x)
+    n = len(ops)
+    deps, succ, pr = [set(x) for x in gr[0]], gr[1], list(gr[2])
+    for i, o in enumerate(ops):
+        o["pick"] = 0 if len(o["alts"]) == 1 or o["tag"] in onv else 1
+        if not deps[i]:
+            pr[i] = 1e4 - i
+    line = sorted((i for i in range(n) if ops[i]["t"] >= 0), key=lambda i: ops[i]["t"] * period + place[ops[i]["tag"]])
+    left = [len(x) for x in deps]
+    ready = [i for i in range(n) if ops[i]["t"] < 0 and left[i] == 0]
+    free = {e: 0.0 for e in "VSTGY"}
+    fin, eng, start = [0.0] * n, [None] * n, [0.0] * n
+    bank = [dict() for _ in range(8)]
+    opened = [False] * 8
+    order, at = [], 0
+
+    def begin(i):
+        o = ops[i]
+        e = o["alts"][o["pick"]][0]
+        late = [fin[j] + HOP for j in deps[i] if not (e == "T" and eng[j] == "T")]
+        late += [fin[j] + HOP for b in o["banks"] for e2, j in bank[b].items() if e2 != e]
+        return max(late + [free[e]]), e
+    while len(order) < n:
+        cand = [(begin(i), i) for i in ready if not (ops[i]["grp"] and any(opened[b] for b in ops[i]["banks"]))]
+        if at < len(line) and left[line[at]] == 0:
+            cand.append((begin(line[at]), line[at]))
+        (s0, e0), _ = min(cand)
+        (s, e), i = max((c for c in cand if c[0][1] == e0 and c[0][0] <= s0 + 0.05), key=lambda c: (ops[c[1]]["t"] >= 0, pr[c[1]]))
+        o = ops[i]
+        eng[i], start[i] = e, s
+        free[e] = s + o["alts"][o["pick"]][1]
+        fin[i] = free[e] + o["lat"]
+        for b in o["banks"]:
+            deps[i].update(j for e2, j in bank[b].items() if e2 != e)
+            bank[b][e] = i
+            if o["grp"] is not None:
+                opened[b] = not o["grp"][1]
+        order.append(i)
+        if o["t"] >= 0:
+            at += 1
+        else:
+            ready.remove(i)
+        for j in succ[i]:
+            left[j] -= 1
+            if left[j] == 0 and ops[j]["t"] < 0:
+                ready.append(j)
+    return order, eng, deps, start, fin
+
+
 def rank_program(g, core, T, topo):
     rank = T.rank_of(core)
     if rank is None:
         return
     nxt = T.cores[(rank + 1) % len(T.cores)]
-    prv = T.cores[(rank - 1) % len(T.cores)]
     rid, pid, _se = topo.addr(nxt)
     ne = min(len(topo.engines(a, b)) for a, b in zip(T.cores, list(T.cores[1:]) + [T.cores[0]]))
     mask = sum(1 << e for e in topo.engines(core, nxt)[:ne])
@@ -646,10 +702,8 @@ def rank_program(g, core, T, topo):
         return fn
 
     ops = build(T, rem)
-    if not BEST:
-        BEST.append(search(ops, ROUNDS))
-    order, eng, deps, start, fin = schedule(ops, BEST[0])
-    PLAN[:] = [ops, order, eng, start, fin]
+    gr = graph(ops)
+    order, eng, deps, start, fin = arrange(ops, gr) if ORDER else schedule(ops, gr, {})
     qs = {"V": g.vector, "S": g.scalar, "T": g.tensor, "G": g, "Y": g.sync}
     needed = set()
     for i in order:

import numpy as np
from concourse.mybir import AluOpType, ActivationFunctionType

ALU = AluOpType
ACT = ActivationFunctionType
NV, W, P, Q = 5, 4096, 256, 128
OFF = 192.0 * 4096.0
BIG16 = 1.5 * 2.0 ** 27
BIGU = 1.5 * 2.0 ** 35
FB = 1.5 * 2.0 ** 37
LCH = 8
OPT = {"g1": [4, 4], "g2": [4, 4], "fzs": [[], [0, 1]], "nch": [2, 2], "sp": [True, True], "c2t": [True, True], "rsc": [True, True], "uy": True, "usc": True}

SCRATCH = {
    "tab": ("sbuf", [128, W], "float32"), "lst": ("sbuf", [128, W], "int32"), "xb": ("sbuf", [128, W], "bfloat16"),
    "jin": ("sbuf", [128, P], "int32"), "wi": ("sbuf", [128, 8], "int32"), "wj": ("sbuf", [128, 8], "int32"), "wf": ("sbuf", [128, 16], "float32"),
    "ybuf": ("sbuf", [128, NV * P], "bfloat16"), "ynew": ("sbuf", [128, NV * P], "bfloat16"),
    "roff": ("sbuf", [128, NV * P], "uint16"), "rnew": ("sbuf", [128, NV * P], "uint16"),
    "rf": ("sbuf", [128, NV * P], "float32"), "nw": ("sbuf", [128, NV * P], "float32"),
    "noff": ("sbuf", [128, P], "uint16"), "soff": ("sbuf", [128, 16], "uint16"), "bcoff": ("sbuf", [128, 8], "uint16"), "toff": ("sbuf", [128, 16], "uint16"),
    "acc": ("sbuf", [128, 16], "float32"), "biasa": ("sbuf", [128, 8], "float32"), "basel": ("sbuf", [128, 16], "float32"),
    "km": ("sbuf", [128, 16], "float32"), "sm": ("sbuf", [128, 64], "float32"), "smi": ("sbuf", [128, 64], "int32"),
    "yzt": ("sbuf", [128, P], "float32"), "yzo": ("sbuf", [128, P], "float32"),
    "ci": ("sbuf", [128, 16], "int32"), "cf": ("sbuf", [128, 24], "float32"),
    "bo8": ("sbuf", [128, 8], "bfloat16"), "wj32": ("sbuf", [128, 8], "float32"), "nwj": ("sbuf", [128, 8], "bfloat16"), "crow": ("sbuf", [128, 8], "bfloat16"),
    "wsel": ("sbuf", [128, 144], "bfloat16"), "onesb": ("sbuf", [128, 512], "bfloat16"), "yc": ("sbuf", [128, P], "bfloat16"),
    "fp": ("sbuf", [128, 2 * P], "bfloat16"), "cbs": ("sbuf", [128, 16 * Q], "bfloat16"),
}
for _h in range(2):
    SCRATCH["pg%d" % _h] = ("sbuf", [128, 16 * Q], "float32")
    for _n in ("d", "ad", "far", "zg", "fz"):
        SCRATCH["%s%d" % (_n, _h)] = ("sbuf", [128, 16 * Q], "bfloat16")
    SCRATCH["dm%d" % _h] = ("sbuf", [128, 32 * Q], "bfloat16")
    for _n in ("zi", "zd", "zt", "zq"):
        SCRATCH["%s%d" % (_n, _h)] = ("sbuf", [128, 160], "bfloat16")
for _n in ("cb", "m", "em", "dr", "dr2", "rr", "dT", "tt", "s2", "gam", "bet", "ur", "dsg", "fl"):
    SCRATCH[_n] = ("sbuf", [128, P], "bfloat16")
for _n in ("io160", "pm160", "cg160"):
    SCRATCH[_n] = ("sbuf", [128, 160], "float32")
SCRATCH["zr"] = ("sbuf", [128, 160], "bfloat16")
SCRATCH["zw"] = ("sbuf", [128, 144], "bfloat16")
for _n in ("nf", "ks", "us", "us2", "y4", "ee", "t2", "lo"):
    SCRATCH[_n] = ("sbuf", [128, P], "float32")
for _n in ("pi", "qi", "si", "fi"):
    SCRATCH[_n] = ("sbuf", [128, P], "int32")
for _n in ("ib", "nib", "i4096", "iz", "ih", "n3bo", "n3i", "ikey", "i16", "bo", "l2", "tri", "mq", "e16", "wh", "wl", "kd", "zero", "ntri"):
    SCRATCH[_n] = ("sbuf", [128, 128], "bfloat16")
for _n in ("pmc", "cg", "cm", "iff", "sel0", "rsel", "rmin", "tmp1", "tmp2", "tmp3"):
    SCRATCH[_n] = ("sbuf", [128, 128], "float32")
for _b in range(8):
    SCRATCH["ps%d" % _b] = ("psum", [128, 512], "float32")

SEMAPHORES = (["sV", "sS", "sT", "sG", "sent", "ldw", "ldj", "ldy", "ldx0", "ldx1", "oj0", "oj1", "oy0", "oy1", "oz0", "oz1"]
              + ["ldl%d" % i for i in range(LCH)]
              + ["ar%d%d" % (t, h) for t in range(1, NV) for h in range(2)]
              + ["af%d%d" % (t, h) for t in range(1, NV) for h in range(2)]
              + ["ay%d%d" % (t, h) for t in range(1, NV) for h in range(2)])

CYC = 0.00083 * 1.25
GC, SC = 1.55, 3.8
PEC = 0.00042 * 1.25
PEO = 0.005
HOP = 0.10


def build(T, rem):
    ops = []
    ctx = {"h": "I", "n": {}, "t": -1}

    def add(alts, r, w, banks=(), grp=None, sem=None, lat=0.0, name=""):
        w = list(w)
        base = (name or str(w[0][0] if isinstance(w[0], tuple) else w[0])) + ctx["h"]
        ctx["n"][base] = ctx["n"].get(base, -1) + 1
        ops.append({"t": ctx["t"], "tag": "%s%d" % (base, ctx["n"][base]), "alts": alts, "r": list(r), "w": list(w), "banks": list(banks), "grp": grp, "sem": sem, "lat": lat, "name": name})

    def pk(b, a, n=1):
        return [("ps", b, a + i) for i in range(n)]

    def bk(keys):
        return sorted(set(k[1] for k in keys if isinstance(k, tuple) and k[0] == "ps"))

    def V(n, fn, r, w, name=""):
        add([("V", 0.06 + max(64, n) * CYC, fn)], r, w, bk(list(r) + list(w)), name=name)

    def S(n, fn, r, w, name=""):
        add([("S", 0.08 + max(64, n) * CYC, fn)], r, w, bk(list(r) + list(w)), name=name)

    def VS(n, fv, fs, r, w, name="", half=False):
        add([("V", 0.06 + n * CYC * (0.5 if half else 1.0), fv), ("S", 0.08 + n * CYC, fs)], r, w, bk(list(r) + list(w)), name=name)

    def G(n, fn, r, w):
        add([("G", 0.17 + 2 * n * CYC, fn)], r, w)

    def MM(mms, r, w, first=True, last=True, each=False, name="", pause=False):
        def fn(g):
            x = None
            for i, (o, l, rr, c) in enumerate(mms):
                x = g.tensor.matmul(o, l, rr, bool(each or (first and i == 0)), bool(each or ((last or pause) and i == len(mms) - 1)))
            return x
        add([("T", 0.03 + sum(m[3] * PEC + PEO for m in mms), fn)], r, w, bk(w), grp=(first, last), name=name)

    def DMA(q, fn, r, w, sem, val, lat):
        add([(q, 0.1, fn)], r, w, sem=(sem, val), lat=lat)

    def ts(o, i, a, b=None, op0=None, op1=None):
        if op1 is None:
            return lambda g: g.vector.tensor_scalar(o, i, a, None, op0)
        return lambda g: g.vector.tensor_scalar(o, i, a, b, op0, op1)

    def tt(o, a, b, op):
        return lambda g: g.vector.tensor_tensor(o, a, b, op)

    def cp(o, i):
        return lambda g: g.vector.tensor_copy(o, i)

    def act(o, i, f, bias=0.0, scale=1.0, acc=None):
        if acc is None:
            return lambda g: g.scalar.activation(o, i, f, bias=bias, scale=scale)
        return lambda g: g.scalar.activation(o, i, f, bias=bias, scale=scale, accum_out=acc)

    def LIN(n, o, i, r, w, scale=1.0, bias=0.0, name=""):
        VS(n, ts(o, i, scale, bias, ALU.mult, ALU.add), act(o, i, ACT.Identity, bias=bias, scale=scale), r, w, name=name)

    def STEP(n, o, i, thr, r, w, up=True, name="", half=False):
        s = 256.0 if up else -256.0
        VS(n, ts(o, i, thr, None, ALU.is_gt if up else ALU.is_lt), act(o, i, ACT.Sigmoid, bias=-s * thr, scale=s), r, w, name=name, half=half)

    ps = [T["ps%d" % b] for b in range(8)]

    cw = W // LCH
    DMA("S", lambda g: g.scalar.dma_start(T.jin[:], T.jur[:]), [], ["jin"], "ldj", 16, 3.0)
    DMA("Y", lambda g: g.sync.dma_start(T.ybuf[:, 0:P], T.own[:]), [], [("y", 0, 0), ("y", 0, 1)], "ldy", 16, 3.0)
    DMA("Y", lambda g: g.sync.dma_start(T.xb[:, 0:W // 2], T.xc[:, 0:W // 2]), [], [("xb", c) for c in range(0, 4)], "ldx0", 16, 4.0)
    DMA("S", lambda g: g.scalar.dma_start(T.xb[:, W // 2:W], T.xc[:, W // 2:W]), [], [("xb", c) for c in range(4, 8)], "ldx1", 16, 5.5)
    for c in range(LCH):
        if c % 2 == 0:
            DMA("Y", lambda g, c=c: g.sync.dma_start(T.lst[:, c * cw:(c + 1) * cw], T.lsr[:, c * cw:(c + 1) * cw]), [], [("lst", c)], "ldl%d" % c, 16, 6.0 + 0.8 * c)
        else:
            DMA("S", lambda g, c=c: g.scalar.dma_start(T.lst[:, c * cw:(c + 1) * cw], T.lsr[:, c * cw:(c + 1) * cw]), [], [("lst", c)], "ldl%d" % c, 16, 6.0 + 0.8 * c)
    DMA("G", lambda g: g.dma_start(T.wi[:, 0:1], T.wgt[:], allow_slow_non_contiguous=True), [], ["wi"], "ldw", 16, 5.0)

    def iota(o, pat, base, cmul, key, n, flt=True):
        if flt:
            G(n, lambda g: g.iota(o, pat, base, cmul, allow_small_or_imprecise_dtypes=True), [], [key])
        else:
            G(n, lambda g: g.iota(o, pat, base, cmul), [], [key])

    def lin(n, o, i, sc, r, w, bias=0.0):
        S(n, act(o, i, ACT.Identity, bias=bias, scale=sc), r, w)

    iota(T.pmc[:], [[1, 128]], 0, -1, "pmc", 128)
    iota(T.ci[:, 0:1], [[0, 1]], 0, 1, "ci0", 1, False)
    iota(T.cg[:], [[16, 8], [0, 16]], 0, 0, "cg", 128)
    iota(T.cm[:], [[0, 8], [1, 16]], 0, 0, "cm", 128)
    iota(T.io160[:], [[1, 160]], -30, 0, "io160", 160)
    iota(T.pm160[:], [[1, 160]], -16, -1, "pm160", 160)
    iota(T.cg160[:], [[16, 10], [0, 16]], -16, 0, "cg160", 160)
    iota(T.e16[:], [[16, 128]], 0, 0, "e16", 128)
    iota(T.ci[:, 8:16], [[1, 8]], 0, 0, "ci8", 8, False)
    V(128, ts(T.iff[:], T.pmc[:], 0.0, None, ALU.is_equal), ["pmc"], ["iff"])
    for nm, sc in (("i4096", 4096.0), ("ib", 1.0), ("nib", -1.0), ("iz", 3.0 / 4096), ("n3i", -3.0), ("ikey", -256.0), ("i16", 16.0), ("ih", 1.0 / 64), ("zero", 0.0)):
        S(128, act(T[nm][:], T.iff[:], ACT.Copy, scale=sc), ["iff"], [nm])
    for c, mk in ((1, 0x70), (2, 15), (4, 0x60)):
        V(1, ts(T.ci[:, c:c + 1], T.ci[:, 0:1], mk, None, ALU.bitwise_and), ["ci0"], [("ci", c)])
    V(1, ts(T.ci[:, 3:4], T.ci[:, 0:1], 4, 1, ALU.logical_shift_right, ALU.bitwise_and), ["ci0"], [("ci", 3)])
    V(4, cp(T.cf[:, 1:5], T.ci[:, 1:5]), [("ci", c) for c in range(1, 5)], ["cf"])
    pg16, pm, odd, pair = (T.cf[:, c:c + 1] for c in range(1, 5))
    col = lambda c: T.cf[:, c:c + 1]
    lin(1, col(5), pm, 1.0, ["cf"], ["cf5"], bias=1.0)
    lin(1, col(6), odd, -1.0, ["cf"], ["cf6"], bias=1.0)
    lin(1, col(7), odd, 1.0, ["cf"], ["cf6"])
    lin(1, col(8), pm, 37.0, ["cf"], ["cf8"])
    V(1, ts(col(10), pm, 0.0, None, ALU.is_equal), ["cf"], ["cf10"])
    V(1, ts(col(11), col(10), 2048.0, pm, ALU.mult, ALU.add), ["cf", "cf10"], ["cf11"])
    V(1, ts(col(13), pm, 0.5, None, ALU.is_gt), ["cf"], ["cf13"])
    V(2, ts(T.cf[:, 14:16], T.cf[:, 6:8], col(13), None, ALU.mult), ["cf6", "cf13"], ["cf14"])
    lin(1, T.biasa[:, 0:1], col(10), 2048.0, ["cf10"], [("bias", 0)], bias=-2944.0)
    V(1, ts(col(17), pg16, -15.0, None, ALU.add), ["cf"], ["cf17"])
    V(2, ts(T.cf[:, 18:20], T.cf[:, 6:8], col(11), None, ALU.mult), ["cf6", "cf11"], ["cf18"])
    V(1, ts(col(20), pm, 14.5, -8192.0, ALU.is_lt, ALU.mult), ["cf"], ["cf20"])
    V(128, ts(T.bo[:], T.cg[:], pg16, None, ALU.is_equal), ["cg", "cf"], ["bo"])
    lin(128, T.n3bo[:], T.bo[:], -3.0, ["bo"], ["n3bo"])
    lin(8, T.bo8[:], T.bo[:, 0:128:16], 1.0, ["bo"], ["bo8"])
    lin(8, T.wj32[:], T.bo8[:], col(5), ["bo8", "cf5"], ["wj32"])
    lin(8, T.nwj[:], T.wj32[:], -1.0, ["wj32"], ["nwj"])
    V(144, ts(T.wsel[:], T.io160[:, 0:144], col(17), None, ALU.is_equal), ["io160", "cf17"], ["wsel"])
    if not all(OPT["rsc"]):
        lin(1, col(9), pm, 16.0, ["cf"], ["cf9"])
        V(1, ts(col(12), pair, odd, None, ALU.add), ["cf"], ["cf12"])
        lin(8, T.crow[:], T.cg[:, 0:128:16], 16.0, ["cg"], ["crow"])
        V(160, ts(T.zr[:], T.io160[:], col(12), col(11), ALU.is_equal, ALU.mult), ["io160", "cf11", "cf12"], ["zr"])
    lin(128, T.l2[:], T.bo[:], 2.0, ["bo"], ["l2"])
    G(128, lambda g: g.affine_select(T.l2[:], T.l2[:], [[-1, 128]], ALU.not_equal, -12.0, 0, 1), ["l2"], ["l2"])
    V(256, lambda g: g.vector.memset(T.onesb[:], 1.0), [], ["onesb"])
    lin(128, T.sel0[:], T.onesb[:, 0:128], col(10), ["onesb", "cf10"], ["sel0"])
    lin(256, T.yc[:], T.onesb[:, 0:P], 136.0 * OFF, ["onesb"], ["yc"])
    S(128, act(T.tmp1[:], T.pmc[:], ACT.Sigmoid, bias=-128.0, scale=256.0), ["pmc"], ["tmp1"])
    V(128, ts(T.tmp1[:], T.tmp1[:], 0.5, None, ALU.is_gt), ["tmp1"], ["tmp1"])
    V(256, tt(T.tmp1[:], T.iff[:], T.tmp1[:], ALU.subtract), ["tmp1", "iff"], ["tmp1"])
    V(256, tt(T.tmp1[:], T.tmp1[:], T.bo[:], ALU.mult), ["tmp1", "bo"], ["tmp1"])
    V(128, ts(T.tmp2[:], T.cm[:], 0.5, 16.0, ALU.is_gt, ALU.mult), ["cm"], ["tmp2"])
    V(256, tt(T.tri[:], T.tmp1[:], T.tmp2[:], ALU.mult), ["tmp1", "tmp2"], ["tri"])
    lin(128, T.ntri[:], T.tri[:], -1.0, ["tri"], ["ntri"])
    V(128, ts(T.tmp3[:], T.cm[:], 0.0, None, ALU.is_equal), ["cm"], ["tmp3"])
    V(256, tt(T.tmp2[:], T.iff[:], T.bo[:], ALU.subtract), ["iff", "bo"], ["tmp2"])
    V(256, tt(T.tmp2[:], T.tmp2[:], T.tmp3[:], ALU.mult), ["tmp2", "tmp3"], ["tmp2"])
    V(256, tt(T.mq[:], T.tmp2[:], T.iff[:], ALU.add), ["tmp2", "iff"], ["mq"])
    for e in range(2):
        V(160, ts(T["zi%d" % e][:], T.pm160[:], 0.0, col(6 + e), ALU.is_equal, ALU.mult), ["pm160", "cf6"], ["zi%d" % e])
        V(160, ts(T["zd%d" % e][:], T.pm160[:], -1.0, col(14 + e), ALU.is_equal, ALU.mult), ["pm160", "cf14"], ["zd%d" % e])
        V(320, tt(T["zd%d" % e][:], T["zi%d" % e][:], T["zd%d" % e][:], ALU.subtract), ["zi%d" % e, "zd%d" % e], ["zd%d" % e])
        V(160, ts(T["zq%d" % e][:], T.cg160[:], pg16, col(18 + e), ALU.is_equal, ALU.mult), ["cg160", "cf", "cf18"], ["zq%d" % e])
        lin(160, T["zt%d" % e][:], T["zi%d" % e][:], 3.0, ["zi%d" % e], ["zt%d" % e])
        V(8, ts(T.basel[:, 8 * e:8 * e + 8], T.cg[:, 0:128:16], pm, 16.0, ALU.add, ALU.mult), ["cg", "cf"], ["basel"])
    V(128, ts(T.rsel[:], T.cm[:], pm, -65536.0, ALU.is_equal, ALU.mult), ["cm", "cf"], ["rsel"])
    V(128, ts(T.tmp1[:], T.cm[:], col(5), 8192.0, ALU.is_equal, ALU.mult), ["cm", "cf5"], ["tmp1"])
    V(256, tt(T.rsel[:], T.rsel[:], T.tmp1[:], ALU.add), ["rsel", "tmp1"], ["rsel"])
    lin(128, T.rmin[:], T.tmp3[:], 4096.0, ["tmp3"], ["rmin"])
    V(8, cp(T.bcoff[:], T.ci[:, 8:16]), ["ci8"], ["bcoff"])
    wc = lambda c: T.wf[:, c:c + 1]
    V(1, ts(T.wj[:, 0:1], T.wi[:, 0:1], 2048.0, None, ALU.add), ["wi"], [("wj", 0)])
    for c, src, mk in ((1, T.wj, 0xFC0), (2, T.wi, 63), (3, T.wi, 15)):
        V(1, ts(T.wj[:, c:c + 1], src[:, 0:1], mk, None, ALU.bitwise_and), ["wi", ("wj", 0)], [("wj", c)])
    V(3, cp(T.wf[:, 1:4], T.wj[:, 1:4]), [("wj", 1), ("wj", 2), ("wj", 3)], ["wf"])
    V(1, ts(wc(1), wc(1), -2048.0, None, ALU.add), ["wf"], ["wf"])
    if not OPT["usc"]:
        lin(144, T.zw[:], T.wsel[:], wc(3), ["wsel", "wf"], ["zw"])
    for c, nm in ((1, "wh"), (2, "wl")):
        lin(128, T[nm][:], T.bo[:], wc(c), ["bo", "wf"], [nm])
    MM([(ps[7][:, Q:Q + 1], T.wh[:], T.onesb[:, 0:1], 64), (ps[7][:, Q:Q + 1], T.wl[:], T.onesb[:, 0:1], 64)], ["wh", "wl", "onesb"], pk(7, 1))
    V(1, ts(wc(4), ps[7][:, Q:Q + 1], 7.5, BIGU, ALU.mult, ALU.add), pk(7, 1), ["wf4"])
    V(1, ts(wc(5), wc(4), BIGU, -1.0, ALU.subtract, ALU.mult), ["wf4"], ["wf5"])
    lin(1, wc(6), wc(5), 1.0, ["wf5"], ["wf6"], bias=OFF)
    lin(1, wc(7), wc(5), 1.0, ["wf5"], ["wf7"], bias=OFF - 2047.5)
    lin(128, T.kd[:], T.ib[:], wc(6), ["ib", "wf6"], ["kd"])
    V(256, cp(T.roff[:, 0:P], T.jin[:]), ["jin"], [("r", 0, 0), ("r", 0, 1)])
    V(256, cp(T.rf[:, 0:P], T.jin[:]), ["jin"], [("rf", 0, 0), ("rf", 0, 1)])

    for e in range(2):
        iota(T["dm%d" % e][:, 0:2048], [[0, 2048]], int(OFF), 0, ("dmc", e), 2048)
    sel = lambda k: T.wsel[:, 15 - k:143 - k]
    r4 = lambda b, i: ps[b][:, i * Q:(i + 1) * Q]
    for q in range(4):
        for kk in range(4):
            MM([(r4(4 + q % 2, kk), T.ib[:], sel(4 * q + kk), 128), (r4(4 + q % 2, kk), T.ib[:], T.ih[:], 128)], ["ib", "ih", "wsel"], pk(4 + q % 2, kk))
        lin(512, T.cbs[:, q * 512:(q + 1) * 512], ps[4 + q % 2][:], 1.0, pk(4 + q % 2, 0, 4), ["cbs"])

    for c in range(8):
        b = 2 + c % 2
        cs = slice(c * 512, (c + 1) * 512)
        MM([(ps[b][:, 0:512], T.i4096[:], T.xb[:, cs], 512)], ["i4096", ("xb", c)], pk(b, 0, 4))
        V(512, tt(T.tab[:, cs], T.lst[:, cs], ps[b][:, 0:512], ALU.add), [("lst", c * 512 // cw)] + pk(b, 0, 4), [("tabc", c)])
    TAB = [("tab", 0), ("tab", 1)]
    zb = [0]

    for t in range(NV):
        TABR = TAB + ([("tabc", c) for c in range(8)] if t == 0 else [])
        ctx["n"], ctx["t"] = {}, t
        def half(h):
            ctx["h"] = "AB"[h]
            hs = slice(h * Q, (h + 1) * Q)
            o = t * P + h * Q
            ts_ = slice(o, o + Q)
            pg, d, ad, far, dm, zg, fz = (T["%s%d" % (n, h)] for n in ("pg", "d", "ad", "far", "dm", "zg", "fz"))
            K = lambda n, h=h: (n, h)
            X, Y, Z = h, 4 + h, 6 + h
            B = ps[X]
            y, yk = T.ybuf[:, ts_], ("y", t, h)
            rf, rfk = T.rf[:, ts_], ("rf", t, h)
            R37, NC, NMR, UU = (r4(Z, i) for i in range(4))
            n1, n2 = OPT["g1"][h], OPT["g2"][h]
            PG = [("pg", h, c) for c in range(n1)]
            ZG = [("zg", h, c) for c in range(n2)]
            pw = Q // n1
            for c in range(n1):
                offs = T.roff[:, o + c * pw:o + (c + 1) * pw]
                out = pg[:, c * pw * 16:(c + 1) * pw * 16]
                VS(16 * pw * GC, (lambda g, out=out, offs=offs: g.vector.tensor_scalar(out, T.tab[:, 0:W].indirect(offs), OFF - 2047.5, None, ALU.add)),
                   (lambda g, out=out, offs=offs: g.scalar.activation(out, T.tab[:, 0:W].indirect(offs), ACT.Identity, bias=OFF - 2047.5)),
                   TABR + [("r", t, h)], [("pg", h, c)], name="G1")
            ub, ur_ = (Y, 1) if OPT["uy"] else (Z, 3)
            UU = r4(ub, ur_)
            LIN(128, R37, rf, [rfk, "cf8"], pk(Z, 0), bias=col(8), name="R37")
            sp = OPT["sp"][h]
            if sp:
                for c, b in enumerate((X, 2 + h)):
                    MM([(ps[b][:, kk:512:8], T.i4096[:], T.ybuf[:, o + 64 * c:o + 64 * c + 64], 64) for kk in range(8)], ["i4096", yk], pk(b, 0, 4), each=True, name="ybc")
            else:
                MM([(B[:, kk:512:4], T.i4096[:], y, 128) for kk in range(4)], ["i4096", yk], pk(X, 0, 4), each=True, name="ybc")
            for q in range(4):
                MM([(ps[Z][:, Q + k:2 * Q:16], pg[:, k:16 * Q:16], T.iff[:, (k + t) % 16:128:16], 256) for k in range(4 * q, 4 * q + 4)],
                   PG + ["iff"], pk(Z, 1) + pk(Z, 9), each=True, name="NT")
            LIN(128, T.nf[:, hs], NC, pk(Z, 1), [K("nf")], bias=2047.5)
            LIN(128, T.rr[:, hs], NC, pk(Z, 1), [K("rr")])
            MM([(NC, T.nf[:, hs], T.iff[:], 512), (NC, T.rr[:, hs], T.nib[:], 128)], [K("nf"), K("rr"), "iff", "nib"], pk(Z, 1) + pk(Z, 9), name="NC")
            V(128, cp(T.noff[:, hs], NC), pk(Z, 1), [K("noff")])
            V(128, tt(NMR, NC, rf, ALU.subtract), pk(Z, 1) + [rfk], pk(Z, 2), name="NMR")
            pw = Q // n2
            for c in range(n2):
                offs = T.noff[:, h * Q + c * pw:h * Q + (c + 1) * pw]
                out = zg[:, c * pw * 16:(c + 1) * pw * 16]
                VS(16 * pw * GC, (lambda g, out=out, offs=offs: g.vector.tensor_scalar(out, T.tab[:, 0:W].indirect(offs), OFF - 2047.5, None, ALU.add)),
                   (lambda g, out=out, offs=offs: g.scalar.activation(out, T.tab[:, 0:W].indirect(offs), ACT.Identity, bias=OFF - 2047.5)),
                   TABR + [K("noff")], [("zg", h, c)], name="G2")
            for q in range(4):
                if sp:
                    c, b = q // 2, (X, 2 + h)[q // 2]
                    qs = slice(c * 1024 + q % 2, (c + 1) * 1024, 2)
                    V(512, tt(d[:, qs], pg[:, qs], ps[b][:], ALU.subtract), PG[c * n1 // 2:(c + 1) * n1 // 2] + pk(b, 0, 4), [("d", h, q)], name="SUB")
                else:
                    V(512, tt(d[:, q:16 * Q:4], pg[:, q:16 * Q:4], B[:, 0:512], ALU.subtract), PG + pk(X, 0, 4), [("d", h, q)], name="SUB")
            yield
            ctx["h"] = "AB"[h]
            DA = [("d", h, q) for q in range(4)]
            AD = [("ad", h, q) for q in range(4)]
            nch = OPT["nch"][h]
            cl = 2048 // nch
            for c in range(nch):
                cs = slice(c * cl, (c + 1) * cl)
                DD = DA[2 * c:2 * c + 2] if sp and nch == 2 else DA
                V(cl // 2, ts(far[:, cs], d[:, cs], FB - OFF, FB, ALU.add, ALU.not_equal), DD, [("far", h, c)], name="FAR")
                S(cl, act(ad[:, cs], d[:, cs], ACT.Abs, bias=-192.0, scale=1.0 / 4096), DD, AD[4 * c // nch:4 * (c + 1) // nch], name="ABS")
                V(cl // 2, (lambda g, c=c, cs=cs, d=d, dm=dm, cl=cl: g.vector.transpose(dm[:, 2048 + c * cl:2048 + (c + 1) * cl], d[:, cs])), DD, [("dm", h, c)], name="TR")
            wd = Q // nch
            for c in range(nch):
                for q in range(2):
                    mm = [(r4(Y, 0), T.zero[0:1, :], T.onesb[0:1, 0:Q], 128)] if nch > 1 and c == 0 and q == 0 else []
                    MM(mm + [(ps[Y][:, wd * c:wd * (c + 1)], T.cbs[:, k * Q:(k + 1) * Q], far[:, c * cl + k:(c + 1) * cl:16], wd) for k in range(8 * q, 8 * q + 8)],
                       ["cbs", "zero", "onesb", ("far", h, c)], pk(Y, 0), first=c == 0 and q == 0, last=c == nch - 1 and q == 1, name="CNT")
            dis, fl = T.dsg[:, hs], T.fl[:, hs]
            S(128, act(dis, r4(Y, 0), ACT.Sign, bias=-4.5), pk(Y, 0), [K("dis")])
            LIN(128, T.cb[:, hs], r4(Y, 0), pk(Y, 0), [K("cb")], bias=191.875)
            LIN(128, fl, r4(Y, 0), pk(Y, 0), [K("fl")], bias=192.5 - 8.5 / 64)
            MM([(r4(X, 0), T.bo[:], dis, 128), (r4(X, 0), T.tri[:], fl, 128), (r4(X, 0), T.ntri[:], T.cb[:, hs], 128)],
               ["bo", "tri", "ntri", K("dis"), K("fl"), K("cb")], pk(X, 0), name="M")
            S(128, act(T.m[:, hs], r4(X, 0), ACT.Sigmoid, bias=T.biasa[:, t:t + 1], scale=128.0, acc=T.acc[:, 2 * t + h:2 * t + h + 1]),
              pk(X, 0) + [("bias", t)], [K("m"), ("acc", t, h)])
            kcol = lambda k: ps[Y][:, 2 * Q + k:3 * Q:16]
            MM([(r4(Y, 2), dis, T.ikey[:], 128)] + [(kcol(k), ad[:, k:16 * Q:16], T.bo8[:], 64) for k in range(8)],
               ["ikey", "bo8", K("dis")] + AD, pk(Y, 2), last=False, name="KEY")
            MM([(kcol(k), ad[:, k:16 * Q:16], T.bo8[:], 64) for k in range(8, 16)], ["bo8"] + AD, pk(Y, 2), first=False, name="KEY")
            V(128, lambda g, hs=hs, Y=Y: g.vector.tensor_tensor_scan(T.ks[:, hs], T.rmin[:], r4(Y, 2), 0.0, ALU.add, ALU.min), ["rmin"] + pk(Y, 2), [K("ks")])
            VS(64, cp(T.km[:, 8 * h:8 * h + 8], T.ks[:, h * Q + 15:(h + 1) * Q:16]), act(T.km[:, 8 * h:8 * h + 8], T.ks[:, h * Q + 15:(h + 1) * Q:16], ACT.Copy), [K("ks")], [K("km")])
            V(128 * GC, lambda g, hs=hs: g.vector.tensor_tensor(T.dT[:, hs], T.km[:, 8 * h:8 * h + 8].indirect(T.bcoff[:, 0:8]), T.ks[:, hs], ALU.is_equal),
              [K("ks"), K("km"), "bcoff"], [K("dT")], name="eq")
            MM([(r4(Y, 2), T.dT[:, hs], T.ib[:], 128)], [K("dT"), "ib"], pk(Y, 2), name="EM")
            LIN(128, T.em[:, hs], r4(Y, 2), pk(Y, 2), [K("em")])
            if OPT["rsc"][h]:
                mm = [(r4(X, 2), T.onesb[0:1, 0:Q], T.e16[0:1, :], 128)]
                for g0 in range(2):
                    for j0 in range(2):
                        sft = 16 * (1 - (j0 - g0))
                        mm.append((B[:, 2 * Q + g0:3 * Q:2], T["zq%d" % g0][:, sft:sft + 128], T.m[:, h * Q + j0:(h + 1) * Q:2], 64))
                MM(mm, ["onesb", "e16", "zq0", "zq1", K("m")], pk(X, 2), name="RHO")
                V(128, lambda g, hs=hs, X=X: g.vector.tensor_tensor_scan(T.us[:, hs], T.rsel[:], r4(X, 2), 0.0, ALU.add, ALU.max), ["rsel"] + pk(X, 2), [K("us")])
                V(8, ts(T.toff[:, 8 * h:8 * h + 8], T.us[:, h * Q + 15:(h + 1) * Q:16], col(20), None, ALU.add), [K("us"), "cf20"], [K("toff")])
            else:
                rho = B[:, 2 * Q:2 * Q + 8]
                mm = [(rho, T.onesb[0:1, 0:Q], T.crow[0:1, :], 64)]
                for i4 in range(16):
                    sft = 30 - 16 * (i4 % 2) - 2 * (i4 // 2)
                    mm.append((rho, T.zr[:, sft:sft + 128], T.m[:, h * Q + i4:(h + 1) * Q:16], 64))
                MM(mm, ["onesb", "crow", "zr", K("m")], pk(X, 2), name="RHO")
                V(8, ts(T.toff[:, 8 * h:8 * h + 8], rho, col(9), None, ALU.add), pk(X, 2) + ["cf9"], [K("toff")])
            VS(128 * GC, (lambda g, h=h, hs=hs, dm=dm: g.vector.tensor_scalar(T.dr2[:, hs], dm[:, 0:4096].indirect(T.toff[:, 8 * h:8 * h + 8]), 1.0 / 4096, -192.0, ALU.mult, ALU.add)),
               (lambda g, h=h, hs=hs, dm=dm: g.scalar.activation(T.dr2[:, hs], dm[:, 0:4096].indirect(T.toff[:, 8 * h:8 * h + 8]), ACT.Identity, bias=-192.0, scale=1.0 / 4096)),
               [K("toff"), K("dmc")] + [("dm", h, c) for c in range(nch)], [K("dr2")], name="dr2")
            back = lambda nm, reg, j0: [(B[:, reg * Q + j0:(reg + 1) * Q:2], T["%s%d" % (nm, j0)][:, 16 * (1 - (g0 - j0)):16 * (1 - (g0 - j0)) + 128],
                                         T.dr2[:, h * Q + g0:(h + 1) * Q:2], 64) for g0 in range(2)]
            for j0 in range(2):
                MM(back("zd", 3, j0), ["zd0", "zd1", K("dr2")], pk(X, 3), name="DR")
            V(128, tt(T.dr[:, hs], r4(X, 3), T.em[:, hs], ALU.mult), pk(X, 3) + [K("em")], [K("dr")], name="de")
            MM([(r4(X, 0), T.bo[:], T.dr[:, hs], 128)], [K("dr"), "bo"], pk(X, 0), name="DEL")
            for j0 in range(2):
                MM(back("zt", 2, j0), ["zt0", "zt1", K("dr2")], pk(X, 2), name="DR3")
            for j0 in range(2):
                MM(back("zt", 1, j0) + [(B[:, Q + j0:2 * Q:2], T.n3bo[:], T.dr[:, h * Q + j0:(h + 1) * Q:2], 64)], ["zt0", "zt1", "n3bo", K("dr2"), K("dr")], pk(X, 1), name="DD3")
            V(128, tt(T.tt[:, hs], r4(X, 0), T.m[:, hs], ALU.mult), pk(X, 0) + [K("m")], [K("tt")])
            V(256, ts(T.fp[:, 2 * h * Q:2 * (h + 1) * Q], B[:, Q:3 * Q], BIG16, BIG16, ALU.add, ALU.not_equal), pk(X, 1, 2), [K("fp")])
            yn, ynk = T.ynew[:, ts_], ("yn", t, h)
            MM([(r4(X, 3), T.ib[:], y, 128), (r4(X, 3), T.mq[:], T.tt[:, hs], 128)], ["ib", "mq", yk, K("tt")], pk(X, 3), name="YN")
            LIN(128, yn, r4(X, 3), pk(X, 3), [ynk], name="ynew")
            LIN(128, T.y4[:, hs], yn, [ynk], [K("y4")], scale=4096.0)
            if t < NV - 1:
                DMA("G", rem(T.ybuf[:, o + P:o + P + Q], yn, "ay%d%d" % (t + 1, h)), [ynk], [("y", t + 1, h)], "ay%d%d" % (t + 1, h), rem(None, None, None), 3.0)
            else:
                DMA("Y", lambda g, yn=yn, hs=hs: g.sync.dma_start(T.yo[:, hs], yn), [ynk], [K("yo")], "oy%d" % h, 16, 2.0)
            MM([(r4(X, 0), T.ib[:], T.cb[:, hs], 128), (r4(X, 0), T.ib[:], T.fp[:, 2 * h * Q:(2 * h + 1) * Q], 128), (r4(X, 0), T.nib[:], T.fp[:, (2 * h + 1) * Q:(2 * h + 2) * Q], 128)],
               ["ib", "nib", K("cb"), K("fp")], pk(X, 0), name="CU")
            STEP(128, T.s2[:, hs], r4(X, 0), 196.5, pk(X, 0), [K("s2")], up=False)
            MM([(r4(X, 2), T.l2[:], T.s2[:, hs], 128)], ["l2", K("s2")], pk(X, 2), name="L2")
            V(128, ts(T.gam[:, hs], r4(X, 2), BIG16, BIG16 + 16.0, ALU.add, ALU.is_equal), pk(X, 2), [K("gam")])
            MM([(UU, T.wh[:], yn, 128), (UU, T.wl[:], yn, 128)], ["wh", "wl", ynk], pk(ub, ur_), name="U")
            LIN(128, T.ur[:, hs], UU, pk(ub, ur_) + ["wf7"], [K("ur")], bias=wc(7))
            MM([(UU, T.kd[:], T.onesb[:, 0:Q], 128), (UU, T.wh[:], yn, 128), (UU, T.wl[:], yn, 128), (UU, T.nib[:], T.ur[:, hs], 128)],
               ["kd", "onesb", "wh", "wl", "nib", ynk, K("ur")], pk(ub, ur_), name="UU")
            V(128, tt(T.pi[:, hs], rf, UU, ALU.mult), [rfk] + pk(ub, ur_), [K("pi")])
            V(128, ts(T.qi[:, hs], T.pi[:, hs], 5, None, ALU.logical_shift_right), [K("pi")], [K("qi")])
            V(128, tt(T.si[:, hs], T.qi[:, hs], R37, ALU.add), [K("qi")] + pk(Z, 0), [K("si")])
            V(128, ts(T.fi[:, hs], T.si[:, hs], W - 1, None, ALU.bitwise_and), [K("si")], [K("fi")])
            c2t = OPT["c2t"][h]
            if c2t:
                V(128, tt(T.ee[:, hs], T.fi[:, hs], NC, ALU.subtract), [K("fi")] + pk(Z, 9), [K("ee")], name="E")
            else:
                V(128, tt(R37, T.fi[:, hs], NC, ALU.subtract), [K("fi")] + pk(Z, 1), pk(Z, 0), name="E")
            V(128, tt(NMR, T.gam[:, hs], NMR, ALU.mult), [K("gam")] + pk(Z, 2), pk(Z, 2), name="g1")
            V(128, tt(NMR, rf, NMR, ALU.add), [rfk] + pk(Z, 2), pk(Z, 2), name="BASE")
            if OPT["usc"]:
                V(128, lambda g, hs=hs, UU=UU: g.vector.tensor_tensor_scan(T.us2[:, hs], T.rsel[:], UU, 0.0, ALU.add, ALU.max), ["rsel"] + pk(ub, ur_), [K("us2")])
            if h == 1:
                if OPT["usc"]:
                    V(16, cp(T.smi[:, 0:16], T.us2[:, 15:P:16]), [("us2", 0), ("us2", 1)], ["sl1"])
                else:
                    MM([(B[:, Q:Q + 16], T.zw[:, 15 - r:143 - r], T.ynew[:, t * P + r:(t + 1) * P:16], 64) for r in range(16)], ["zw", ("yn", t, 0), ynk], pk(X, 1), name="U2")
                    V(16, cp(T.smi[:, 0:16], B[:, Q:Q + 16]), pk(X, 1), ["sl1"])
                V(16, ts(T.smi[:, 16:32], T.smi[:, 0:16], 15, None, ALU.bitwise_and), ["sl1"], ["sl2"])
                V(32, tt(T.sm[:, 16:32], T.smi[:, 16:32], T.basel[:], ALU.add), ["sl2", "basel"], ["sl3"])
                V(16, cp(T.soff[:], T.sm[:, 16:32]), ["sl3"], ["soff"])
            for q in range(4):
                b = 2 + zb[0] % 2
                zb[0] += 1
                qs = slice(q * 512, (q + 1) * 512)
                c, e = q // 2, q % 2
                qs = slice(e * 1024 + c * 512, e * 1024 + (c + 1) * 512)
                MM([(ps[b][:], T.iz[:], zg[:, c * 1024 + e:(c + 1) * 1024:2], 512)]
                   + [(ps[b][:, kk:512:8], T.n3i[:], T.ynew[:, o + 64 * c:o + 64 * c + 64], 64) for kk in range(8)],
                   ZG[c * n2 // 2:(c + 1) * n2 // 2] + ["iz", "n3i", ynk], pk(b, 0, 4), name="ZD")
                if q not in OPT["fzs"][h]:
                    V(512, ts(fz[:, qs], ps[b][:, 0:512], BIG16 - 576.0, BIG16, ALU.add, ALU.not_equal), pk(b, 0, 4), [("fz", h, q)], name="FZ")
                else:
                    aq = ad[:, q * 512:(q + 1) * 512]
                    S(512, act(aq, ps[b][:, 0:512], ACT.Abs, bias=-576.0), pk(b, 0, 4), [("ad", h, q)], name="FZa")
                    STEP(512, fz[:, qs], aq, 7.5, [("ad", h, q)], [("fz", h, q)], name="FZb", half=True)
            fzk = lambda k: fz[:, (k % 2) * 1024 + k // 2:(k % 2 + 1) * 1024:8]
            MM([(r4(Y, 3), T.s2[:, hs], T.i16[:], 128), (r4(Y, 3), T.gam[:, hs], T.i16[:], 128)],
               ["i16", K("s2"), K("gam")], pk(Y, 3), last=False, name="CNT2")
            for e in range(2):
                MM([(ps[Y][:, 3 * Q + k:4 * Q:16], fzk(k), T.bo8[:], 64) for k in range(e, 16, 2)],
                   ["bo8", ("fz", h, e), ("fz", h, e + 2)], pk(Y, 3), first=False, last=e == 1, name="CNT2")
            STEP(128, T.bet[:, hs], r4(Y, 3), 36.5, pk(Y, 3), [K("bet")])
            if c2t:
                MM([(r4(Y, 0), T.bet[:, hs], T.ib[:], 128)], [K("bet"), "ib"], pk(Y, 0), name="BT")
                V(128, tt(T.t2[:, hs], T.ee[:, hs], r4(Y, 0), ALU.mult), [K("ee")] + pk(Y, 0), [K("t2")])
            else:
                V(128, tt(T.t2[:, hs], T.bet[:, hs], R37, ALU.mult), [K("bet")] + pk(Z, 0), [K("t2")])
            nw, nwk = T.nw[:, ts_], ("nw", t, h)
            V(128, tt(nw, T.t2[:, hs], NMR, ALU.add), [K("t2")] + pk(Z, 2), [nwk], name="new")
            if t < NV - 1:
                V(128, cp(T.rnew[:, ts_], nw), [nwk], [("rn", t, h)])
                DMA("G", rem(T.roff[:, o + P:o + P + Q], T.rnew[:, ts_], "ar%d%d" % (t + 1, h)), [("rn", t, h)], [("r", t + 1, h)], "ar%d%d" % (t + 1, h), rem(None, None, None), 3.0)
                DMA("G", rem(T.rf[:, o + P:o + P + Q], nw, "af%d%d" % (t + 1, h)), [nwk, ("rn", t, h)], [("rf", t + 1, h)], "af%d%d" % (t + 1, h), rem(None, None, None), 3.5)
            else:
                DMA("Y", lambda g, hs=hs, nw=nw: g.sync.dma_start(T.yj[:, hs], nw), [nwk], [K("yj")], "oj%d" % h, 16, 2.0)
        parts = [half(0), half(1)]
        for part in parts + parts:
            next(part, None)
        for h in range(2):
            hs = slice(h * Q, (h + 1) * Q)
            nw = T.nw[:, t * P + h * Q:t * P + (h + 1) * Q]
            V(128 * SC, (lambda g, h=h, hs=hs, nw=nw: g.vector.tensor_tensor(T.tab[:, h * 2048:(h + 1) * 2048].indirect(T.soff[:, 8 * h:8 * h + 8]), nw, T.y4[:, hs], ALU.add)),
              ["soff", ("nw", t, h), ("y4", h)], [("tab", h)], name="SCAT%d" % h)
        if t < NV - 1:
            tot = ps[5][:, Q:Q + 1]
            MM([(tot, T.sel0[:], T.acc[:, 2 * t:2 * t + 1], 256), (tot, T.sel0[:], T.acc[:, 2 * t + 1:2 * t + 2], 256)], ["sel0", ("acc", t, 0), ("acc", t, 1)], pk(5, 1), name="TOT")
            V(1, cp(T.smi[:, 40:41], tot), pk(5, 1), ["tot1"])
            V(1, ts(T.smi[:, 41:42], T.smi[:, 40:41], 1, None, ALU.bitwise_and), ["tot1"], ["tot2"])
            V(1, ts(T.biasa[:, t + 1:t + 2], T.smi[:, 41:42], 256.0, T.biasa[:, 0:1], ALU.mult, ALU.add), ["tot2", ("bias", 0)], [("bias", t + 1)])

    ctx["h"] = "Z"
    for c in range(8):
        cs = slice(c * 512, (c + 1) * 512)
        LIN(512, T.xb[:, cs], T.tab[:, cs], [("tab", c // 4)], [("xb", c)], bias=OFF - 2047.5, name="XR")
    for c in range(8):
        mm = [(ps[2][:, 0:P], T.onesb[0:1, 0:Q], T.yc[0:1, :], 256)] if c == 0 else []
        for e in range(4 * c, 4 * c + 4):
            mm.append((ps[2][:, e:P:32], T.xb[:, e * Q:(e + 1) * Q], T.nwj[:], 64))
            mm.append((ps[2][:, e:P:32], T.tab[:, e * Q:(e + 1) * Q], T.wj32[:], 256))
        MM(mm, ["onesb", "yc", "nwj", "wj32", ("xb", c), ("tab", c // 4)], pk(2, 0, 2), first=c == 0, last=c == 7, name="YZ")
    V(256, cp(T.yzt[:], ps[2][:, 0:P]), pk(2, 0, 2), ["yzt"])
    for h in range(2):
        hs = slice(h * Q, (h + 1) * Q)
        MM([(ps[h][:, 0:Q], T.yzt[:, hs], T.iff[:], 512)], ["yzt", "iff"], pk(h, 0))
        if h == 0:
            V(128, cp(T.yzo[:, hs], ps[h][:, 0:Q]), pk(h, 0), [("yzo", h)])
            DMA("Y", lambda g, hs=hs: g.sync.dma_start(T.yz[0:4, :], T.yzo[:, hs]), [("yzo", h)], [("yz", h)], "oz0", 16, 2.0)
        else:
            S(128, act(T.yzo[:, hs], ps[h][:, 0:Q], ACT.Copy), pk(h, 0), [("yzo", h)])
            DMA("S", lambda g, hs=hs: g.scalar.dma_start(T.yz[4:8, :], T.yzo[:, hs]), [("yzo", h)], [("yz", h)], "oz1", 16, 2.0)
    return ops


def graph(ops):
    n = len(ops)
    deps = [set() for _ in range(n)]
    lastw, readers = {}, {}
    for i, o in enumerate(ops):
        for k in o["r"]:
            if k in lastw:
                deps[i].add(lastw[k])
        for k in o["w"]:
            if k in lastw:
                deps[i].add(lastw[k])
            deps[i].update(readers.get(k, ()))
        for k in o["r"]:
            readers.setdefault(k, []).append(i)
        for k in o["w"]:
            lastw[k] = i
            readers[k] = []
        deps[i].discard(i)
    succ = [[] for _ in range(n)]
    for i in range(n):
        for j in deps[i]:
            succ[j].append(i)
    pr = [0.0] * n
    for i in range(n - 1, -1, -1):
        pr[i] = min(a[1] for a in ops[i]["alts"]) + ops[i]["lat"] + HOP + max([pr[j] for j in succ[i]] + [0.0])
    return deps, succ, pr


def schedule(ops, gr, tune):
    n = len(ops)
    deps = [set(x) for x in gr[0]]
    succ, pr = gr[1], list(gr[2])
    left = [len(x) for x in deps]
    ready = [i for i in range(n) if left[i] == 0]
    free = {e: 0.0 for e in "VSTGY"}
    fin, eng, start = [0.0] * n, [None] * n, [0.0] * n
    bank = [dict() for _ in range(8)]
    opened = [None] * 8
    order = []
    rdy = [None] * n
    pen = [tune.get("e" + o["tag"], 0.0) for o in ops]
    slack = tune.get("slack", 0.05)
    for i in range(n):
        pr[i] += tune.get(ops[i]["tag"], 0.0)
        if ops[i]["sem"] is not None and not deps[i]:
            pr[i] = 1e4 - i
    while ready:
        cand = []
        for i in ready:
            o = ops[i]
            if o["grp"] is not None and o["grp"][0] and any(opened[b] is not None for b in o["banks"]):
                continue
            if rdy[i] is None:
                pe = o["alts"][0][0] == "T"
                rdy[i] = max([fin[j] + HOP for j in deps[i] if not (pe and eng[j] == "T")] + [0.0])
            best = None
            for a, (e, c, f) in enumerate(o["alts"]):
                s = max(free[e], rdy[i])
                for b in o["banks"]:
                    for e2, j in bank[b].items():
                        if e2 != e and fin[j] + HOP > s:
                            s = fin[j] + HOP
                if best is None or s + c < best[0] + best[1] + pen[i] + 1.0:
                    best = (s, c, a, e)
            cand.append((best[0], i, best))
        c0 = min(cand)
        s0, e0 = c0[0], c0[2][3]
        near = [c for c in cand if c[2][3] == e0 and c[0] <= s0 + slack]
        s, i, best = max(near, key=lambda c: pr[c[1]])
        o = ops[i]
        e = best[3]
        eng[i], start[i] = e, s
        o["pick"] = best[2]
        free[e] = s + best[1]
        fin[i] = s + best[1] + o["lat"]
        for b in o["banks"]:
            for e2, j in bank[b].items():
                if e2 != e:
                    deps[i].add(j)
            bank[b][e] = i
            if o["grp"] is not None:
                opened[b] = None if o["grp"][1] else i
        order.append(i)
        ready.remove(i)
        for j in succ[i]:
            left[j] -= 1
            if left[j] == 0:
                ready.append(j)
    return order, eng, deps, start, fin


TUNE = {}
ROUNDS = 0
SPREAD = [(1, 1, 1, 1, HOP), (1, 1, 0.8, 1, HOP), (1, 1, 1, 1, 2 * HOP), (1, 1, 1, 0.7, HOP), (1, 1, 1, 1.3, HOP)]
BEST = []


def length(ops, order, eng, deps, fv, fs, ft, fg, hop):
    fin, free = [0.0] * len(ops), {}
    f = {"V": fv, "S": fs, "T": ft, "G": 1, "Y": 1}
    for i in order:
        o, e = ops[i], eng[i]
        c = o["alts"][o["pick"]][1] * f[e] * (fg if o["name"] in ("G1", "G2") else 1)
        s = free.get(e, 0.0)
        for j in deps[i]:
            if fin[j] + hop > s and not (e == "T" and eng[j] == "T"):
                s = fin[j] + hop
        free[e] = s + c
        fin[i] = s + c + o["lat"]
    return max(fin)


def search(ops, gr, rounds, seed=0, tune=None):
    rng = np.random.RandomState(seed)
    tags = sorted(set(o["tag"] for o in ops if o["tag"][-2] in "ABZ"))
    flex = sorted(set("e" + o["tag"] for o in ops if len(o["alts"]) > 1))

    def score(tune):
        order, eng, deps, start, fin = schedule(ops, gr, tune)
        return sum(length(ops, order, eng, deps, *p) for p in SPREAD) / len(SPREAD)
    tune = dict(TUNE if tune is None else tune)
    best = score(tune)
    for _ in range(rounds):
        t2 = dict(tune)
        for _m in range(int(rng.choice([1, 1, 2, 3]))):
            if rng.rand() < 0.3:
                t2[flex[rng.randint(len(flex))]] = float(rng.choice([-3, -1, -0.7, -0.4, 0, 1, 8]))
            else:
                k = tags[rng.randint(len(tags))]
                t2[k] = t2.get(k, 0.0) + float(rng.choice([-8, -4, -2, -1, -0.5, 0.5, 1, 2, 4, 8]))
        s = score(t2)
        if s < best + 0.03:
            best, tune = s, t2
    return tune


ORDER = "KEYB1 TRB1 ttA0 RHOB0 nfB0* DD3A1 R37A0* G2A2 YNA0 usB0 ynewA0* toffB0 NCB0 fpA0 ZDA1 dr2B0 ksB0 G2A3 noffB0 kmB0* CUA0 ZDA0 UA0 eqB0 FZA1 DRB0 EMB0 s2A0* L2A0 FZA0 DRB1 urA0 emB0 deB0 UUA0 ZDA2 us2A0 NMRA0 G2B1 DELB0 ZDA3 gamA0 piA0 ttB0 yA0 G2B0 FZA2 FZA3 CNT2A0 DR3B0 DD3B0 qiA0 DD3B1 DR3B1 YNB0 ynewB0* yB0 CNT2A1 CNT2A2 G2B3 siA0 g1A0 ZDB0 G2B2 fpB0 CUB0 betA0* UB0 FZaB0 fiA0 BASEA0 BTA0 yoB0 EA0 s2B0* y4A0 urB0 ZDB1 L2B0 t2A0 ZDB2 FZaB1 NMRB0 newA0 gamB0 UUB0 rnA0 g1B0 ZDB3 FZB0 piB0 us2B0 qiB0 FZB1 FZbB0 FZbB1 CNT2B0 R37B0 sl1B0 rA0 CNT2B1 CNT2B2 betB0 ybcA0+ siB0 sl2B0 fiB0 BTB0 sl3B0 EB0 BASEB0 t2B0 soffB0 ybcB0+ y4B0 TOTB0 newB0 rnB0 SCAT0B0 XRZ0* SCAT1B0 tot1B0 ybcB1+ G1A3+ ybcA1+ G1A1+* G1A2+ G1A0+* rB0 NTA0+ tot2B0 SUBA0+ SUBA2+ NTA1+ G1B2+ SUBA1+ NTA2+ SUBA3+ NTA3+ FARA0+ G1B1+ G1B0+ FARA1+ CNTA0+ XRZ1 biasB0 YZZ0 SUBB0+ rrA0+ G1B3+ SUBB1+ CNTA1+ CNTA2+ ABSA1+ SUBB2+ CNTA3+ NTB0+ cbA0+ FARB0+ SUBB3+ flA0+ XRZ2 nfA0+* disA0+ NTB1+ ABSA0+ NTB2+ FARB1+ XRZ3* MA0+ CNTB0+ TRA1+ KEYA0+ mA0+ YZZ1 KEYA1+ CNTB1+ ABSB0+ ABSB1+ RHOA0+ CNTB2+ TRA0+ YZZ2 CNTB3+ ksA0+ TRB0+ kmA0+* usA0+ eqA0+ NCA0+ toffA0+ disB0+ flB0+ NTB3+ cbB0+ EMA0+ rfB0 dr2A0+ rrB0+ MB0+ emA0+ DRA0+ mB0+ noffA0+ DR3A0+ G2A1+ DRA1+ G2A0+* DR3A1+ deA0+ KEYB0+ DD3A0+ DELA0+ rfA0 XRZ4* yoA0 XRZ6* yjB0 YZZ3 YZZ4 XRZ5 YZZ5 YZZ6 XRZ7 YZZ7 yztZ0 psZ1 yzoZ1 psZ0 yzZ1 yjA0 yzoZ0 yzZ0"


def arrange(ops, gr):
    names = ORDER.split()
    bare = [x.rstrip("+-*") for x in names]
    period = max(n for n, x in enumerate(bare) if x[-2] != "Z" and x[:2] not in ("yo", "yj")) + 1
    place = {b: n + period * (("-" in x) - ("+" in x)) for n, (b, x) in enumerate(zip(bare, names))}
    onv = set(b for b, x in zip(bare, names) if "*" in x)
    n = len(ops)
    deps, succ, pr = [set(x) for x in gr[0]], gr[1], list(gr[2])
    for i, o in enumerate(ops):
        o["pick"] = 0 if len(o["alts"]) == 1 or o["tag"] in onv else 1
        if not deps[i]:
            pr[i] = 1e4 - i
    line = sorted((i for i in range(n) if ops[i]["t"] >= 0), key=lambda i: ops[i]["t"] * period + place[ops[i]["tag"]])
    left = [len(x) for x in deps]
    ready = [i for i in range(n) if ops[i]["t"] < 0 and left[i] == 0]
    free = {e: 0.0 for e in "VSTGY"}
    fin, eng, start = [0.0] * n, [None] * n, [0.0] * n
    bank = [dict() for _ in range(8)]
    opened = [False] * 8
    order, at = [], 0

    def begin(i):
        o = ops[i]
        e = o["alts"][o["pick"]][0]
        late = [fin[j] + HOP for j in deps[i] if not (e == "T" and eng[j] == "T")]
        late += [fin[j] + HOP for b in o["banks"] for e2, j in bank[b].items() if e2 != e]
        return max(late + [free[e]]), e
    while len(order) < n:
        cand = [(begin(i), i) for i in ready if not (ops[i]["grp"] and any(opened[b] for b in ops[i]["banks"]))]
        if at < len(line) and left[line[at]] == 0:
            cand.append((begin(line[at]), line[at]))
        (s0, e0), _ = min(cand)
        (s, e), i = max((c for c in cand if c[0][1] == e0 and c[0][0] <= s0 + 0.05), key=lambda c: (ops[c[1]]["t"] >= 0, pr[c[1]]))
        o = ops[i]
        eng[i], start[i] = e, s
        free[e] = s + o["alts"][o["pick"]][1]
        fin[i] = free[e] + o["lat"]
        for b in o["banks"]:
            deps[i].update(j for e2, j in bank[b].items() if e2 != e)
            bank[b][e] = i
            if o["grp"] is not None:
                opened[b] = not o["grp"][1]
        order.append(i)
        if o["t"] >= 0:
            at += 1
        else:
            ready.remove(i)
        for j in succ[i]:
            left[j] -= 1
            if left[j] == 0 and ops[j]["t"] < 0:
                ready.append(j)
    return order, eng, deps, start, fin


def rank_program(g, core, T, topo):
    rank = T.rank_of(core)
    if rank is None:
        return
    nxt = T.cores[(rank + 1) % len(T.cores)]
    rid, pid, _se = topo.addr(nxt)
    ne = min(len(topo.engines(a, b)) for a, b in zip(T.cores, list(T.cores[1:]) + [T.cores[0]]))
    mask = sum(1 << e for e in topo.engines(core, nxt)[:ne])
    nsent = [0]

    def rem(dst, src, sem):
        if dst is None:
            return ne
        def fn(g):
            g.remote_dma(dst, src, T.sem[sem], T.sem.sent, pid, rid, mask)
            nsent[0] += ne
            return None
        return fn

    ops = build(T, rem)
    gr = graph(ops)
    order, eng, deps, start, fin = arrange(ops, gr) if ORDER else schedule(ops, gr, {})
    qs = {"V": g.vector, "S": g.scalar, "T": g.tensor, "G": g, "Y": g.sync}
    needed = set()
    for i in order:
        for j in deps[i]:
            if ops[j]["sem"] is None and not (eng[i] == "T" and eng[j] == "T"):
                needed.add(j)
    count = {e: 0 for e in "VSTG"}
    tick = {}
    for i in order:
        if ops[i]["sem"] is not None:
            tick[i] = ops[i]["sem"]
        elif i in needed:
            count[eng[i]] += 1
            tick[i] = ("s" + eng[i], count[eng[i]])
    seen = {e: {} for e in qs}
    waited = {}
    for i in order:
        e = eng[i]
        want = {}
        for j in deps[i]:
            if e == "T" and eng[j] == "T":
                continue
            s, v = tick[j]
            want[s] = max(want.get(s, 0), v)
        for s in sorted(want):
            if seen[e].get(s, 0) < want[s]:
                qs[e].wait_ge(T.sem[s], want[s])
                seen[e][s] = want[s]
                waited[s] = max(waited.get(s, 0), want[s])
        x = ops[i]["alts"][ops[i]["pick"]][2](g)
        if x is not None and i in tick:
            x.then_inc(T.sem[tick[i][0]], 16 if ops[i]["sem"] is not None else 1)
    total = {}
    for i in tick:
        total[tick[i][0]] = max(total.get(tick[i][0], 0), tick[i][1])
    total["sent"] = nsent[0]
    for s in sorted(total):
        if waited.get(s, 0) < total[s]:
            g.wait_ge(T.sem[s], total[s])
